import numpy as np
import ml_dtypes


def mxq(x, axis, fmt="e4m3"):
    dtype, down = {"e4m3": (ml_dtypes.float8_e4m3fn, 7), "e5m2": (ml_dtypes.float8_e5m2, 14)}[fmt]
    v = np.moveaxis(np.asarray(x, np.float32).astype(ml_dtypes.bfloat16).astype(np.float64), axis, -1)
    blocks = v.reshape(v.shape[:-1] + (-1, 32))
    amax = np.abs(blocks).max(-1, keepdims=True)
    byte = np.maximum(np.where(amax > 0, np.frexp(amax)[1] - 1 + 127, 0) - down, 1)
    scale = np.exp2(byte - 127.0)
    codes = (blocks / scale).astype(np.float32).astype(dtype).astype(np.float64)
    return np.moveaxis((codes * scale).reshape(v.shape), -1, axis)


WIDE = False


def mx_kscale(k):
    if not WIDE:
        return np.ones(k)
    levels = np.array([10, -10, 5, -5, 0])
    if k % 512:
        return np.exp2(np.random.permutation(np.resize(levels, k // 32))).repeat(32)
    a = np.empty((k // 512, 16))
    for p in range(k // 512):
        a[p, :8] = np.random.permutation(np.resize(levels, 8))
        for g in range(8):
            far = levels[np.abs(levels - a[p, g]) >= 10]
            a[p, g + 8] = far[np.random.randint(len(far))]
    return np.exp2(a.ravel()).repeat(32)


def f64(x):
    return np.asarray(x).astype(np.float64)


def striped(idx):
    return np.tile(idx.reshape(-1, 16).T, (8, 1)).astype(np.uint16)


def unstriped(offs):
    return offs[:16].T.reshape(-1).astype(np.int64)


E2M1 = np.array([0.0, 0.5, 1.0, 1.5, 2.0, 3.0, 4.0, 6.0, -0.0, -0.5, -1.0, -1.5, -2.0, -3.0, -4.0, -6.0])


def pack_weight(w, fmt):
    k, n = w.shape
    w = f64(np.asarray(w, np.float32).astype(ml_dtypes.bfloat16)).reshape(k // 32, 32, n)
    amax = np.abs(w).max(1)
    if fmt == "e4m3":
        byte = np.frexp(amax)[1] - 1 + 127 - 7
    else:
        mant, ex = np.frexp(amax / 6.0)
        byte = np.where(mant > 0.5, ex, ex - 1) + 127
    byte = np.clip(np.where(amax > 0, byte, 1), 1, 254)
    scaled = (w * np.exp2(127.0 - byte)[:, None, :]).reshape(k, n).astype(np.float32)
    by_word = np.ascontiguousarray(scaled.reshape(k // 512, 128, 4, n).transpose(0, 1, 3, 2))
    if fmt == "e4m3":
        words = by_word.astype(ml_dtypes.float8_e4m3fn).view(np.uint8)
    else:
        c = by_word.astype(ml_dtypes.float4_e2m1fn).view(np.uint8) & 0xF
        words = (c[..., 0::2] | (c[..., 1::2] << 4)).reshape(k // 512, 128, 2 * n)
    return np.ascontiguousarray(words), np.ascontiguousarray(byte.astype(np.uint8).reshape(k // 512, 16, n))


def unpack_weight(words, scales, fmt):
    g, _, n = scales.shape
    words = np.ascontiguousarray(words).reshape(g, 128, n, -1)
    if fmt == "e4m3":
        vals = words.view(ml_dtypes.float8_e4m3fn).astype(np.float64)
    else:
        nib = np.empty((g, 128, n, 4), np.uint8)
        nib[..., 0::2] = words & 0xF
        nib[..., 1::2] = words >> 4
        vals = E2M1[nib]
    vals = vals * np.repeat(np.exp2(scales.astype(np.float64) - 127.0), 8, axis=1)[..., None]
    return vals.transpose(0, 1, 3, 2).reshape(g * 512, n)


def gelu(v):
    return 0.5 * v * (1.0 + np.tanh(np.sqrt(2.0 / np.pi) * (v + 0.044715 * v**3)))


K, H, T, S, T2, T3, S2, P = 1024, 512, 2048, 1024, 2048, 2048, 1024, 1024

def setup_inputs():
    n = np.random.standard_normal
    s = mx_kscale(K)[:, None]
    u = mx_kscale(H)[:, None]
    d = {}
    d["tab_words"], d["tab_scales"] = pack_weight(n((K, T)) * s, "e4m3")
    d["tab2_words"], d["tab2_scales"] = pack_weight(n((H, T3)) / np.sqrt(H) / u, "e4m3")
    d["offs"] = striped(np.random.permutation(T)[:S])
    d["offs2"] = striped(np.random.permutation(T3)[:S2])
    d["offs3"] = striped(np.random.permutation(T2)[:S])
    d["offs4"] = striped(np.random.permutation(T2)[:P])
    d["wq_words"], d["wq_scales"] = pack_weight(0.5 * n((K, H)) / np.sqrt(K) / s, "e2m1")
    d["wp"] = (n((K, H)) / np.sqrt(K) / s * u.T).astype(np.float32)
    d["kap"] = (2.0 * np.exp(0.2 * n(H)) * u[:, 0]).astype(np.float32)
    d["gq"] = (0.7 * np.exp(0.2 * n(H)) * u[:, 0]).astype(np.float32)
    d["page0"] = (n((H, T2)) * u).astype(np.float32)
    d["wgs"] = np.exp(0.3 * n((128, S))).astype(np.float32)
    d["prior"] = n((S2, P)).astype(np.float32)
    return d

def reference(tab_words, tab_scales, tab2_words, tab2_scales, offs, offs2, offs3, offs4,
              wq_words, wq_scales, wp, kap, gq, page0, wgs, prior):
    v = unpack_weight(tab_words, tab_scales, "e4m3")[:, unstriped(offs)]
    v2 = unpack_weight(tab2_words, tab2_scales, "e4m3")[:, unstriped(offs2)]
    wq = unpack_weight(wq_words, wq_scales, "e2m1")
    q = wq.T @ v
    mom = mxq(f64(wp), 0, "e4m3").T @ v
    kicked = mom - f64(kap)[:, None] * np.sin(q)
    h = f64(gq)[:, None] * q + kicked
    page = f64(page0).copy()
    page[:, unstriped(offs3)] = np.tile(f64(wgs), (H // 128, 1)) * h
    e = v2.T @ mxq(page, 0, "e4m3")
    return e[:, unstriped(offs4)] + f64(prior)

@@ -1,0 +1,278 @@
+from contextlib import ExitStack
+
+import concourse.mybir as mybir
+
+K, H, T, S = 1024, 512, 2048, 1024
+FLOPS = 2 * 2 * K * H * S + 2 * H * S * T
+
+F32 = mybir.dt.float32
+BF16 = mybir.dt.bfloat16
+I32 = mybir.dt.int32
+U32 = mybir.dt.uint32
+U16 = mybir.dt.uint16
+U8 = mybir.dt.uint8
+FP8X4 = mybir.dt.float8_e4m3fn_x4
+FP4X4 = mybir.dt.float4_e2m1fn_x4
+MULT = mybir.AluOpType.mult
+ADD = mybir.AluOpType.add
+SUB = mybir.AluOpType.subtract
+SIN = mybir.ActivationFunctionType.Sin
+
+P = 128
+PACK = 4
+BANK = 512
+PASSES = K // (P * PACK)
+QUADS = 4
+
+
+def tile_list_mancala_kick_drift_kernel(
+    tc, tab_words, tab_scales, tab2_words, tab2_scales, offs, offs2, offs3, offs4,
+    wq_words, wq_scales, wp, kap, gq, page0, wgs, prior, out,
+):
+    nc = tc.nc
+    with ExitStack() as ctx:
+        lists = ctx.enter_context(tc.tile_pool(name="lists", bufs=1))
+        keep = ctx.enter_context(tc.tile_pool(name="keep", bufs=1))
+        ring = ctx.enter_context(tc.tile_pool(name="ring", bufs=2))
+        psum = ctx.enter_context(tc.psum_pool(name="psum", bufs=8))
+
+        def load_list(src, name):
+            tile = lists.tile([P, S // 16], U16, name=name)
+            nc.sync.dma_start(tile[:], src)
+            return tile
+
+        def zeroed(shape, name, engine):
+            tile = keep.tile(shape, U8, name=name, align_bytes=64)
+            engine.memset(tile[:].bitcast(I32), 0)
+            return tile
+
+        def load_words(src, name):
+            tile = keep.tile([P, T], I32, name=name, align_bytes=64)
+            nc.sync.dma_start(tile[:], src.rearrange("p n i -> p (n i)").bitcast(I32))
+            return tile
+
+        def gather(dst, window, offsets, dtype):
+            nc.vector.tensor_copy(dst.bitcast(dtype), window.bitcast(dtype).indirect(offsets))
+
+        tab_plane = zeroed([P, T], "tab_plane", nc.gpsimd)
+        wq_plane_raw = zeroed([P, PASSES, H], "wq_plane_raw", nc.vector)
+        v_plane1 = zeroed([P, S], "v_plane1", nc.vector)
+        warm = keep.tile([P, 16], F32, name="warm")
+        nc.vector.memset(warm[:, 0:8], 0.0)
+
+        def load_wp(a):
+            tile = keep.tile([P, PACK, H], F32, name="wp_raw", tag="wide_stage", bufs=4)
+            rows = wp[a * P * PACK : (a + 1) * P * PACK, :]
+            nc.sync.dma_start(tile[:], rows.rearrange("(p j) c -> p j c", j=PACK))
+            return tile
+
+        def load_page(t):
+            tile = keep.tile([P, T], F32, name="page%d" % t)
+            nc.sync.dma_start(tile[:], page0.rearrange("(p t) c -> t p c", t=PACK)[t])
+            return tile
+
+        for quad in range(QUADS):
+            nc.gpsimd.dma_start(
+                tab_plane[32 * quad : 32 * quad + 4 * PASSES, :].bitcast(I32),
+                tab_scales[:, 4 * quad : 4 * quad + 4, :].bitcast(I32),
+            )
+        for quad in range(QUADS):
+            nc.scalar.dma_start(
+                wq_plane_raw[32 * quad : 32 * quad + 4, :, :].bitcast(I32),
+                wq_scales[:, 4 * quad : 4 * quad + 4, :].rearrange("a r c -> r a c").bitcast(I32),
+            )
+        nc.scalar.activation(warm[:, 8:16], warm[:, 0:8], SIN)
+        idx = load_list(offs, "idx")
+        wq_raw = keep.tile([P, PASSES, 2 * H], U8, name="wq_raw", align_bytes=64)
+        nc.sync.dma_start(wq_raw[:].bitcast(I32), wq_words.rearrange("a p c -> p a c").bitcast(I32))
+        tab_w = [load_words(tab_words[0], "tab_w0")]
+        wp_raw = [load_wp(0)]
+        tab2_plane = keep.tile([P, T], U8, name="tab2_plane", align_bytes=64)
+        for quad in range(QUADS):
+            rows = tab2_scales[0, 4 * quad : 4 * quad + 4, :].bitcast(I32)
+            nc.sync.dma_start(
+                tab2_plane[32 * quad : 32 * quad + 32, :].bitcast(I32),
+                rows.unsqueeze(0).broadcast_to([8, 4, T // 4]),
+            )
+        idx2 = load_list(offs2, "idx2")
+        wp_raw.append(load_wp(1))
+        tab_w.append(load_words(tab_words[1], "tab_w1"))
+        kap_sb = keep.tile([P, PACK], F32, name="kap_sb")
+        nc.sync.dma_start(kap_sb[:], kap.rearrange("(p t) -> p t", t=PACK))
+        gq_sb = keep.tile([P, PACK], F32, name="gq_sb")
+        nc.sync.dma_start(gq_sb[:], gq.rearrange("(p t) -> p t", t=PACK))
+        idx3 = load_list(offs3, "idx3")
+        page = [load_page(0)]
+        wg = keep.tile([P, PACK, S], F32, name="wg")
+        for quad in range(QUADS):
+            nc.sync.dma_start(
+                wg[32 * quad : 32 * quad + 32, :, :], wgs.rearrange("(p t) j -> p t j", t=PACK)
+            )
+        for t in range(1, PACK):
+            page.append(load_page(t))
+        tab2_w = load_words(tab2_words[0], "tab2_w")
+        idx4 = load_list(offs4, "idx4")
+
+        wq_perm = keep.tile([P, PASSES, 2 * H], U8, name="wq_perm", align_bytes=64)
+        nc.vector.tensor_copy(
+            wq_perm[:].bitcast(U16).rearrange("p a (t m) -> p a t m", t=PACK),
+            wq_raw[:].bitcast(U16).rearrange("p a (m t) -> p a t m", t=PACK),
+        )
+        v_w0 = keep.tile([P, S], U32, name="v_w0", align_bytes=64)
+        gather(v_w0[:], tab_w[0][:], idx[:], U32)
+        v_plane = keep.tile([P, S], U8, name="v_plane", align_bytes=64)
+        gather(v_plane[:], tab_plane[:], idx[:], U8)
+        nc.gpsimd.dma_start(v_plane1[0:112, :].bitcast(I32), v_plane[4:116, :].bitcast(I32))
+        v_planes = [v_plane, v_plane1]
+
+        def quantise_wp(a):
+            grouped = keep.tile([P, H * PACK], BF16, name="wp_grouped%d" % a, align_bytes=64)
+            nc.scalar.copy(
+                grouped[:].rearrange("p (t m j) -> p m t j", t=PACK, j=PACK),
+                wp_raw[a][:].rearrange("p j (m t) -> p m t j", t=PACK),
+            )
+            codes = keep.tile([P, H], U32, name="wp_codes%d" % a, align_bytes=64)
+            plane = keep.tile([P, H], U8, name="wp_plane%d" % a, align_bytes=64)
+            nc.vector.quantize_mx(out=codes[:].bitcast(FP8X4), scales=plane[:], in_=grouped[:])
+            return codes, plane
+
+        v2_plane = keep.tile([P, S], U8, name="v2_plane", align_bytes=64)
+        gather(v2_plane[:], tab2_plane[:], idx2[:], U8)
+        wp_mx = [quantise_wp(0)]
+        wq_plane = keep.tile([P, PASSES, H], U8, name="wq_plane", align_bytes=64)
+        nc.vector.tensor_copy(
+            wq_plane[:].rearrange("p a (t m) -> p a t m", t=PACK),
+            wq_plane_raw[:].rearrange("p a (m t) -> p a t m", t=PACK),
+        )
+        v_w1a = keep.tile([P, BANK], U32, name="v_w1a", tag="wp_grouped0", align_bytes=64)
+        gather(v_w1a[:], tab_w[1][:], idx[:, 0:32], U32)
+        wp_mx.append(quantise_wp(1))
+        v_w1b = keep.tile([P, BANK], U32, name="v_w1b", tag="wp_grouped1", align_bytes=64)
+        gather(v_w1b[:], tab_w[1][:], idx[:, 32:64], U32)
+        v_w = [[v_w0[:, 0:BANK], v_w0[:, BANK:S]], [v_w1a[:], v_w1b[:]]]
+        wp_codes = [pair[0] for pair in wp_mx]
+        wp_planes = [pair[1] for pair in wp_mx]
+
+        prior_sb = []
+        for i in range(S // (2 * P)):
+            tile = keep.tile([P, 2, S], F32, name="prior_sb", tag="wide_stage", bufs=4)
+            nc.sync.dma_start(
+                tile[:], prior[2 * P * i : 2 * P * (i + 1), :].rearrange("(g p) m -> p g m", p=P)
+            )
+            prior_sb.append(tile)
+
+        grouped_page = [
+            keep.tile([P, BANK, PACK], BF16, name="grouped_page%d" % c, align_bytes=64)
+            for c in range(T // BANK)
+        ]
+
+        def advance(t):
+            h = ring.tile([P, S], F32, name="h", align_bytes=64)
+            todo = []
+            for u in range(S // BANK):
+                cols = slice(u * BANK, (u + 1) * BANK)
+                q = psum.tile([P, BANK], F32, name="q", tag="bank")
+                for a in range(PASSES):
+                    nc.tensor.matmul_mx(
+                        out=q[:],
+                        lhsT=wq_perm[:, a, 2 * P * t : 2 * P * (t + 1)].bitcast(FP4X4),
+                        lhsT_scale=wq_plane[:, a, P * t : P * (t + 1)],
+                        rhs=v_w[a][u].bitcast(FP8X4),
+                        rhs_scale=v_planes[a][:, cols],
+                        start=(a == 0),
+                        stop=(a == PASSES - 1),
+                    )
+                mom = psum.tile([P, BANK], F32, name="mom", tag="bank")
+                for a in range(PASSES):
+                    nc.tensor.matmul_mx(
+                        out=mom[:],
+                        lhsT=wp_codes[a][:, P * t : P * (t + 1)].bitcast(FP8X4),
+                        lhsT_scale=wp_planes[a][:, P * t : P * (t + 1)],
+                        rhs=v_w[a][u].bitcast(FP8X4),
+                        rhs_scale=v_planes[a][:, cols],
+                        start=(a == 0),
+                        stop=(a == PASSES - 1),
+                    )
+                sine = ring.tile([P, BANK], F32, name="sine", bufs=3)
+                nc.scalar.activation(sine[:], q[:], SIN)
+                neg_kicked = ring.tile([P, BANK], F32, name="neg_kicked")
+                nc.vector.scalar_tensor_tensor(
+                    neg_kicked[:], sine[:], kap_sb[:, t : t + 1], mom[:], MULT, SUB
+                )
+                todo.append((cols, q, neg_kicked))
+            for cols, q, neg_kicked in todo:
+                nc.vector.scalar_tensor_tensor(
+                    h[:, cols], q[:], gq_sb[:, t : t + 1], neg_kicked[:], MULT, SUB
+                )
+            return h
+
+        def scatter(t, h):
+            nc.vector.tensor_tensor(page[t][:].indirect(idx3[:]), h[:], wg[:, t, :], MULT)
+
+        def interleave(t, c, on_vector):
+            dst = grouped_page[c][:, :, t]
+            src = page[t][:, c * BANK : (c + 1) * BANK]
+            if on_vector:
+                nc.vector.tensor_copy(dst, src)
+            elif t == PACK - 2 and c % 2 == 0:
+                nc.scalar.copy(
+                    grouped_page[c][:, :, t:], src.unsqueeze(2).broadcast_to([P, BANK, 2])
+                )
+            else:
+                nc.scalar.copy(dst, src)
+
+        hs = [advance(0)]
+        for t in range(PACK):
+            if t + 1 < PACK:
+                hs.append(advance(t + 1))
+            scatter(t, hs[t])
+            if t + 1 < PACK:
+                for c in range(T // BANK):
+                    interleave(t, c, False)
+
+        last = PACK - 1
+        chunk_order = [0, 2, 1, 3]
+        for c in range(T // BANK):
+            interleave(last, c, c % 2 == 0)
+        v2_w = ring.tile([P, S], U32, name="v2_w", tag="h", align_bytes=64)
+        gather(v2_w[:, 0:256], tab2_w[:], idx2[:, 0:16], U32)
+        page_codes, page_planes = {}, {}
+        for c in chunk_order:
+            codes = keep.tile([P, BANK], U32, name="page_codes%d" % c, align_bytes=64)
+            plane = keep.tile([P, BANK], U8, name="page_plane%d" % c, align_bytes=64)
+            nc.vector.quantize_mx(
+                out=codes[:].bitcast(FP8X4),
+                scales=plane[:],
+                in_=grouped_page[c][:].rearrange("p n t -> p (n t)"),
+            )
+            page_codes[c] = codes
+            page_planes[c] = plane
+        gather(v2_w[:, 256:S], tab2_w[:], idx2[:, 16:64], U32)
+
+        tiles = S // P
+        for n in range(tiles):
+            scores = ring.tile([P, T], F32, name="scores", bufs=3)
+            for c in chunk_order:
+                e = psum.tile([P, BANK], F32, name="e", tag="bank")
+                nc.tensor.matmul_mx(
+                    out=e[:],
+                    lhsT=v2_w[:, n * P : (n + 1) * P].bitcast(FP8X4),
+                    lhsT_scale=v2_plane[:, n * P : (n + 1) * P],
+                    rhs=page_codes[c][:].bitcast(FP8X4),
+                    rhs_scale=page_planes[c][:],
+                    start=True,
+                    stop=True,
+                )
+                nc.scalar.copy(scores[:, c * BANK : (c + 1) * BANK], e[:])
+            picked = ring.tile([P, S], F32, name="picked", bufs=3)
+            pieces = 2 if n == tiles - 1 else 1
+            width = S // pieces
+            for i in range(pieces):
+                cols = slice(i * width, (i + 1) * width)
+                nc.vector.tensor_tensor(
+                    picked[:, cols],
+                    scores[:].indirect(idx4[:, i * width // 16 : (i + 1) * width // 16]),
+                    prior_sb[n // 2][:, n % 2, cols],
+                    ADD,
+                )
+                nc.sync.dma_start(out[n * P : (n + 1) * P, cols], picked[:, cols])

@@ -54,8 +54,7 @@ def tile_list_mancala_kick_drift_kernel(
         def gather(dst, window, offsets, dtype):
             nc.vector.tensor_copy(dst.bitcast(dtype), window.bitcast(dtype).indirect(offsets))
 
-        tab_plane = zeroed([P, T], "tab_plane", nc.gpsimd)
-        wq_plane_raw = zeroed([P, PASSES, H], "wq_plane_raw", nc.vector)
+        wq_plane_raw = zeroed([P, PASSES, H], "wq_plane_raw", nc.gpsimd)
         v_plane1 = zeroed([P, S], "v_plane1", nc.vector)
         warm = keep.tile([P, 16], F32, name="warm")
         nc.vector.memset(warm[:, 0:8], 0.0)
@@ -73,20 +72,29 @@ def tile_list_mancala_kick_drift_kernel(
 
         for quad in range(QUADS):
             nc.gpsimd.dma_start(
-                tab_plane[32 * quad : 32 * quad + 4 * PASSES, :].bitcast(I32),
-                tab_scales[:, 4 * quad : 4 * quad + 4, :].bitcast(I32),
-            )
-        for quad in range(QUADS):
-            nc.scalar.dma_start(
                 wq_plane_raw[32 * quad : 32 * quad + 4, :, :].bitcast(I32),
                 wq_scales[:, 4 * quad : 4 * quad + 4, :].rearrange("a r c -> r a c").bitcast(I32),
             )
         nc.scalar.activation(warm[:, 8:16], warm[:, 0:8], SIN)
         idx = load_list(offs, "idx")
+        tab_plane = keep.tile([P, T], U8, name="tab_plane", align_bytes=64)
+        tab_rows = tab_scales.rearrange("a q c -> (a q) c").bitcast(I32)
+
+        def load_tab_rows(piece):
+            first = 4 * (piece // 2) + 4 * (piece % 2)
+            nc.sync.dma_start(
+                tab_plane[16 * piece : 16 * piece + 16, :].bitcast(I32),
+                tab_rows[first : first + 16, :],
+            )
+
+        for piece in range(6):
+            load_tab_rows(piece)
+        tab_w = [load_words(tab_words[0], "tab_w0")]
+        for piece in range(6, 8):
+            load_tab_rows(piece)
+        wp_raw = [load_wp(0)]
         wq_raw = keep.tile([P, PASSES, 2 * H], U8, name="wq_raw", align_bytes=64)
         nc.sync.dma_start(wq_raw[:].bitcast(I32), wq_words.rearrange("a p c -> p a c").bitcast(I32))
-        tab_w = [load_words(tab_words[0], "tab_w0")]
-        wp_raw = [load_wp(0)]
         tab2_plane = keep.tile([P, T], U8, name="tab2_plane", align_bytes=64)
         for quad in range(QUADS):
             rows = tab2_scales[0, 4 * quad : 4 * quad + 4, :].bitcast(I32)
@@ -102,51 +110,53 @@ def tile_list_mancala_kick_drift_kernel(
         gq_sb = keep.tile([P, PACK], F32, name="gq_sb")
         nc.sync.dma_start(gq_sb[:], gq.rearrange("(p t) -> p t", t=PACK))
         idx3 = load_list(offs3, "idx3")
-        page = [load_page(0)]
-        wg = keep.tile([P, PACK, S], F32, name="wg")
-        for quad in range(QUADS):
-            nc.sync.dma_start(
-                wg[32 * quad : 32 * quad + 32, :, :], wgs.rearrange("(p t) j -> p t j", t=PACK)
-            )
-        for t in range(1, PACK):
+        page, wg = [], []
+        for t in range(PACK):
             page.append(load_page(t))
+            tile = keep.tile([P, S], F32, name="wg%d" % t)
+            for quad in (0, 2, 1, 3):
+                nc.sync.dma_start(
+                    tile[32 * quad : 32 * quad + 32, :],
+                    wgs.rearrange("(p t) j -> t p j", t=PACK)[t],
+                )
+            wg.append(tile)
         tab2_w = load_words(tab2_words[0], "tab2_w")
         idx4 = load_list(offs4, "idx4")
 
+        v_plane = keep.tile([P, S], U8, name="v_plane", align_bytes=64)
+        gather(v_plane[:], tab_plane[:], idx[:], U8)
+        nc.gpsimd.dma_start(v_plane1[0:100, :].bitcast(I32), v_plane[28:P, :].bitcast(I32))
+        v_planes = [v_plane, v_plane1]
+        v_w0 = keep.tile([P, S], U32, name="v_w0", align_bytes=64)
+        gather(v_w0[:], tab_w[0][:], idx[:], U32)
         wq_perm = keep.tile([P, PASSES, 2 * H], U8, name="wq_perm", align_bytes=64)
         nc.vector.tensor_copy(
             wq_perm[:].bitcast(U16).rearrange("p a (t m) -> p a t m", t=PACK),
             wq_raw[:].bitcast(U16).rearrange("p a (m t) -> p a t m", t=PACK),
         )
-        v_w0 = keep.tile([P, S], U32, name="v_w0", align_bytes=64)
-        gather(v_w0[:], tab_w[0][:], idx[:], U32)
-        v_plane = keep.tile([P, S], U8, name="v_plane", align_bytes=64)
-        gather(v_plane[:], tab_plane[:], idx[:], U8)
-        nc.gpsimd.dma_start(v_plane1[0:112, :].bitcast(I32), v_plane[4:116, :].bitcast(I32))
-        v_planes = [v_plane, v_plane1]
 
-        def quantise_wp(a):
+        def quantise_wp(a, codes_tag):
             grouped = keep.tile([P, H * PACK], BF16, name="wp_grouped%d" % a, align_bytes=64)
             nc.scalar.copy(
                 grouped[:].rearrange("p (t m j) -> p m t j", t=PACK, j=PACK),
                 wp_raw[a][:].rearrange("p j (m t) -> p m t j", t=PACK),
             )
-            codes = keep.tile([P, H], U32, name="wp_codes%d" % a, align_bytes=64)
+            codes = keep.tile([P, H], U32, name="wp_codes", tag=codes_tag, align_bytes=64)
             plane = keep.tile([P, H], U8, name="wp_plane%d" % a, align_bytes=64)
             nc.vector.quantize_mx(out=codes[:].bitcast(FP8X4), scales=plane[:], in_=grouped[:])
             return codes, plane
 
         v2_plane = keep.tile([P, S], U8, name="v2_plane", align_bytes=64)
         gather(v2_plane[:], tab2_plane[:], idx2[:], U8)
-        wp_mx = [quantise_wp(0)]
-        wq_plane = keep.tile([P, PASSES, H], U8, name="wq_plane", align_bytes=64)
+        wq_plane = keep.tile([P, PASSES, H], U8, name="wq_plane", tag="tab2_plane", align_bytes=64)
         nc.vector.tensor_copy(
             wq_plane[:].rearrange("p a (t m) -> p a t m", t=PACK),
             wq_plane_raw[:].rearrange("p a (m t) -> p a t m", t=PACK),
         )
+        wp_mx = [quantise_wp(0, "wq_plane_raw")]
         v_w1a = keep.tile([P, BANK], U32, name="v_w1a", tag="wp_grouped0", align_bytes=64)
         gather(v_w1a[:], tab_w[1][:], idx[:, 0:32], U32)
-        wp_mx.append(quantise_wp(1))
+        wp_mx.append(quantise_wp(1, "wp_codes1"))
         v_w1b = keep.tile([P, BANK], U32, name="v_w1b", tag="wp_grouped1", align_bytes=64)
         gather(v_w1b[:], tab_w[1][:], idx[:, 32:64], U32)
         v_w = [[v_w0[:, 0:BANK], v_w0[:, BANK:S]], [v_w1a[:], v_w1b[:]]]
@@ -166,15 +176,19 @@ def tile_list_mancala_kick_drift_kernel(
             for c in range(T // BANK)
         ]
 
+        halves = range(S // BANK)
+
         def advance(t):
             h = ring.tile([P, S], F32, name="h", align_bytes=64)
-            todo = []
-            for u in range(S // BANK):
-                cols = slice(u * BANK, (u + 1) * BANK)
-                q = psum.tile([P, BANK], F32, name="q", tag="bank")
-                for a in range(PASSES):
+            q, mom = [], []
+            for u in halves:
+                q.append(psum.tile([P, BANK], F32, name="q", tag="bank"))
+                mom.append(psum.tile([P, BANK], F32, name="mom", tag="bank"))
+            for a in range(PASSES):
+                for u in halves:
+                    cols = slice(u * BANK, (u + 1) * BANK)
                     nc.tensor.matmul_mx(
-                        out=q[:],
+                        out=q[u][:],
                         lhsT=wq_perm[:, a, 2 * P * t : 2 * P * (t + 1)].bitcast(FP4X4),
                         lhsT_scale=wq_plane[:, a, P * t : P * (t + 1)],
                         rhs=v_w[a][u].bitcast(FP8X4),
@@ -182,10 +196,8 @@ def tile_list_mancala_kick_drift_kernel(
                         start=(a == 0),
                         stop=(a == PASSES - 1),
                     )
-                mom = psum.tile([P, BANK], F32, name="mom", tag="bank")
-                for a in range(PASSES):
                     nc.tensor.matmul_mx(
-                        out=mom[:],
+                        out=mom[u][:],
                         lhsT=wp_codes[a][:, P * t : P * (t + 1)].bitcast(FP8X4),
                         lhsT_scale=wp_planes[a][:, P * t : P * (t + 1)],
                         rhs=v_w[a][u].bitcast(FP8X4),
@@ -193,21 +205,24 @@ def tile_list_mancala_kick_drift_kernel(
                         start=(a == 0),
                         stop=(a == PASSES - 1),
                     )
+            neg_kicked = []
+            for u in halves:
                 sine = ring.tile([P, BANK], F32, name="sine", bufs=3)
-                nc.scalar.activation(sine[:], q[:], SIN)
-                neg_kicked = ring.tile([P, BANK], F32, name="neg_kicked")
+                nc.scalar.activation(sine[:], q[u][:], SIN)
+                tile = ring.tile([P, BANK], F32, name="neg_kicked")
                 nc.vector.scalar_tensor_tensor(
-                    neg_kicked[:], sine[:], kap_sb[:, t : t + 1], mom[:], MULT, SUB
+                    tile[:], sine[:], kap_sb[:, t : t + 1], mom[u][:], MULT, SUB
                 )
-                todo.append((cols, q, neg_kicked))
-            for cols, q, neg_kicked in todo:
+                neg_kicked.append(tile)
+            for u in halves:
                 nc.vector.scalar_tensor_tensor(
-                    h[:, cols], q[:], gq_sb[:, t : t + 1], neg_kicked[:], MULT, SUB
+                    h[:, u * BANK : (u + 1) * BANK],
+                    q[u][:], gq_sb[:, t : t + 1], neg_kicked[u][:], MULT, SUB,
                 )
             return h
 
         def scatter(t, h):
-            nc.vector.tensor_tensor(page[t][:].indirect(idx3[:]), h[:], wg[:, t, :], MULT)
+            nc.vector.tensor_tensor(page[t][:].indirect(idx3[:]), h[:], wg[t][:], MULT)
 
         def interleave(t, c, on_vector):
             dst = grouped_page[c][:, :, t]
@@ -223,9 +238,11 @@ def tile_list_mancala_kick_drift_kernel(
 
         hs = [advance(0)]
         for t in range(PACK):
-            if t + 1 < PACK:
-                hs.append(advance(t + 1))
             scatter(t, hs[t])
+            if t == 0:
+                hs.append(advance(1))
+            if t + 2 < PACK:
+                hs.append(advance(t + 2))
             if t + 1 < PACK:
                 for c in range(T // BANK):
                     interleave(t, c, False)
@@ -265,7 +282,7 @@ def tile_list_mancala_kick_drift_kernel(
                 )
                 nc.scalar.copy(scores[:, c * BANK : (c + 1) * BANK], e[:])
             picked = ring.tile([P, S], F32, name="picked", bufs=3)
-            pieces = 2 if n == tiles - 1 else 1
+            pieces = 4 if n == tiles - 1 else 1
             width = S // pieces
             for i in range(pieces):
                 cols = slice(i * width, (i + 1) * width)

@@ -17,12 +17,15 @@ MULT = mybir.AluOpType.mult
 ADD = mybir.AluOpType.add
 SUB = mybir.AluOpType.subtract
 SIN = mybir.ActivationFunctionType.Sin
+COPY = mybir.ActivationFunctionType.Copy
 
 P = 128
 PACK = 4
 BANK = 512
 PASSES = K // (P * PACK)
 QUADS = 4
+MOVED = 100
+AHEAD = 3
 
 
 def tile_list_mancala_kick_drift_kernel(
@@ -54,13 +57,8 @@ def tile_list_mancala_kick_drift_kernel(
         def gather(dst, window, offsets, dtype):
             nc.vector.tensor_copy(dst.bitcast(dtype), window.bitcast(dtype).indirect(offsets))
 
-        wq_plane_raw = zeroed([P, PASSES, H], "wq_plane_raw", nc.gpsimd)
-        v_plane1 = zeroed([P, S], "v_plane1", nc.vector)
-        warm = keep.tile([P, 16], F32, name="warm")
-        nc.vector.memset(warm[:, 0:8], 0.0)
-
         def load_wp(a):
-            tile = keep.tile([P, PACK, H], F32, name="wp_raw", tag="wide_stage", bufs=4)
+            tile = keep.tile([P, PACK, H], F32, name="wp_raw%d" % a, align_bytes=64)
             rows = wp[a * P * PACK : (a + 1) * P * PACK, :]
             nc.sync.dma_start(tile[:], rows.rearrange("(p j) c -> p j c", j=PACK))
             return tile
@@ -70,12 +68,22 @@ def tile_list_mancala_kick_drift_kernel(
             nc.sync.dma_start(tile[:], page0.rearrange("(p t) c -> t p c", t=PACK)[t])
             return tile
 
-        for quad in range(QUADS):
-            nc.gpsimd.dma_start(
-                wq_plane_raw[32 * quad : 32 * quad + 4, :, :].bitcast(I32),
-                wq_scales[:, 4 * quad : 4 * quad + 4, :].rearrange("a r c -> r a c").bitcast(I32),
-            )
+        def load_wg(t):
+            tile = keep.tile([P, S], F32, name="wg%d" % t)
+            for quad in (0, 2, 1, 3):
+                nc.sync.dma_start(
+                    tile[32 * quad : 32 * quad + 32, :],
+                    wgs.rearrange("(p t) j -> t p j", t=PACK)[t],
+                )
+            return tile
+
+        wq_plane_raw = zeroed([P, PASSES, H], "wq_plane_raw", nc.gpsimd)
+        tab2_plane = zeroed([P, T], "tab2_plane", nc.vector)
+        v_plane1 = zeroed([P, S], "v_plane1", nc.vector)
+        warm = keep.tile([P, 16], F32, name="warm")
+        nc.vector.memset(warm[:, 0:8], 0.0)
         nc.scalar.activation(warm[:, 8:16], warm[:, 0:8], SIN)
+
         idx = load_list(offs, "idx")
         tab_plane = keep.tile([P, T], U8, name="tab_plane", align_bytes=64)
         tab_rows = tab_scales.rearrange("a q c -> (a q) c").bitcast(I32)
@@ -92,47 +100,49 @@ def tile_list_mancala_kick_drift_kernel(
         tab_w = [load_words(tab_words[0], "tab_w0")]
         for piece in range(6, 8):
             load_tab_rows(piece)
+        for quad in range(QUADS):
+            nc.sync.dma_start(
+                wq_plane_raw[32 * quad : 32 * quad + 4, :, :].bitcast(I32),
+                wq_scales[:, 4 * quad : 4 * quad + 4, :].rearrange("a r c -> r a c").bitcast(I32),
+            )
         wp_raw = [load_wp(0)]
         wq_raw = keep.tile([P, PASSES, 2 * H], U8, name="wq_raw", align_bytes=64)
         nc.sync.dma_start(wq_raw[:].bitcast(I32), wq_words.rearrange("a p c -> p a c").bitcast(I32))
-        tab2_plane = keep.tile([P, T], U8, name="tab2_plane", align_bytes=64)
-        for quad in range(QUADS):
-            rows = tab2_scales[0, 4 * quad : 4 * quad + 4, :].bitcast(I32)
-            nc.sync.dma_start(
-                tab2_plane[32 * quad : 32 * quad + 32, :].bitcast(I32),
-                rows.unsqueeze(0).broadcast_to([8, 4, T // 4]),
-            )
-        idx2 = load_list(offs2, "idx2")
         wp_raw.append(load_wp(1))
-        tab_w.append(load_words(tab_words[1], "tab_w1"))
         kap_sb = keep.tile([P, PACK], F32, name="kap_sb")
         nc.sync.dma_start(kap_sb[:], kap.rearrange("(p t) -> p t", t=PACK))
         gq_sb = keep.tile([P, PACK], F32, name="gq_sb")
         nc.sync.dma_start(gq_sb[:], gq.rearrange("(p t) -> p t", t=PACK))
+        tab_w.append(load_words(tab_words[1], "tab_w1"))
+        page = [load_page(0)]
+        idx2 = load_list(offs2, "idx2")
+        for quad in range(QUADS):
+            nc.sync.dma_start(
+                tab2_plane[32 * quad : 32 * quad + 4, :].bitcast(I32),
+                tab2_scales[0, 4 * quad : 4 * quad + 4, :].bitcast(I32),
+            )
+        wg = [load_wg(0)]
         idx3 = load_list(offs3, "idx3")
-        page, wg = [], []
-        for t in range(PACK):
+        for t in range(1, PACK):
             page.append(load_page(t))
-            tile = keep.tile([P, S], F32, name="wg%d" % t)
-            for quad in (0, 2, 1, 3):
-                nc.sync.dma_start(
-                    tile[32 * quad : 32 * quad + 32, :],
-                    wgs.rearrange("(p t) j -> t p j", t=PACK)[t],
-                )
-            wg.append(tile)
+            wg.append(load_wg(t))
         tab2_w = load_words(tab2_words[0], "tab2_w")
         idx4 = load_list(offs4, "idx4")
 
         v_plane = keep.tile([P, S], U8, name="v_plane", align_bytes=64)
         gather(v_plane[:], tab_plane[:], idx[:], U8)
-        nc.gpsimd.dma_start(v_plane1[0:100, :].bitcast(I32), v_plane[28:P, :].bitcast(I32))
-        v_planes = [v_plane, v_plane1]
-        v_w0 = keep.tile([P, S], U32, name="v_w0", align_bytes=64)
+        nc.gpsimd.dma_start(v_plane1[0:MOVED, :].bitcast(I32), v_plane[P - MOVED : P, :].bitcast(I32))
+        v_w0 = keep.tile([P, S], U32, name="v_w0", tag="tab_plane", align_bytes=64)
         gather(v_w0[:], tab_w[0][:], idx[:], U32)
-        wq_perm = keep.tile([P, PASSES, 2 * H], U8, name="wq_perm", align_bytes=64)
+        wq_perm = keep.tile([P, PASSES, 2 * H], U8, name="wq_perm", tag="tab_w0", align_bytes=64)
         nc.vector.tensor_copy(
             wq_perm[:].bitcast(U16).rearrange("p a (t m) -> p a t m", t=PACK),
             wq_raw[:].bitcast(U16).rearrange("p a (m t) -> p a t m", t=PACK),
+        )
+        wq_plane = keep.tile([P, PASSES, H], U8, name="wq_plane", tag="wq_raw", align_bytes=64)
+        nc.vector.tensor_copy(
+            wq_plane[:].rearrange("p a (t m) -> p a t m", t=PACK),
+            wq_plane_raw[:].rearrange("p a (m t) -> p a t m", t=PACK),
         )
 
         def quantise_wp(a, codes_tag):
@@ -146,13 +156,6 @@ def tile_list_mancala_kick_drift_kernel(
             nc.vector.quantize_mx(out=codes[:].bitcast(FP8X4), scales=plane[:], in_=grouped[:])
             return codes, plane
 
-        v2_plane = keep.tile([P, S], U8, name="v2_plane", align_bytes=64)
-        gather(v2_plane[:], tab2_plane[:], idx2[:], U8)
-        wq_plane = keep.tile([P, PASSES, H], U8, name="wq_plane", tag="tab2_plane", align_bytes=64)
-        nc.vector.tensor_copy(
-            wq_plane[:].rearrange("p a (t m) -> p a t m", t=PACK),
-            wq_plane_raw[:].rearrange("p a (m t) -> p a t m", t=PACK),
-        )
         wp_mx = [quantise_wp(0, "wq_plane_raw")]
         v_w1a = keep.tile([P, BANK], U32, name="v_w1a", tag="wp_grouped0", align_bytes=64)
         gather(v_w1a[:], tab_w[1][:], idx[:, 0:32], U32)
@@ -160,69 +163,54 @@ def tile_list_mancala_kick_drift_kernel(
         v_w1b = keep.tile([P, BANK], U32, name="v_w1b", tag="wp_grouped1", align_bytes=64)
         gather(v_w1b[:], tab_w[1][:], idx[:, 32:64], U32)
         v_w = [[v_w0[:, 0:BANK], v_w0[:, BANK:S]], [v_w1a[:], v_w1b[:]]]
-        wp_codes = [pair[0] for pair in wp_mx]
-        wp_planes = [pair[1] for pair in wp_mx]
-
-        prior_sb = []
-        for i in range(S // (2 * P)):
-            tile = keep.tile([P, 2, S], F32, name="prior_sb", tag="wide_stage", bufs=4)
-            nc.sync.dma_start(
-                tile[:], prior[2 * P * i : 2 * P * (i + 1), :].rearrange("(g p) m -> p g m", p=P)
-            )
-            prior_sb.append(tile)
 
         grouped_page = [
             keep.tile([P, BANK, PACK], BF16, name="grouped_page%d" % c, align_bytes=64)
             for c in range(T // BANK)
         ]
+        halves = [(t, u) for t in range(PACK) for u in range(S // BANK)]
 
-        halves = range(S // BANK)
-
-        def advance(t):
-            h = ring.tile([P, S], F32, name="h", align_bytes=64)
-            q, mom = [], []
-            for u in halves:
-                q.append(psum.tile([P, BANK], F32, name="q", tag="bank"))
-                mom.append(psum.tile([P, BANK], F32, name="mom", tag="bank"))
+        def products(t, u):
+            cols = slice(u * BANK, (u + 1) * BANK)
+            q = psum.tile([P, BANK], F32, name="q", tag="bank")
+            mom = psum.tile([P, BANK], F32, name="mom", tag="bank")
             for a in range(PASSES):
-                for u in halves:
-                    cols = slice(u * BANK, (u + 1) * BANK)
-                    nc.tensor.matmul_mx(
-                        out=q[u][:],
-                        lhsT=wq_perm[:, a, 2 * P * t : 2 * P * (t + 1)].bitcast(FP4X4),
-                        lhsT_scale=wq_plane[:, a, P * t : P * (t + 1)],
-                        rhs=v_w[a][u].bitcast(FP8X4),
-                        rhs_scale=v_planes[a][:, cols],
-                        start=(a == 0),
-                        stop=(a == PASSES - 1),
-                    )
-                    nc.tensor.matmul_mx(
-                        out=mom[u][:],
-                        lhsT=wp_codes[a][:, P * t : P * (t + 1)].bitcast(FP8X4),
-                        lhsT_scale=wp_planes[a][:, P * t : P * (t + 1)],
-                        rhs=v_w[a][u].bitcast(FP8X4),
-                        rhs_scale=v_planes[a][:, cols],
-                        start=(a == 0),
-                        stop=(a == PASSES - 1),
-                    )
-            neg_kicked = []
-            for u in halves:
-                sine = ring.tile([P, BANK], F32, name="sine", bufs=3)
-                nc.scalar.activation(sine[:], q[u][:], SIN)
-                tile = ring.tile([P, BANK], F32, name="neg_kicked")
-                nc.vector.scalar_tensor_tensor(
-                    tile[:], sine[:], kap_sb[:, t : t + 1], mom[u][:], MULT, SUB
+                nc.tensor.matmul_mx(
+                    out=q[:],
+                    lhsT=wq_perm[:, a, 2 * P * t : 2 * P * (t + 1)].bitcast(FP4X4),
+                    lhsT_scale=wq_plane[:, a, P * t : P * (t + 1)],
+                    rhs=v_w[a][u].bitcast(FP8X4),
+                    rhs_scale=(v_plane, v_plane1)[a][:, cols],
+                    start=(a == 0),
+                    stop=(a == PASSES - 1),
                 )
-                neg_kicked.append(tile)
-            for u in halves:
-                nc.vector.scalar_tensor_tensor(
-                    h[:, u * BANK : (u + 1) * BANK],
-                    q[u][:], gq_sb[:, t : t + 1], neg_kicked[u][:], MULT, SUB,
+            for a in range(PASSES):
+                nc.tensor.matmul_mx(
+                    out=mom[:],
+                    lhsT=wp_mx[a][0][:, P * t : P * (t + 1)].bitcast(FP8X4),
+                    lhsT_scale=wp_mx[a][1][:, P * t : P * (t + 1)],
+                    rhs=v_w[a][u].bitcast(FP8X4),
+                    rhs_scale=(v_plane, v_plane1)[a][:, cols],
+                    start=(a == 0),
+                    stop=(a == PASSES - 1),
                 )
-            return h
+            sine = keep.tile([P, BANK], F32, name="sine%d_%d" % (t, u), align_bytes=64)
+            nc.scalar.activation(sine[:], q[:], SIN)
+            state = keep.tile([P, BANK], F32, name="state%d_%d" % (t, u), align_bytes=64)
+            nc.scalar.activation(state[:], q[:], COPY, scale=gq_sb[:, t : t + 1])
+            return sine, state, mom
 
-        def scatter(t, h):
-            nc.vector.tensor_tensor(page[t][:].indirect(idx3[:]), h[:], wg[t][:], MULT)
+        def advance(t, u, sine, state, mom):
+            tag = "new%d" % ((2 * t + u) % AHEAD)
+            new = keep.tile([P, BANK], F32, name="new", tag=tag, align_bytes=64)
+            nc.vector.scalar_tensor_tensor(new[:], sine[:], kap_sb[:, t : t + 1], mom[:], MULT, SUB)
+            h = keep.tile([P, BANK], F32, name="h")
+            nc.gpsimd.tensor_tensor(h[:], state[:], new[:], SUB)
+            nc.gpsimd.tensor_tensor(new[:], h[:], wg[t][:, u * BANK : (u + 1) * BANK], MULT)
+            return new
+
+        def scatter(t, u, state):
+            nc.vector.tensor_copy(page[t][:].indirect(idx3[:, 32 * u : 32 * (u + 1)]), state[:])
 
         def interleave(t, c, on_vector):
             dst = grouped_page[c][:, :, t]
@@ -236,14 +224,25 @@ def tile_list_mancala_kick_drift_kernel(
             else:
                 nc.scalar.copy(dst, src)
 
-        hs = [advance(0)]
-        for t in range(PACK):
-            scatter(t, hs[t])
-            if t == 0:
-                hs.append(advance(1))
-            if t + 2 < PACK:
-                hs.append(advance(t + 2))
-            if t + 1 < PACK:
+        made = [products(t, u) for t, u in halves]
+        prior_sb = []
+        for i, tag in enumerate(("wp_raw0", "wp_raw1", "tab_w1", "tab_w0")):
+            tile = keep.tile([P, 2, S], F32, name="prior_sb", tag=tag, align_bytes=64)
+            nc.sync.dma_start(
+                tile[:], prior[2 * P * i : 2 * P * (i + 1), :].rearrange("(g p) m -> p g m", p=P)
+            )
+            prior_sb.append(tile)
+
+        news = [advance(*halves[0], *made[0])]
+        v2_plane = keep.tile([P, S], U8, name="v2_plane", tag="sine0_0", align_bytes=64)
+        gather(v2_plane[:], tab2_plane[:], idx2[:], U8)
+        news.extend(advance(*halves[i], *made[i]) for i in range(1, AHEAD - 1))
+        for i, (t, u) in enumerate(halves):
+            ahead = i + AHEAD - 1
+            if ahead < len(halves):
+                news.append(advance(*halves[ahead], *made[ahead]))
+            scatter(t, u, news[i])
+            if u == 1 and t + 1 < PACK:
                 for c in range(T // BANK):
                     interleave(t, c, False)
 
@@ -251,8 +250,8 @@ def tile_list_mancala_kick_drift_kernel(
         chunk_order = [0, 2, 1, 3]
         for c in range(T // BANK):
             interleave(last, c, c % 2 == 0)
-        v2_w = ring.tile([P, S], U32, name="v2_w", tag="h", align_bytes=64)
-        gather(v2_w[:, 0:256], tab2_w[:], idx2[:, 0:16], U32)
+        v2_early = keep.tile([P, 256], U32, name="v2_early", tag="new1", align_bytes=64)
+        gather(v2_early[:], tab2_w[:], idx2[:, 0:16], U32)
         page_codes, page_planes = {}, {}
         for c in chunk_order:
             codes = keep.tile([P, BANK], U32, name="page_codes%d" % c, align_bytes=64)
@@ -264,16 +263,18 @@ def tile_list_mancala_kick_drift_kernel(
             )
             page_codes[c] = codes
             page_planes[c] = plane
-        gather(v2_w[:, 256:S], tab2_w[:], idx2[:, 16:64], U32)
+        v2_late = keep.tile([P, S - 256], U32, name="v2_late", tag="grouped_page3", align_bytes=64)
+        gather(v2_late[:], tab2_w[:], idx2[:, 16:64], U32)
 
         tiles = S // P
         for n in range(tiles):
             scores = ring.tile([P, T], F32, name="scores", bufs=3)
+            words = v2_early[:, n * P : (n + 1) * P] if n < 2 else v2_late[:, (n - 2) * P : (n - 1) * P]
             for c in chunk_order:
                 e = psum.tile([P, BANK], F32, name="e", tag="bank")
                 nc.tensor.matmul_mx(
                     out=e[:],
-                    lhsT=v2_w[:, n * P : (n + 1) * P].bitcast(FP8X4),
+                    lhsT=words.bitcast(FP8X4),
                     lhsT_scale=v2_plane[:, n * P : (n + 1) * P],
                     rhs=page_codes[c][:].bitcast(FP8X4),
                     rhs_scale=page_planes[c][:],

@@ -25,7 +25,6 @@ BANK = 512
 PASSES = K // (P * PACK)
 QUADS = 4
 MOVED = 100
-AHEAD = 3
 
 
 def tile_list_mancala_kick_drift_kernel(
@@ -132,14 +131,14 @@ def tile_list_mancala_kick_drift_kernel(
         v_plane = keep.tile([P, S], U8, name="v_plane", align_bytes=64)
         gather(v_plane[:], tab_plane[:], idx[:], U8)
         nc.gpsimd.dma_start(v_plane1[0:MOVED, :].bitcast(I32), v_plane[P - MOVED : P, :].bitcast(I32))
-        v_w0 = keep.tile([P, S], U32, name="v_w0", tag="tab_plane", align_bytes=64)
+        v_w0 = keep.tile([P, S], U32, name="v_w0", align_bytes=64)
         gather(v_w0[:], tab_w[0][:], idx[:], U32)
-        wq_perm = keep.tile([P, PASSES, 2 * H], U8, name="wq_perm", tag="tab_w0", align_bytes=64)
+        wq_perm = keep.tile([P, PASSES, 2 * H], U8, name="wq_perm", tag="tab_plane", align_bytes=64)
         nc.vector.tensor_copy(
             wq_perm[:].bitcast(U16).rearrange("p a (t m) -> p a t m", t=PACK),
             wq_raw[:].bitcast(U16).rearrange("p a (m t) -> p a t m", t=PACK),
         )
-        wq_plane = keep.tile([P, PASSES, H], U8, name="wq_plane", tag="wq_raw", align_bytes=64)
+        wq_plane = keep.tile([P, PASSES, H], U8, name="wq_plane", tag="tab_w0", align_bytes=64)
         nc.vector.tensor_copy(
             wq_plane[:].rearrange("p a (t m) -> p a t m", t=PACK),
             wq_plane_raw[:].rearrange("p a (m t) -> p a t m", t=PACK),
@@ -156,11 +155,11 @@ def tile_list_mancala_kick_drift_kernel(
             nc.vector.quantize_mx(out=codes[:].bitcast(FP8X4), scales=plane[:], in_=grouped[:])
             return codes, plane
 
-        wp_mx = [quantise_wp(0, "wq_plane_raw")]
-        v_w1a = keep.tile([P, BANK], U32, name="v_w1a", tag="wp_grouped0", align_bytes=64)
+        wp_mx = [quantise_wp(0, "wq_raw")]
+        v_w1a = keep.tile([P, BANK], U32, name="v_w1a", tag="wq_plane_raw", align_bytes=64)
         gather(v_w1a[:], tab_w[1][:], idx[:, 0:32], U32)
         wp_mx.append(quantise_wp(1, "wp_codes1"))
-        v_w1b = keep.tile([P, BANK], U32, name="v_w1b", tag="wp_grouped1", align_bytes=64)
+        v_w1b = keep.tile([P, BANK], U32, name="v_w1b", tag="wp_raw1", align_bytes=64)
         gather(v_w1b[:], tab_w[1][:], idx[:, 32:64], U32)
         v_w = [[v_w0[:, 0:BANK], v_w0[:, BANK:S]], [v_w1a[:], v_w1b[:]]]
 
@@ -200,17 +199,23 @@ def tile_list_mancala_kick_drift_kernel(
             nc.scalar.activation(state[:], q[:], COPY, scale=gq_sb[:, t : t + 1])
             return sine, state, mom
 
-        def advance(t, u, sine, state, mom):
-            tag = "new%d" % ((2 * t + u) % AHEAD)
-            new = keep.tile([P, BANK], F32, name="new", tag=tag, align_bytes=64)
-            nc.vector.scalar_tensor_tensor(new[:], sine[:], kap_sb[:, t : t + 1], mom[:], MULT, SUB)
-            h = keep.tile([P, BANK], F32, name="h")
-            nc.gpsimd.tensor_tensor(h[:], state[:], new[:], SUB)
-            nc.gpsimd.tensor_tensor(new[:], h[:], wg[t][:, u * BANK : (u + 1) * BANK], MULT)
-            return new
+        new = [keep.tile([P, S], F32, name="new%d" % t, align_bytes=64) for t in range(PACK)]
 
-        def scatter(t, u, state):
-            nc.vector.tensor_copy(page[t][:].indirect(idx3[:, 32 * u : 32 * (u + 1)]), state[:])
+        def advance(t, u, sine, state, mom):
+            cols = slice(u * BANK, (u + 1) * BANK)
+            neg_kicked = keep.tile([P, BANK], F32, name="neg_kicked", tag="neg_kicked%d" % u)
+            nc.vector.scalar_tensor_tensor(
+                neg_kicked[:], sine[:], kap_sb[:, t : t + 1], mom[:], MULT, SUB
+            )
+            h = keep.tile([P, BANK], F32, name="h", align_bytes=64)
+            nc.gpsimd.tensor_tensor(h[:], state[:], neg_kicked[:], SUB)
+            nc.gpsimd.tensor_tensor(new[t][:, cols], h[:], wg[t][:, cols], MULT)
+
+        def scatter(t, first, count):
+            nc.vector.tensor_copy(
+                page[t][:].indirect(idx3[:, first // 16 : (first + count) // 16]),
+                new[t][:, first : first + count],
+            )
 
         def interleave(t, c, on_vector):
             dst = grouped_page[c][:, :, t]
@@ -226,32 +231,37 @@ def tile_list_mancala_kick_drift_kernel(
 
         made = [products(t, u) for t, u in halves]
         prior_sb = []
-        for i, tag in enumerate(("wp_raw0", "wp_raw1", "tab_w1", "tab_w0")):
+        for i, tag in enumerate(("wp_raw0", "tab_w1", "wp_raw1", "tab_w0")):
             tile = keep.tile([P, 2, S], F32, name="prior_sb", tag=tag, align_bytes=64)
             nc.sync.dma_start(
                 tile[:], prior[2 * P * i : 2 * P * (i + 1), :].rearrange("(g p) m -> p g m", p=P)
             )
             prior_sb.append(tile)
 
-        news = [advance(*halves[0], *made[0])]
+        chunk_order = [0, 2, 1, 3]
+        last = PACK - 1
+        advance(0, 0, *made[0])
         v2_plane = keep.tile([P, S], U8, name="v2_plane", tag="sine0_0", align_bytes=64)
         gather(v2_plane[:], tab2_plane[:], idx2[:], U8)
-        news.extend(advance(*halves[i], *made[i]) for i in range(1, AHEAD - 1))
-        for i, (t, u) in enumerate(halves):
-            ahead = i + AHEAD - 1
-            if ahead < len(halves):
-                news.append(advance(*halves[ahead], *made[ahead]))
-            scatter(t, u, news[i])
-            if u == 1 and t + 1 < PACK:
-                for c in range(T // BANK):
+        advance(0, 1, *made[1])
+        advance(1, 0, *made[2])
+        scatter(0, 0, BANK)
+        advance(1, 1, *made[3])
+        scatter(0, BANK, BANK)
+        for t in range(PACK):
+            if t > 0:
+                if t < last:
+                    for u in range(2):
+                        advance(t + 1, u, *made[2 * (t + 1) + u])
+                scatter(t, 0, S)
+            if t < last:
+                for c in chunk_order:
                     interleave(t, c, False)
 
-        last = PACK - 1
-        chunk_order = [0, 2, 1, 3]
+        v2_early = keep.tile([P, 256], U32, name="v2_early", tag="h", align_bytes=64)
+        gather(v2_early[:], tab2_w[:], idx2[:, 0:16], U32)
         for c in range(T // BANK):
             interleave(last, c, c % 2 == 0)
-        v2_early = keep.tile([P, 256], U32, name="v2_early", tag="new1", align_bytes=64)
-        gather(v2_early[:], tab2_w[:], idx2[:, 0:16], U32)
         page_codes, page_planes = {}, {}
         for c in chunk_order:
             codes = keep.tile([P, BANK], U32, name="page_codes%d" % c, align_bytes=64)
@@ -263,7 +273,7 @@ def tile_list_mancala_kick_drift_kernel(
             )
             page_codes[c] = codes
             page_planes[c] = plane
-        v2_late = keep.tile([P, S - 256], U32, name="v2_late", tag="grouped_page3", align_bytes=64)
+        v2_late = keep.tile([P, S - 256], U32, name="v2_late", tag="grouped_page1", align_bytes=64)
         gather(v2_late[:], tab2_w[:], idx2[:, 16:64], U32)
 
         tiles = S // P

@@ -25,6 +25,7 @@ BANK = 512
 PASSES = K // (P * PACK)
 QUADS = 4
 MOVED = 100
+LAST_WIDTHS = (512, 384, 128)
 
 
 def tile_list_mancala_kick_drift_kernel(
@@ -79,9 +80,6 @@ def tile_list_mancala_kick_drift_kernel(
         wq_plane_raw = zeroed([P, PASSES, H], "wq_plane_raw", nc.gpsimd)
         tab2_plane = zeroed([P, T], "tab2_plane", nc.vector)
         v_plane1 = zeroed([P, S], "v_plane1", nc.vector)
-        warm = keep.tile([P, 16], F32, name="warm")
-        nc.vector.memset(warm[:, 0:8], 0.0)
-        nc.scalar.activation(warm[:, 8:16], warm[:, 0:8], SIN)
 
         idx = load_list(offs, "idx")
         tab_plane = keep.tile([P, T], U8, name="tab_plane", align_bytes=64)
@@ -94,10 +92,11 @@ def tile_list_mancala_kick_drift_kernel(
                 tab_rows[first : first + 16, :],
             )
 
-        for piece in range(6):
+        pieces = (0, 4, 1, 5, 2, 6, 3, 7)
+        for piece in pieces[:6]:
             load_tab_rows(piece)
         tab_w = [load_words(tab_words[0], "tab_w0")]
-        for piece in range(6, 8):
+        for piece in pieces[6:]:
             load_tab_rows(piece)
         for quad in range(QUADS):
             nc.sync.dma_start(
@@ -169,6 +168,11 @@ def tile_list_mancala_kick_drift_kernel(
         ]
         halves = [(t, u) for t in range(PACK) for u in range(S // BANK)]
 
+        last = PACK - 1
+        new = [keep.tile([P, S], F32, name="new%d" % t, align_bytes=64) for t in range(PACK)]
+        last_sine = keep.tile([P, S], F32, name="last_sine", align_bytes=64)
+        last_state = keep.tile([P, S], F32, name="last_state", align_bytes=64)
+
         def products(t, u):
             cols = slice(u * BANK, (u + 1) * BANK)
             q = psum.tile([P, BANK], F32, name="q", tag="bank")
@@ -193,22 +197,33 @@ def tile_list_mancala_kick_drift_kernel(
                     start=(a == 0),
                     stop=(a == PASSES - 1),
                 )
-            sine = keep.tile([P, BANK], F32, name="sine%d_%d" % (t, u), align_bytes=64)
-            nc.scalar.activation(sine[:], q[:], SIN)
-            state = keep.tile([P, BANK], F32, name="state%d_%d" % (t, u), align_bytes=64)
-            nc.scalar.activation(state[:], q[:], COPY, scale=gq_sb[:, t : t + 1])
+            if t == last:
+                sine, state = last_sine[:, cols], last_state[:, cols]
+            else:
+                sine = keep.tile([P, BANK], F32, name="sine%d_%d" % (t, u), align_bytes=64)[:]
+                state = keep.tile([P, BANK], F32, name="state%d_%d" % (t, u), align_bytes=64)[:]
+            nc.scalar.activation(sine, q[:], SIN)
+            nc.scalar.activation(state, q[:], COPY, scale=gq_sb[:, t : t + 1])
+            if t == last:
+                nc.scalar.copy(new[t][:, cols], mom[:])
             return sine, state, mom
 
-        new = [keep.tile([P, S], F32, name="new%d" % t, align_bytes=64) for t in range(PACK)]
+        def advance_last():
+            nc.scalar.activation(last_sine[:], last_sine[:], COPY, scale=kap_sb[:, last : last + 1])
+            h = keep.tile([P, S], F32, name="h", align_bytes=64)
+            nc.gpsimd.tensor_tensor(h[:], last_state[:], new[last][:], ADD)
+            nc.gpsimd.tensor_tensor(h[:], h[:], last_sine[:], SUB)
+            nc.gpsimd.tensor_tensor(new[last][:], h[:], wg[last][:], MULT)
 
         def advance(t, u, sine, state, mom):
             cols = slice(u * BANK, (u + 1) * BANK)
-            neg_kicked = keep.tile([P, BANK], F32, name="neg_kicked", tag="neg_kicked%d" % u)
+            tag = ("kick0", "kick1", "kick0", "kick1", "state0_1", "kick0")[2 * t + u]
+            neg_kicked = keep.tile([P, BANK], F32, name="neg_kicked", tag=tag, align_bytes=64)
             nc.vector.scalar_tensor_tensor(
-                neg_kicked[:], sine[:], kap_sb[:, t : t + 1], mom[:], MULT, SUB
+                neg_kicked[:], sine, kap_sb[:, t : t + 1], mom[:], MULT, SUB
             )
             h = keep.tile([P, BANK], F32, name="h", align_bytes=64)
-            nc.gpsimd.tensor_tensor(h[:], state[:], neg_kicked[:], SUB)
+            nc.gpsimd.tensor_tensor(h[:], state, neg_kicked[:], SUB)
             nc.gpsimd.tensor_tensor(new[t][:, cols], h[:], wg[t][:, cols], MULT)
 
         def scatter(t, first, count):
@@ -239,7 +254,6 @@ def tile_list_mancala_kick_drift_kernel(
             prior_sb.append(tile)
 
         chunk_order = [0, 2, 1, 3]
-        last = PACK - 1
         advance(0, 0, *made[0])
         v2_plane = keep.tile([P, S], U8, name="v2_plane", tag="sine0_0", align_bytes=64)
         gather(v2_plane[:], tab2_plane[:], idx2[:], U8)
@@ -247,12 +261,12 @@ def tile_list_mancala_kick_drift_kernel(
         advance(1, 0, *made[2])
         scatter(0, 0, BANK)
         advance(1, 1, *made[3])
+        advance(2, 0, *made[4])
         scatter(0, BANK, BANK)
+        advance(2, 1, *made[5])
+        advance_last()
         for t in range(PACK):
             if t > 0:
-                if t < last:
-                    for u in range(2):
-                        advance(t + 1, u, *made[2 * (t + 1) + u])
                 scatter(t, 0, S)
             if t < last:
                 for c in chunk_order:
@@ -293,14 +307,15 @@ def tile_list_mancala_kick_drift_kernel(
                 )
                 nc.scalar.copy(scores[:, c * BANK : (c + 1) * BANK], e[:])
             picked = ring.tile([P, S], F32, name="picked", bufs=3)
-            pieces = 4 if n == tiles - 1 else 1
-            width = S // pieces
-            for i in range(pieces):
-                cols = slice(i * width, (i + 1) * width)
+            widths = LAST_WIDTHS if n == tiles - 1 else (S,)
+            first = 0
+            for width in widths:
+                cols = slice(first, first + width)
                 nc.vector.tensor_tensor(
                     picked[:, cols],
-                    scores[:].indirect(idx4[:, i * width // 16 : (i + 1) * width // 16]),
+                    scores[:].indirect(idx4[:, first // 16 : (first + width) // 16]),
                     prior_sb[n // 2][:, n % 2, cols],
                     ADD,
                 )
                 nc.sync.dma_start(out[n * P : (n + 1) * P, cols], picked[:, cols])
+                first = first + width

@@ -25,6 +25,7 @@ BANK = 512
 PASSES = K // (P * PACK)
 QUADS = 4
 MOVED = 100
+KICKED = ((0, 0), (0, 1), (1, 0), (1, 1), (2, 0))
 LAST_WIDTHS = (512, 384, 128)
 
 
@@ -37,6 +38,7 @@ def tile_list_mancala_kick_drift_kernel(
         lists = ctx.enter_context(tc.tile_pool(name="lists", bufs=1))
         keep = ctx.enter_context(tc.tile_pool(name="keep", bufs=1))
         ring = ctx.enter_context(tc.tile_pool(name="ring", bufs=2))
+        shared = ctx.enter_context(tc.tile_pool(name="shared", bufs=1))
         psum = ctx.enter_context(tc.psum_pool(name="psum", bufs=8))
 
         def load_list(src, name):
@@ -77,71 +79,65 @@ def tile_list_mancala_kick_drift_kernel(
                 )
             return tile
 
-        wq_plane_raw = zeroed([P, PASSES, H], "wq_plane_raw", nc.gpsimd)
-        tab2_plane = zeroed([P, T], "tab2_plane", nc.vector)
+        wq_plane_raw = zeroed([P, PASSES, H], "wq_plane_raw", nc.vector)
         v_plane1 = zeroed([P, S], "v_plane1", nc.vector)
+        tab2_plane = zeroed([P, T], "tab2_plane", nc.vector)
 
         idx = load_list(offs, "idx")
         tab_plane = keep.tile([P, T], U8, name="tab_plane", align_bytes=64)
         tab_rows = tab_scales.rearrange("a q c -> (a q) c").bitcast(I32)
 
-        def load_tab_rows(piece):
+        def load_tab_rows(piece, queue):
             first = 4 * (piece // 2) + 4 * (piece % 2)
-            nc.sync.dma_start(
+            queue.dma_start(
                 tab_plane[16 * piece : 16 * piece + 16, :].bitcast(I32),
                 tab_rows[first : first + 16, :],
             )
 
         pieces = (0, 4, 1, 5, 2, 6, 3, 7)
         for piece in pieces[:6]:
-            load_tab_rows(piece)
-        tab_w = [load_words(tab_words[0], "tab_w0")]
+            load_tab_rows(piece, nc.sync)
+        wp_raw = [load_wp(0)]
         for piece in pieces[6:]:
-            load_tab_rows(piece)
+            load_tab_rows(piece, nc.sync)
+        tab_w = [load_words(tab_words[0], "tab_w0")]
+        wp_raw.append(load_wp(1))
+        wq_raw = keep.tile([P, PASSES, 2 * H], U8, name="wq_raw", align_bytes=64)
+        nc.sync.dma_start(wq_raw[:].bitcast(I32), wq_words.rearrange("a p c -> p a c").bitcast(I32))
         for quad in range(QUADS):
             nc.sync.dma_start(
                 wq_plane_raw[32 * quad : 32 * quad + 4, :, :].bitcast(I32),
                 wq_scales[:, 4 * quad : 4 * quad + 4, :].rearrange("a r c -> r a c").bitcast(I32),
             )
-        wp_raw = [load_wp(0)]
-        wq_raw = keep.tile([P, PASSES, 2 * H], U8, name="wq_raw", align_bytes=64)
-        nc.sync.dma_start(wq_raw[:].bitcast(I32), wq_words.rearrange("a p c -> p a c").bitcast(I32))
-        wp_raw.append(load_wp(1))
+        tab_w.append(load_words(tab_words[1], "tab_w1"))
+        v_plane = keep.tile([P, S], U8, name="v_plane", align_bytes=64)
+        gather(v_plane[:], tab_plane[:], idx[:], U8)
+        nc.sync.dma_start(v_plane1[0:MOVED, :].bitcast(I32), v_plane[P - MOVED : P, :].bitcast(I32))
         kap_sb = keep.tile([P, PACK], F32, name="kap_sb")
         nc.sync.dma_start(kap_sb[:], kap.rearrange("(p t) -> p t", t=PACK))
         gq_sb = keep.tile([P, PACK], F32, name="gq_sb")
         nc.sync.dma_start(gq_sb[:], gq.rearrange("(p t) -> p t", t=PACK))
-        tab_w.append(load_words(tab_words[1], "tab_w1"))
+        wg = [load_wg(0)]
+        idx3 = load_list(offs3, "idx3")
         page = [load_page(0)]
+        wg.append(load_wg(1))
+        page.append(load_page(1))
         idx2 = load_list(offs2, "idx2")
         for quad in range(QUADS):
             nc.sync.dma_start(
                 tab2_plane[32 * quad : 32 * quad + 4, :].bitcast(I32),
                 tab2_scales[0, 4 * quad : 4 * quad + 4, :].bitcast(I32),
             )
-        wg = [load_wg(0)]
-        idx3 = load_list(offs3, "idx3")
-        for t in range(1, PACK):
-            page.append(load_page(t))
-            wg.append(load_wg(t))
         tab2_w = load_words(tab2_words[0], "tab2_w")
+        for t in range(2, PACK):
+            wg.append(load_wg(t))
+            page.append(load_page(t))
         idx4 = load_list(offs4, "idx4")
 
-        v_plane = keep.tile([P, S], U8, name="v_plane", align_bytes=64)
-        gather(v_plane[:], tab_plane[:], idx[:], U8)
-        nc.gpsimd.dma_start(v_plane1[0:MOVED, :].bitcast(I32), v_plane[P - MOVED : P, :].bitcast(I32))
-        v_w0 = keep.tile([P, S], U32, name="v_w0", align_bytes=64)
-        gather(v_w0[:], tab_w[0][:], idx[:], U32)
-        wq_perm = keep.tile([P, PASSES, 2 * H], U8, name="wq_perm", tag="tab_plane", align_bytes=64)
-        nc.vector.tensor_copy(
-            wq_perm[:].bitcast(U16).rearrange("p a (t m) -> p a t m", t=PACK),
-            wq_raw[:].bitcast(U16).rearrange("p a (m t) -> p a t m", t=PACK),
-        )
-        wq_plane = keep.tile([P, PASSES, H], U8, name="wq_plane", tag="tab_w0", align_bytes=64)
-        nc.vector.tensor_copy(
-            wq_plane[:].rearrange("p a (t m) -> p a t m", t=PACK),
-            wq_plane_raw[:].rearrange("p a (m t) -> p a t m", t=PACK),
-        )
+        v_w0a = keep.tile([P, BANK], U32, name="v_w0a", align_bytes=64)
+        gather(v_w0a[:], tab_w[0][:], idx[:, 0:32], U32)
+        v_w0b = keep.tile([P, BANK], U32, name="v_w0b", align_bytes=64)
+        gather(v_w0b[:], tab_w[0][:], idx[:, 32:64], U32)
 
         def quantise_wp(a, codes_tag):
             grouped = keep.tile([P, H * PACK], BF16, name="wp_grouped%d" % a, align_bytes=64)
@@ -154,76 +150,102 @@ def tile_list_mancala_kick_drift_kernel(
             nc.vector.quantize_mx(out=codes[:].bitcast(FP8X4), scales=plane[:], in_=grouped[:])
             return codes, plane
 
-        wp_mx = [quantise_wp(0, "wq_raw")]
-        v_w1a = keep.tile([P, BANK], U32, name="v_w1a", tag="wq_plane_raw", align_bytes=64)
-        gather(v_w1a[:], tab_w[1][:], idx[:, 0:32], U32)
+        wp_mx = [quantise_wp(0, "tab_w0")]
+        wq_perm = keep.tile([P, PASSES, 2 * H], U8, name="wq_perm", tag="tab_plane", align_bytes=64)
+        nc.vector.tensor_copy(
+            wq_perm[:].bitcast(U16).rearrange("p a (t m) -> p a t m", t=PACK),
+            wq_raw[:].bitcast(U16).rearrange("p a (m t) -> p a t m", t=PACK),
+        )
+        wq_plane = keep.tile([P, PASSES, H], U8, name="wq_plane", align_bytes=64)
+        nc.vector.tensor_copy(
+            wq_plane[:].rearrange("p a (t m) -> p a t m", t=PACK),
+            wq_plane_raw[:].rearrange("p a (m t) -> p a t m", t=PACK),
+        )
         wp_mx.append(quantise_wp(1, "wp_codes1"))
-        v_w1b = keep.tile([P, BANK], U32, name="v_w1b", tag="wp_raw1", align_bytes=64)
+        v_w1a = keep.tile([P, BANK], U32, name="v_w1a", align_bytes=64)
+        gather(v_w1a[:], tab_w[1][:], idx[:, 0:32], U32)
+        v_w1b = keep.tile([P, BANK], U32, name="v_w1b", tag="wp_grouped1", align_bytes=64)
         gather(v_w1b[:], tab_w[1][:], idx[:, 32:64], U32)
-        v_w = [[v_w0[:, 0:BANK], v_w0[:, BANK:S]], [v_w1a[:], v_w1b[:]]]
-
-        grouped_page = [
-            keep.tile([P, BANK, PACK], BF16, name="grouped_page%d" % c, align_bytes=64)
-            for c in range(T // BANK)
-        ]
-        halves = [(t, u) for t in range(PACK) for u in range(S // BANK)]
+        v_w = [[v_w0a[:], v_w0b[:]], [v_w1a[:], v_w1b[:]]]
 
         last = PACK - 1
-        new = [keep.tile([P, S], F32, name="new%d" % t, align_bytes=64) for t in range(PACK)]
-        last_sine = keep.tile([P, S], F32, name="last_sine", align_bytes=64)
-        last_state = keep.tile([P, S], F32, name="last_state", align_bytes=64)
+        new = [keep.tile([P, S], F32, name="new%d" % t, align_bytes=64) for t in range(last)]
+        new.append(shared.tile([P, S], F32, name="new3", offset=17408, align_bytes=64))
+        sine = [keep.tile([P, S], F32, name="sine%d" % t, align_bytes=64) for t in range(PACK)]
+        state = [keep.tile([P, S], F32, name="state%d" % t, align_bytes=64) for t in range(PACK)]
 
-        def products(t, u):
-            cols = slice(u * BANK, (u + 1) * BANK)
-            q = psum.tile([P, BANK], F32, name="q", tag="bank")
-            mom = psum.tile([P, BANK], F32, name="mom", tag="bank")
-            for a in range(PASSES):
-                nc.tensor.matmul_mx(
-                    out=q[:],
-                    lhsT=wq_perm[:, a, 2 * P * t : 2 * P * (t + 1)].bitcast(FP4X4),
-                    lhsT_scale=wq_plane[:, a, P * t : P * (t + 1)],
-                    rhs=v_w[a][u].bitcast(FP8X4),
-                    rhs_scale=(v_plane, v_plane1)[a][:, cols],
-                    start=(a == 0),
-                    stop=(a == PASSES - 1),
-                )
-            for a in range(PASSES):
-                nc.tensor.matmul_mx(
-                    out=mom[:],
-                    lhsT=wp_mx[a][0][:, P * t : P * (t + 1)].bitcast(FP8X4),
-                    lhsT_scale=wp_mx[a][1][:, P * t : P * (t + 1)],
-                    rhs=v_w[a][u].bitcast(FP8X4),
-                    rhs_scale=(v_plane, v_plane1)[a][:, cols],
-                    start=(a == 0),
-                    stop=(a == PASSES - 1),
-                )
-            if t == last:
-                sine, state = last_sine[:, cols], last_state[:, cols]
-            else:
-                sine = keep.tile([P, BANK], F32, name="sine%d_%d" % (t, u), align_bytes=64)[:]
-                state = keep.tile([P, BANK], F32, name="state%d_%d" % (t, u), align_bytes=64)[:]
-            nc.scalar.activation(sine, q[:], SIN)
-            nc.scalar.activation(state, q[:], COPY, scale=gq_sb[:, t : t + 1])
-            if t == last:
-                nc.scalar.copy(new[t][:, cols], mom[:])
-            return sine, state, mom
-
-        def advance_last():
-            nc.scalar.activation(last_sine[:], last_sine[:], COPY, scale=kap_sb[:, last : last + 1])
-            h = keep.tile([P, S], F32, name="h", align_bytes=64)
-            nc.gpsimd.tensor_tensor(h[:], last_state[:], new[last][:], ADD)
-            nc.gpsimd.tensor_tensor(h[:], h[:], last_sine[:], SUB)
-            nc.gpsimd.tensor_tensor(new[last][:], h[:], wg[last][:], MULT)
-
-        def advance(t, u, sine, state, mom):
-            cols = slice(u * BANK, (u + 1) * BANK)
-            tag = ("kick0", "kick1", "kick0", "kick1", "state0_1", "kick0")[2 * t + u]
-            neg_kicked = keep.tile([P, BANK], F32, name="neg_kicked", tag=tag, align_bytes=64)
-            nc.vector.scalar_tensor_tensor(
-                neg_kicked[:], sine, kap_sb[:, t : t + 1], mom[:], MULT, SUB
+        def q_pass(q, t, u, a):
+            nc.tensor.matmul_mx(
+                out=q[:],
+                lhsT=wq_perm[:, a, 2 * P * t : 2 * P * (t + 1)].bitcast(FP4X4),
+                lhsT_scale=wq_plane[:, a, P * t : P * (t + 1)],
+                rhs=v_w[a][u].bitcast(FP8X4),
+                rhs_scale=(v_plane, v_plane1)[a][:, u * BANK : (u + 1) * BANK],
+                start=(a == 0),
+                stop=(a == PASSES - 1),
             )
+
+        def mom_pass(mom, t, u, a):
+            nc.tensor.matmul_mx(
+                out=mom[:],
+                lhsT=wp_mx[a][0][:, P * t : P * (t + 1)].bitcast(FP8X4),
+                lhsT_scale=wp_mx[a][1][:, P * t : P * (t + 1)],
+                rhs=v_w[a][u].bitcast(FP8X4),
+                rhs_scale=(v_plane, v_plane1)[a][:, u * BANK : (u + 1) * BANK],
+                start=(a == 0),
+                stop=(a == PASSES - 1),
+            )
+
+        def open_group(name, one_pass, t, u):
+            bank = psum.tile([P, BANK], F32, name=name, tag="bank")
+            one_pass(bank, t, u, 0)
+            return bank
+
+        def products(t, u, q=None, mom=None):
+            cols = slice(u * BANK, (u + 1) * BANK)
+            if q is None:
+                q = open_group("q", q_pass, t, u)
+            q_pass(q, t, u, 1)
+            if mom is None:
+                mom = open_group("mom", mom_pass, t, u)
+            mom_pass(mom, t, u, 1)
+            if (t, u) in KICKED:
+                nc.scalar.activation(sine[t][:, cols], q[:], SIN)
+                if (t, u) != (0, 0):
+                    nc.scalar.activation(state[t][:, cols], q[:], COPY, scale=gq_sb[:, t : t + 1])
+                return q, mom
+            if (t, u) == (last, 1):
+                raw = shared.tile([P, BANK], F32, name="last_raw_sine", offset=0, align_bytes=64)
+            else:
+                raw = ring.tile([P, BANK], F32, name="raw_sine", align_bytes=64)
+            nc.scalar.activation(raw[:], q[:], SIN)
+            nc.scalar.activation(state[t][:, cols], q[:], COPY, scale=gq_sb[:, t : t + 1])
+            nc.scalar.copy(new[t][:, cols], mom[:])
+            nc.scalar.activation(sine[t][:, cols], raw[:], COPY, scale=kap_sb[:, t : t + 1])
+            return q, mom
+
+        neg_kicked = {}
+
+        def kick(t, u, mom):
+            cols = slice(u * BANK, (u + 1) * BANK)
+            tag = "first_kick" if u == 0 and t < 2 else "kick%d_%d" % (t, u)
+            neg_kicked[t, u] = keep.tile([P, BANK], F32, name="neg_kicked", tag=tag, align_bytes=64)
+            nc.vector.scalar_tensor_tensor(
+                neg_kicked[t, u][:], sine[t][:, cols], kap_sb[:, t : t + 1], mom[:], MULT, SUB
+            )
+
+        def advance(t, u, q):
+            cols = slice(u * BANK, (u + 1) * BANK)
             h = keep.tile([P, BANK], F32, name="h", align_bytes=64)
-            nc.gpsimd.tensor_tensor(h[:], state, neg_kicked[:], SUB)
+            if (t, u) == (0, 0):
+                nc.vector.scalar_tensor_tensor(
+                    h[:], q[:], gq_sb[:, t : t + 1], neg_kicked[t, u][:], MULT, SUB
+                )
+            elif (t, u) in KICKED:
+                nc.gpsimd.tensor_tensor(h[:], state[t][:, cols], neg_kicked[t, u][:], SUB)
+            else:
+                nc.gpsimd.tensor_tensor(h[:], state[t][:, cols], new[t][:, cols], ADD)
+                nc.gpsimd.tensor_tensor(h[:], h[:], sine[t][:, cols], SUB)
             nc.gpsimd.tensor_tensor(new[t][:, cols], h[:], wg[t][:, cols], MULT)
 
         def scatter(t, first, count):
@@ -232,50 +254,66 @@ def tile_list_mancala_kick_drift_kernel(
                 new[t][:, first : first + count],
             )
 
-        def interleave(t, c, on_vector):
-            dst = grouped_page[c][:, :, t]
-            src = page[t][:, c * BANK : (c + 1) * BANK]
-            if on_vector:
-                nc.vector.tensor_copy(dst, src)
-            elif t == PACK - 2 and c % 2 == 0:
-                nc.scalar.copy(
-                    grouped_page[c][:, :, t:], src.unsqueeze(2).broadcast_to([P, BANK, 2])
-                )
+        def interleave(t, c, copy, both):
+            cols = slice(c * BANK, (c + 1) * BANK)
+            src = page[t][:, cols]
+            if both:
+                copy(grouped_page[:, cols, t:], src.unsqueeze(2).broadcast_to([P, BANK, 2]))
             else:
-                nc.scalar.copy(dst, src)
+                copy(grouped_page[:, cols, t], src)
 
-        made = [products(t, u) for t, u in halves]
+        def round_on_gpsimd(dst, src):
+            nc.gpsimd.tensor_scalar(dst, src, one[:], 0.0, MULT, ADD)
+
+        made = {}
+        first = [(t, u) for u in range(S // BANK) for t in range(2)]
+        moms = [open_group("mom", mom_pass, t, u) for t, u in first]
+        qs = [open_group("q", q_pass, t, u) for t, u in first]
+        for (t, u), q, mom in zip(first, qs, moms):
+            made[t, u] = products(t, u, q, mom)
+        kick(0, 0, made[0, 0][1])
+        advance(0, 0, made[0, 0][0])
+        for t, u in ((1, 0), (0, 1), (1, 1)):
+            kick(t, u, made[t, u][1])
+        scatter(0, 0, BANK)
+        made[2, 0] = products(2, 0)
+        kick(2, 0, made[2, 0][1])
+        for t, u in ((2, 1), (3, 0), (3, 1)):
+            products(t, u)
+        for t in range(PACK):
+            for u in range(S // BANK):
+                if (t, u) != (0, 0):
+                    advance(t, u, None)
+                    scatter(t, u * BANK, BANK)
+
         prior_sb = []
-        for i, tag in enumerate(("wp_raw0", "tab_w1", "wp_raw1", "tab_w0")):
+        for i, tag in enumerate(("wp_raw0", "wp_raw1", "tab_w1", "tab_w0")):
             tile = keep.tile([P, 2, S], F32, name="prior_sb", tag=tag, align_bytes=64)
             nc.sync.dma_start(
                 tile[:], prior[2 * P * i : 2 * P * (i + 1), :].rearrange("(g p) m -> p g m", p=P)
             )
             prior_sb.append(tile)
 
-        chunk_order = [0, 2, 1, 3]
-        advance(0, 0, *made[0])
-        v2_plane = keep.tile([P, S], U8, name="v2_plane", tag="sine0_0", align_bytes=64)
-        gather(v2_plane[:], tab2_plane[:], idx2[:], U8)
-        advance(0, 1, *made[1])
-        advance(1, 0, *made[2])
-        scatter(0, 0, BANK)
-        advance(1, 1, *made[3])
-        advance(2, 0, *made[4])
-        scatter(0, BANK, BANK)
-        advance(2, 1, *made[5])
-        advance_last()
-        for t in range(PACK):
-            if t > 0:
-                scatter(t, 0, S)
-            if t < last:
-                for c in chunk_order:
-                    interleave(t, c, False)
+        grouped_page = shared.tile([P, T, PACK], BF16, name="grouped_page", offset=0, align_bytes=64)
+        for t in range(2):
+            for c in range(T // BANK):
+                interleave(t, c, nc.scalar.copy, False)
+        one = keep.tile([P, 1], F32, name="one", tag="h", align_bytes=64)
+        nc.gpsimd.memset(one[:], 1.0)
+        for c in (1, 2, 3):
+            interleave(2, c, nc.scalar.copy, c == 1)
+        interleave(2, 0, round_on_gpsimd, False)
+        for c in (2, 3):
+            interleave(last, c, nc.scalar.copy, False)
+        for c in (0, 1):
+            interleave(last, c, round_on_gpsimd, False)
 
-        v2_early = keep.tile([P, 256], U32, name="v2_early", tag="h", align_bytes=64)
-        gather(v2_early[:], tab2_w[:], idx2[:, 0:16], U32)
-        for c in range(T // BANK):
-            interleave(last, c, c % 2 == 0)
+        v2_words = shared.tile([P, S], U32, name="v2_words", offset=16384, align_bytes=64)
+        v2_plane = [shared.tile([P, BANK], U8, name="v2_plane_a", offset=20480, align_bytes=64)]
+        gather(v2_words[:, 0:BANK], tab2_w[:], idx2[:, 0:32], U32)
+        gather(v2_plane[0][:], tab2_plane[:], idx2[:, 0:32], U8)
+        gather(v2_words[:, BANK:S], tab2_w[:], idx2[:, 32:64], U32)
+        chunk_order = [2, 0, 3, 1]
         page_codes, page_planes = {}, {}
         for c in chunk_order:
             codes = keep.tile([P, BANK], U32, name="page_codes%d" % c, align_bytes=64)
@@ -283,30 +321,29 @@ def tile_list_mancala_kick_drift_kernel(
             nc.vector.quantize_mx(
                 out=codes[:].bitcast(FP8X4),
                 scales=plane[:],
-                in_=grouped_page[c][:].rearrange("p n t -> p (n t)"),
+                in_=grouped_page[:, c * BANK : (c + 1) * BANK, :].rearrange("p n t -> p (n t)"),
             )
             page_codes[c] = codes
             page_planes[c] = plane
-        v2_late = keep.tile([P, S - 256], U32, name="v2_late", tag="grouped_page1", align_bytes=64)
-        gather(v2_late[:], tab2_w[:], idx2[:, 16:64], U32)
+        v2_plane.append(shared.tile([P, BANK], U8, name="v2_plane_b", offset=0, align_bytes=64))
+        gather(v2_plane[1][:], tab2_plane[:], idx2[:, 32:64], U8)
 
         tiles = S // P
         for n in range(tiles):
             scores = ring.tile([P, T], F32, name="scores", bufs=3)
-            words = v2_early[:, n * P : (n + 1) * P] if n < 2 else v2_late[:, (n - 2) * P : (n - 1) * P]
             for c in chunk_order:
                 e = psum.tile([P, BANK], F32, name="e", tag="bank")
                 nc.tensor.matmul_mx(
                     out=e[:],
-                    lhsT=words.bitcast(FP8X4),
-                    lhsT_scale=v2_plane[:, n * P : (n + 1) * P],
+                    lhsT=v2_words[:, n * P : (n + 1) * P].bitcast(FP8X4),
+                    lhsT_scale=v2_plane[n // 4][:, (n % 4) * P : (n % 4 + 1) * P],
                     rhs=page_codes[c][:].bitcast(FP8X4),
                     rhs_scale=page_planes[c][:],
                     start=True,
                     stop=True,
                 )
                 nc.scalar.copy(scores[:, c * BANK : (c + 1) * BANK], e[:])
-            picked = ring.tile([P, S], F32, name="picked", bufs=3)
+            picked = keep.tile([P, S], F32, name="picked", tag="wg%d" % (n % 3))
             widths = LAST_WIDTHS if n == tiles - 1 else (S,)
             first = 0
             for width in widths:

@@ -25,7 +25,8 @@ BANK = 512
 PASSES = K // (P * PACK)
 QUADS = 4
 MOVED = 100
-KICKED = ((0, 0), (0, 1), (1, 0), (1, 1), (2, 0))
+KICK_AT = {(0, 0): 22528, (1, 0): 21504, (0, 1): 23552}
+KICKED = ((0, 0), (0, 1), (1, 0), (1, 1), (2, 0), (2, 1))
 LAST_WIDTHS = (512, 384, 128)
 
 
@@ -79,27 +80,16 @@ def tile_list_mancala_kick_drift_kernel(
                 )
             return tile
 
+        tab_plane = zeroed([P, T], "tab_plane", nc.gpsimd)
         wq_plane_raw = zeroed([P, PASSES, H], "wq_plane_raw", nc.vector)
         v_plane1 = zeroed([P, S], "v_plane1", nc.vector)
         tab2_plane = zeroed([P, T], "tab2_plane", nc.vector)
 
         idx = load_list(offs, "idx")
-        tab_plane = keep.tile([P, T], U8, name="tab_plane", align_bytes=64)
-        tab_rows = tab_scales.rearrange("a q c -> (a q) c").bitcast(I32)
-
-        def load_tab_rows(piece, queue):
-            first = 4 * (piece // 2) + 4 * (piece % 2)
-            queue.dma_start(
-                tab_plane[16 * piece : 16 * piece + 16, :].bitcast(I32),
-                tab_rows[first : first + 16, :],
-            )
-
-        pieces = (0, 4, 1, 5, 2, 6, 3, 7)
-        for piece in pieces[:6]:
-            load_tab_rows(piece, nc.sync)
+        tab_rows = tab_scales.rearrange("a (q r) c -> r q a c", r=4).bitcast(I32)
+        for r in range(4):
+            nc.sync.dma_start(tab_plane[r:P:16, :].bitcast(I32), tab_rows[r])
         wp_raw = [load_wp(0)]
-        for piece in pieces[6:]:
-            load_tab_rows(piece, nc.sync)
         tab_w = [load_words(tab_words[0], "tab_w0")]
         wp_raw.append(load_wp(1))
         wq_raw = keep.tile([P, PASSES, 2 * H], U8, name="wq_raw", align_bytes=64)
@@ -112,16 +102,16 @@ def tile_list_mancala_kick_drift_kernel(
         tab_w.append(load_words(tab_words[1], "tab_w1"))
         v_plane = keep.tile([P, S], U8, name="v_plane", align_bytes=64)
         gather(v_plane[:], tab_plane[:], idx[:], U8)
-        nc.sync.dma_start(v_plane1[0:MOVED, :].bitcast(I32), v_plane[P - MOVED : P, :].bitcast(I32))
+        nc.sync.dma_start(v_plane1[0:MOVED, :].bitcast(I32), v_plane[16 : 16 + MOVED, :].bitcast(I32))
         kap_sb = keep.tile([P, PACK], F32, name="kap_sb")
         nc.sync.dma_start(kap_sb[:], kap.rearrange("(p t) -> p t", t=PACK))
         gq_sb = keep.tile([P, PACK], F32, name="gq_sb")
         nc.sync.dma_start(gq_sb[:], gq.rearrange("(p t) -> p t", t=PACK))
-        wg = [load_wg(0)]
-        idx3 = load_list(offs3, "idx3")
         page = [load_page(0)]
-        wg.append(load_wg(1))
+        idx3 = load_list(offs3, "idx3")
+        wg = [load_wg(0)]
         page.append(load_page(1))
+        wg.append(load_wg(1))
         idx2 = load_list(offs2, "idx2")
         for quad in range(QUADS):
             nc.sync.dma_start(
@@ -129,8 +119,13 @@ def tile_list_mancala_kick_drift_kernel(
                 tab2_scales[0, 4 * quad : 4 * quad + 4, :].bitcast(I32),
             )
         tab2_w = load_words(tab2_words[0], "tab2_w")
+        late_wg = keep.tile([P, 2, S], F32, name="late_wg")
+        for quad in (0, 2, 1, 3):
+            nc.sync.dma_start(
+                late_wg[32 * quad : 32 * quad + 32, :, :],
+                wgs.rearrange("(p t) j -> p t j", t=PACK)[:, 2:PACK, :],
+            )
         for t in range(2, PACK):
-            wg.append(load_wg(t))
             page.append(load_page(t))
         idx4 = load_list(offs4, "idx4")
 
@@ -151,7 +146,7 @@ def tile_list_mancala_kick_drift_kernel(
             return codes, plane
 
         wp_mx = [quantise_wp(0, "tab_w0")]
-        wq_perm = keep.tile([P, PASSES, 2 * H], U8, name="wq_perm", tag="tab_plane", align_bytes=64)
+        wq_perm = keep.tile([P, PASSES, 2 * H], U8, name="wq_perm", tag="wp_grouped0", align_bytes=64)
         nc.vector.tensor_copy(
             wq_perm[:].bitcast(U16).rearrange("p a (t m) -> p a t m", t=PACK),
             wq_raw[:].bitcast(U16).rearrange("p a (m t) -> p a t m", t=PACK),
@@ -161,7 +156,7 @@ def tile_list_mancala_kick_drift_kernel(
             wq_plane[:].rearrange("p a (t m) -> p a t m", t=PACK),
             wq_plane_raw[:].rearrange("p a (m t) -> p a t m", t=PACK),
         )
-        wp_mx.append(quantise_wp(1, "wp_codes1"))
+        wp_mx.append(quantise_wp(1, "wq_plane_raw"))
         v_w1a = keep.tile([P, BANK], U32, name="v_w1a", align_bytes=64)
         gather(v_w1a[:], tab_w[1][:], idx[:, 0:32], U32)
         v_w1b = keep.tile([P, BANK], U32, name="v_w1b", tag="wp_grouped1", align_bytes=64)
@@ -169,10 +164,22 @@ def tile_list_mancala_kick_drift_kernel(
         v_w = [[v_w0a[:], v_w0b[:]], [v_w1a[:], v_w1b[:]]]
 
         last = PACK - 1
-        new = [keep.tile([P, S], F32, name="new%d" % t, align_bytes=64) for t in range(last)]
-        new.append(shared.tile([P, S], F32, name="new3", offset=17408, align_bytes=64))
-        sine = [keep.tile([P, S], F32, name="sine%d" % t, align_bytes=64) for t in range(PACK)]
-        state = [keep.tile([P, S], F32, name="state%d" % t, align_bytes=64) for t in range(PACK)]
+        halves = range(S // BANK)
+        early = [(t, u) for u in halves for t in range(2)]
+        new, sine, state, neg_kicked = {}, {}, {}, {}
+        for t, u in early:
+            sine[t, u] = keep.tile([P, BANK], F32, name="sine%d_%d" % (t, u), align_bytes=64)[:]
+            if (t, u) != (0, 0):
+                state[t, u] = keep.tile([P, BANK], F32, name="state%d_%d" % (t, u), align_bytes=64)[:]
+        late_new = {2: keep.tile([P, S], F32, name="late_new2", align_bytes=64)}
+        late_new[last] = shared.tile([P, S], F32, name="late_new3", offset=17408, align_bytes=64)
+        late_sine = {t: keep.tile([P, S], F32, name="late_sine%d" % t, align_bytes=64) for t in (2, last)}
+        late_state = {t: keep.tile([P, S], F32, name="late_state%d" % t, align_bytes=64) for t in (2, last)}
+        for t in (2, last):
+            for u in halves:
+                new[t, u] = late_new[t][:, u * BANK : (u + 1) * BANK]
+                sine[t, u] = late_sine[t][:, u * BANK : (u + 1) * BANK]
+                state[t, u] = late_state[t][:, u * BANK : (u + 1) * BANK]
 
         def q_pass(q, t, u, a):
             nc.tensor.matmul_mx(
@@ -202,7 +209,6 @@ def tile_list_mancala_kick_drift_kernel(
             return bank
 
         def products(t, u, q=None, mom=None):
-            cols = slice(u * BANK, (u + 1) * BANK)
             if q is None:
                 q = open_group("q", q_pass, t, u)
             q_pass(q, t, u, 1)
@@ -210,49 +216,49 @@ def tile_list_mancala_kick_drift_kernel(
                 mom = open_group("mom", mom_pass, t, u)
             mom_pass(mom, t, u, 1)
             if (t, u) in KICKED:
-                nc.scalar.activation(sine[t][:, cols], q[:], SIN)
+                nc.scalar.activation(sine[t, u], q[:], SIN)
                 if (t, u) != (0, 0):
-                    nc.scalar.activation(state[t][:, cols], q[:], COPY, scale=gq_sb[:, t : t + 1])
+                    nc.scalar.activation(state[t, u], q[:], COPY, scale=gq_sb[:, t : t + 1])
                 return q, mom
             if (t, u) == (last, 1):
                 raw = shared.tile([P, BANK], F32, name="last_raw_sine", offset=0, align_bytes=64)
             else:
                 raw = ring.tile([P, BANK], F32, name="raw_sine", align_bytes=64)
             nc.scalar.activation(raw[:], q[:], SIN)
-            nc.scalar.activation(state[t][:, cols], q[:], COPY, scale=gq_sb[:, t : t + 1])
-            nc.scalar.copy(new[t][:, cols], mom[:])
-            nc.scalar.activation(sine[t][:, cols], raw[:], COPY, scale=kap_sb[:, t : t + 1])
+            nc.scalar.activation(state[t, u], q[:], COPY, scale=gq_sb[:, t : t + 1])
+            nc.scalar.copy(new[t, u], mom[:])
+            nc.scalar.activation(sine[t, u], raw[:], COPY, scale=kap_sb[:, t : t + 1])
             return q, mom
 
-        neg_kicked = {}
+        def in_turn(shape):
+            return ring.tile(shape, F32, name="in_turn", bufs=6, align_bytes=64)
 
         def kick(t, u, mom):
-            cols = slice(u * BANK, (u + 1) * BANK)
-            tag = "first_kick" if u == 0 and t < 2 else "kick%d_%d" % (t, u)
-            neg_kicked[t, u] = keep.tile([P, BANK], F32, name="neg_kicked", tag=tag, align_bytes=64)
+            if (t, u) in KICK_AT:
+                neg_kicked[t, u] = shared.tile(
+                    [P, BANK], F32, name="neg_kicked%d_%d" % (t, u), offset=KICK_AT[t, u], align_bytes=64
+                )[:]
+            elif t < 2:
+                neg_kicked[t, u] = in_turn([P, BANK])[:]
+            else:
+                neg_kicked[t, u] = late_kick[:, u * BANK : (u + 1) * BANK]
             nc.vector.scalar_tensor_tensor(
-                neg_kicked[t, u][:], sine[t][:, cols], kap_sb[:, t : t + 1], mom[:], MULT, SUB
+                neg_kicked[t, u], sine[t, u], kap_sb[:, t : t + 1], mom[:], MULT, SUB
             )
 
         def advance(t, u, q):
-            cols = slice(u * BANK, (u + 1) * BANK)
             h = keep.tile([P, BANK], F32, name="h", align_bytes=64)
             if (t, u) == (0, 0):
                 nc.vector.scalar_tensor_tensor(
-                    h[:], q[:], gq_sb[:, t : t + 1], neg_kicked[t, u][:], MULT, SUB
+                    h[:], q[:], gq_sb[:, t : t + 1], neg_kicked[t, u], MULT, SUB
                 )
-            elif (t, u) in KICKED:
-                nc.gpsimd.tensor_tensor(h[:], state[t][:, cols], neg_kicked[t, u][:], SUB)
             else:
-                nc.gpsimd.tensor_tensor(h[:], state[t][:, cols], new[t][:, cols], ADD)
-                nc.gpsimd.tensor_tensor(h[:], h[:], sine[t][:, cols], SUB)
-            nc.gpsimd.tensor_tensor(new[t][:, cols], h[:], wg[t][:, cols], MULT)
+                nc.gpsimd.tensor_tensor(h[:], state[t, u], neg_kicked[t, u], SUB)
+            new[t, u] = in_turn([P, BANK])[:]
+            nc.gpsimd.tensor_tensor(new[t, u], h[:], wg[t][:, u * BANK : (u + 1) * BANK], MULT)
 
-        def scatter(t, first, count):
-            nc.vector.tensor_copy(
-                page[t][:].indirect(idx3[:, first // 16 : (first + count) // 16]),
-                new[t][:, first : first + count],
-            )
+        def scatter(t, u):
+            nc.vector.tensor_copy(page[t][:].indirect(idx3[:, 32 * u : 32 * (u + 1)]), new[t, u])
 
         def interleave(t, c, copy, both):
             cols = slice(c * BANK, (c + 1) * BANK)
@@ -266,28 +272,41 @@ def tile_list_mancala_kick_drift_kernel(
             nc.gpsimd.tensor_scalar(dst, src, one[:], 0.0, MULT, ADD)
 
         made = {}
-        first = [(t, u) for u in range(S // BANK) for t in range(2)]
-        moms = [open_group("mom", mom_pass, t, u) for t, u in first]
-        qs = [open_group("q", q_pass, t, u) for t, u in first]
-        for (t, u), q, mom in zip(first, qs, moms):
+        moms = [open_group("mom", mom_pass, t, u) for t, u in early]
+        qs = [open_group("q", q_pass, t, u) for t, u in early]
+        for (t, u), q, mom in zip(early, qs, moms):
             made[t, u] = products(t, u, q, mom)
         kick(0, 0, made[0, 0][1])
         advance(0, 0, made[0, 0][0])
-        for t, u in ((1, 0), (0, 1), (1, 1)):
+        for t, u in early[1:3]:
             kick(t, u, made[t, u][1])
-        scatter(0, 0, BANK)
-        made[2, 0] = products(2, 0)
-        kick(2, 0, made[2, 0][1])
-        for t, u in ((2, 1), (3, 0), (3, 1)):
-            products(t, u)
-        for t in range(PACK):
-            for u in range(S // BANK):
-                if (t, u) != (0, 0):
-                    advance(t, u, None)
-                    scatter(t, u * BANK, BANK)
+        scatter(0, 0)
+        advance(1, 0, None)
+        kick(1, 1, made[1, 1][1])
+        scatter(1, 0)
+        advance(0, 1, None)
+        late_kick = in_turn([P, S])
+        for u in halves:
+            kick(2, u, products(2, u)[1])
+        for u in halves:
+            products(last, u)
+        scatter(0, 1)
+        advance(1, 1, None)
+        scatter(1, 1)
+        h = keep.tile([P, S], F32, name="h", align_bytes=64)
+        nc.gpsimd.tensor_tensor(h[:], late_state[2][:], late_kick[:], SUB)
+        nc.gpsimd.tensor_tensor(late_new[2][:], h[:], late_wg[:, 0, :], MULT)
+        nc.vector.tensor_copy(page[2][:].indirect(idx3[:]), late_new[2][:])
+        h = keep.tile([P, S], F32, name="h", align_bytes=64)
+        nc.gpsimd.tensor_tensor(h[:], late_state[last][:], late_new[last][:], ADD)
+        nc.gpsimd.tensor_tensor(h[:], h[:], late_sine[last][:], SUB)
+        for u in halves:
+            cols = slice(u * BANK, (u + 1) * BANK)
+            nc.gpsimd.tensor_tensor(new[last, u], h[:, cols], late_wg[:, 1, cols], MULT)
+            scatter(last, u)
 
         prior_sb = []
-        for i, tag in enumerate(("wp_raw0", "wp_raw1", "tab_w1", "tab_w0")):
+        for i, tag in enumerate(("late_state2", "late_sine2", "late_state3", "late_sine3")):
             tile = keep.tile([P, 2, S], F32, name="prior_sb", tag=tag, align_bytes=64)
             nc.sync.dma_start(
                 tile[:], prior[2 * P * i : 2 * P * (i + 1), :].rearrange("(g p) m -> p g m", p=P)
@@ -300,13 +319,11 @@ def tile_list_mancala_kick_drift_kernel(
                 interleave(t, c, nc.scalar.copy, False)
         one = keep.tile([P, 1], F32, name="one", tag="h", align_bytes=64)
         nc.gpsimd.memset(one[:], 1.0)
-        for c in (1, 2, 3):
-            interleave(2, c, nc.scalar.copy, c == 1)
-        interleave(2, 0, round_on_gpsimd, False)
-        for c in (2, 3):
-            interleave(last, c, nc.scalar.copy, False)
-        for c in (0, 1):
-            interleave(last, c, round_on_gpsimd, False)
+        for t in (2, last):
+            for c in (2, 3):
+                interleave(t, c, nc.scalar.copy, False)
+            for c in (0, 1):
+                interleave(t, c, round_on_gpsimd, False)
 
         v2_words = shared.tile([P, S], U32, name="v2_words", offset=16384, align_bytes=64)
         v2_plane = [shared.tile([P, BANK], U8, name="v2_plane_a", offset=20480, align_bytes=64)]
@@ -330,7 +347,7 @@ def tile_list_mancala_kick_drift_kernel(
 
         tiles = S // P
         for n in range(tiles):
-            scores = ring.tile([P, T], F32, name="scores", bufs=3)
+            scores = keep.tile([P, T], F32, name="scores", tag=("wp_raw0", "wp_raw1", "tab_w1")[n % 3], align_bytes=64)
             for c in chunk_order:
                 e = psum.tile([P, BANK], F32, name="e", tag="bank")
                 nc.tensor.matmul_mx(
@@ -343,7 +360,7 @@ def tile_list_mancala_kick_drift_kernel(
                     stop=True,
                 )
                 nc.scalar.copy(scores[:, c * BANK : (c + 1) * BANK], e[:])
-            picked = keep.tile([P, S], F32, name="picked", tag="wg%d" % (n % 3))
+            picked = keep.tile([P, S], F32, name="picked", tag=("wg0", "wg1", "late_wg")[n % 3])
             widths = LAST_WIDTHS if n == tiles - 1 else (S,)
             first = 0
             for width in widths:

@@ -25,8 +25,6 @@ BANK = 512
 PASSES = K // (P * PACK)
 QUADS = 4
 MOVED = 100
-KICK_AT = {(0, 0): 22528, (1, 0): 21504, (0, 1): 23552}
-KICKED = ((0, 0), (0, 1), (1, 0), (1, 1), (2, 0), (2, 1))
 LAST_WIDTHS = (512, 384, 128)
 
 
@@ -107,11 +105,11 @@ def tile_list_mancala_kick_drift_kernel(
         nc.sync.dma_start(kap_sb[:], kap.rearrange("(p t) -> p t", t=PACK))
         gq_sb = keep.tile([P, PACK], F32, name="gq_sb")
         nc.sync.dma_start(gq_sb[:], gq.rearrange("(p t) -> p t", t=PACK))
-        page = [load_page(0)]
-        idx3 = load_list(offs3, "idx3")
         wg = [load_wg(0)]
-        page.append(load_page(1))
+        idx3 = load_list(offs3, "idx3")
+        page = [load_page(0)]
         wg.append(load_wg(1))
+        page.append(load_page(1))
         idx2 = load_list(offs2, "idx2")
         for quad in range(QUADS):
             nc.sync.dma_start(
@@ -167,10 +165,6 @@ def tile_list_mancala_kick_drift_kernel(
         halves = range(S // BANK)
         early = [(t, u) for u in halves for t in range(2)]
         new, sine, state, neg_kicked = {}, {}, {}, {}
-        for t, u in early:
-            sine[t, u] = keep.tile([P, BANK], F32, name="sine%d_%d" % (t, u), align_bytes=64)[:]
-            if (t, u) != (0, 0):
-                state[t, u] = keep.tile([P, BANK], F32, name="state%d_%d" % (t, u), align_bytes=64)[:]
         late_new = {2: keep.tile([P, S], F32, name="late_new2", align_bytes=64)}
         late_new[last] = shared.tile([P, S], F32, name="late_new3", offset=17408, align_bytes=64)
         late_sine = {t: keep.tile([P, S], F32, name="late_sine%d" % t, align_bytes=64) for t in (2, last)}
@@ -215,10 +209,13 @@ def tile_list_mancala_kick_drift_kernel(
             if mom is None:
                 mom = open_group("mom", mom_pass, t, u)
             mom_pass(mom, t, u, 1)
-            if (t, u) in KICKED:
+            if t < 2:
+                sine[t, u] = ring.tile([P, BANK], F32, name="emptied", bufs=7, align_bytes=64)[:]
                 nc.scalar.activation(sine[t, u], q[:], SIN)
-                if (t, u) != (0, 0):
-                    nc.scalar.activation(state[t, u], q[:], COPY, scale=gq_sb[:, t : t + 1])
+                return q, mom
+            if t == 2:
+                nc.scalar.activation(sine[t, u], q[:], SIN)
+                nc.scalar.activation(state[t, u], q[:], COPY, scale=gq_sb[:, t : t + 1])
                 return q, mom
             if (t, u) == (last, 1):
                 raw = shared.tile([P, BANK], F32, name="last_raw_sine", offset=0, align_bytes=64)
@@ -230,32 +227,23 @@ def tile_list_mancala_kick_drift_kernel(
             nc.scalar.activation(sine[t, u], raw[:], COPY, scale=kap_sb[:, t : t + 1])
             return q, mom
 
-        def in_turn(shape):
-            return ring.tile(shape, F32, name="in_turn", bufs=6, align_bytes=64)
+        def in_turn(width):
+            return ring.tile([P, width], F32, name="in_turn", bufs=9, align_bytes=64)
 
-        def kick(t, u, mom):
-            if (t, u) in KICK_AT:
-                neg_kicked[t, u] = shared.tile(
-                    [P, BANK], F32, name="neg_kicked%d_%d" % (t, u), offset=KICK_AT[t, u], align_bytes=64
-                )[:]
-            elif t < 2:
-                neg_kicked[t, u] = in_turn([P, BANK])[:]
-            else:
-                neg_kicked[t, u] = late_kick[:, u * BANK : (u + 1) * BANK]
-            nc.vector.scalar_tensor_tensor(
-                neg_kicked[t, u], sine[t, u], kap_sb[:, t : t + 1], mom[:], MULT, SUB
-            )
+        def kick(t, u, mom, dst):
+            neg_kicked[t, u] = dst
+            nc.vector.scalar_tensor_tensor(dst, sine[t, u], kap_sb[:, t : t + 1], mom[:], MULT, SUB)
 
-        def advance(t, u, q):
+        def advance(t, u, dst):
+            new[t, u] = dst
             h = keep.tile([P, BANK], F32, name="h", align_bytes=64)
             if (t, u) == (0, 0):
                 nc.vector.scalar_tensor_tensor(
-                    h[:], q[:], gq_sb[:, t : t + 1], neg_kicked[t, u], MULT, SUB
+                    h[:], made[t, u][0][:], gq_sb[:, t : t + 1], neg_kicked[t, u], MULT, SUB
                 )
             else:
                 nc.gpsimd.tensor_tensor(h[:], state[t, u], neg_kicked[t, u], SUB)
-            new[t, u] = in_turn([P, BANK])[:]
-            nc.gpsimd.tensor_tensor(new[t, u], h[:], wg[t][:, u * BANK : (u + 1) * BANK], MULT)
+            nc.gpsimd.tensor_tensor(dst, h[:], wg[t][:, u * BANK : (u + 1) * BANK], MULT)
 
         def scatter(t, u):
             nc.vector.tensor_copy(page[t][:].indirect(idx3[:, 32 * u : 32 * (u + 1)]), new[t, u])
@@ -276,22 +264,24 @@ def tile_list_mancala_kick_drift_kernel(
         qs = [open_group("q", q_pass, t, u) for t, u in early]
         for (t, u), q, mom in zip(early, qs, moms):
             made[t, u] = products(t, u, q, mom)
-        kick(0, 0, made[0, 0][1])
-        advance(0, 0, made[0, 0][0])
-        for t, u in early[1:3]:
-            kick(t, u, made[t, u][1])
+        for t, u in ((0, 1), (1, 0), (1, 1)):
+            state[t, u] = ring.tile([P, BANK], F32, name="emptied", bufs=7, align_bytes=64)[:]
+            nc.scalar.activation(state[t, u], made[t, u][0][:], COPY, scale=gq_sb[:, t : t + 1])
+        kick(0, 0, made[0, 0][1], in_turn(BANK)[:])
+        advance(0, 0, in_turn(BANK)[:])
+        for t, u in ((0, 1), (1, 0), (1, 1)):
+            kick(t, u, made[t, u][1], in_turn(BANK)[:])
         scatter(0, 0)
-        advance(1, 0, None)
-        kick(1, 1, made[1, 1][1])
-        scatter(1, 0)
-        advance(0, 1, None)
-        late_kick = in_turn([P, S])
+        advance(0, 1, in_turn(BANK)[:])
+        scatter(0, 1)
+        advance(1, 0, in_turn(BANK)[:])
+        late_kick = in_turn(S)
         for u in halves:
-            kick(2, u, products(2, u)[1])
+            kick(2, u, products(2, u)[1], late_kick[:, u * BANK : (u + 1) * BANK])
         for u in halves:
             products(last, u)
-        scatter(0, 1)
-        advance(1, 1, None)
+        scatter(1, 0)
+        advance(1, 1, in_turn(BANK)[:])
         scatter(1, 1)
         h = keep.tile([P, S], F32, name="h", align_bytes=64)
         nc.gpsimd.tensor_tensor(h[:], late_state[2][:], late_kick[:], SUB)
@@ -333,7 +323,7 @@ def tile_list_mancala_kick_drift_kernel(
         chunk_order = [2, 0, 3, 1]
         page_codes, page_planes = {}, {}
         for c in chunk_order:
-            codes = keep.tile([P, BANK], U32, name="page_codes%d" % c, align_bytes=64)
+            codes = keep.tile([P, BANK], U32, name="page_codes", tag=("v_w0a", "v_w0b", "v_w1a", "wp_grouped1")[c], align_bytes=64)
             plane = keep.tile([P, BANK], U8, name="page_plane%d" % c, align_bytes=64)
             nc.vector.quantize_mx(
                 out=codes[:].bitcast(FP8X4),

@@ -167,8 +167,14 @@ def tile_list_mancala_kick_drift_kernel(
         new, sine, state, neg_kicked = {}, {}, {}, {}
         late_new = {2: keep.tile([P, S], F32, name="late_new2", align_bytes=64)}
         late_new[last] = shared.tile([P, S], F32, name="late_new3", offset=17408, align_bytes=64)
-        late_sine = {t: keep.tile([P, S], F32, name="late_sine%d" % t, align_bytes=64) for t in (2, last)}
-        late_state = {t: keep.tile([P, S], F32, name="late_state%d" % t, align_bytes=64) for t in (2, last)}
+        late_sine = {
+            t: shared.tile([P, S], F32, name="late_sine%d" % t, offset=21504 + 4096 * (t - 2), align_bytes=64)
+            for t in (2, last)
+        }
+        late_state = {
+            t: shared.tile([P, S], F32, name="late_state%d" % t, offset=29696 + 4096 * (t - 2), align_bytes=64)
+            for t in (2, last)
+        }
         for t in (2, last):
             for u in halves:
                 new[t, u] = late_new[t][:, u * BANK : (u + 1) * BANK]
@@ -295,13 +301,12 @@ def tile_list_mancala_kick_drift_kernel(
             nc.gpsimd.tensor_tensor(new[last, u], h[:, cols], late_wg[:, 1, cols], MULT)
             scatter(last, u)
 
-        prior_sb = []
-        for i, tag in enumerate(("late_state2", "late_sine2", "late_state3", "late_sine3")):
-            tile = keep.tile([P, 2, S], F32, name="prior_sb", tag=tag, align_bytes=64)
+        prior_sb = shared.tile([P, S // P, S], F32, name="prior_sb", offset=20992, align_bytes=64)
+        for n in range(0, S // P, 2):
             nc.sync.dma_start(
-                tile[:], prior[2 * P * i : 2 * P * (i + 1), :].rearrange("(g p) m -> p g m", p=P)
+                prior_sb[:, n : n + 2, :],
+                prior[P * n : P * (n + 2), :].rearrange("(g p) m -> p g m", p=P),
             )
-            prior_sb.append(tile)
 
         grouped_page = shared.tile([P, T, PACK], BF16, name="grouped_page", offset=0, align_bytes=64)
         for t in range(2):
@@ -358,7 +363,7 @@ def tile_list_mancala_kick_drift_kernel(
                 nc.vector.tensor_tensor(
                     picked[:, cols],
                     scores[:].indirect(idx4[:, first // 16 : (first + width) // 16]),
-                    prior_sb[n // 2][:, n % 2, cols],
+                    prior_sb[:, n, cols],
                     ADD,
                 )
                 nc.sync.dma_start(out[n * P : (n + 1) * P, cols], picked[:, cols])

@@ -24,8 +24,9 @@ PACK = 4
 BANK = 512
 PASSES = K // (P * PACK)
 QUADS = 4
-MOVED = 100
+SPLIT = 768
 LAST_WIDTHS = (512, 384, 128)
+KB = 1024
 
 
 def tile_list_mancala_kick_drift_kernel(
@@ -38,16 +39,16 @@ def tile_list_mancala_kick_drift_kernel(
         keep = ctx.enter_context(tc.tile_pool(name="keep", bufs=1))
         ring = ctx.enter_context(tc.tile_pool(name="ring", bufs=2))
         shared = ctx.enter_context(tc.tile_pool(name="shared", bufs=1))
-        psum = ctx.enter_context(tc.psum_pool(name="psum", bufs=8))
+        psum = ctx.enter_context(tc.psum_pool(name="psum", bufs=6))
 
         def load_list(src, name):
             tile = lists.tile([P, S // 16], U16, name=name)
             nc.sync.dma_start(tile[:], src)
             return tile
 
-        def zeroed(shape, name, engine):
+        def zeroed(shape, name):
             tile = keep.tile(shape, U8, name=name, align_bytes=64)
-            engine.memset(tile[:].bitcast(I32), 0)
+            nc.vector.memset(tile[:].bitcast(I32), 0)
             return tile
 
         def load_words(src, name):
@@ -78,18 +79,30 @@ def tile_list_mancala_kick_drift_kernel(
                 )
             return tile
 
-        tab_plane = zeroed([P, T], "tab_plane", nc.gpsimd)
-        wq_plane_raw = zeroed([P, PASSES, H], "wq_plane_raw", nc.vector)
-        v_plane1 = zeroed([P, S], "v_plane1", nc.vector)
-        tab2_plane = zeroed([P, T], "tab2_plane", nc.vector)
+        def load_column(src, name):
+            tile = keep.tile([P, PACK], F32, name=name)
+            nc.sync.dma_start(tile[:], src.rearrange("(p t) -> p t", t=PACK))
+            return tile
+
+        def in_turn(width, dtype):
+            return ring.tile([P, width], dtype, name="in_turn", bufs=17, align_bytes=64)
+
+        def half(u):
+            return slice(u * BANK, (u + 1) * BANK)
+
+        tab_rows = keep.tile([P, T], U8, name="tab_rows", align_bytes=64)
+        wq_plane_raw = zeroed([P, PASSES, H], "wq_plane_raw")
+        v_planes = zeroed([P, PASSES, S], "v_planes")
+        tab2_plane = zeroed([P, T], "tab2_plane")
 
         idx = load_list(offs, "idx")
-        tab_rows = tab_scales.rearrange("a (q r) c -> r q a c", r=4).bitcast(I32)
-        for r in range(4):
-            nc.sync.dma_start(tab_plane[r:P:16, :].bitcast(I32), tab_rows[r])
-        wp_raw = [load_wp(0)]
+        nc.sync.dma_start(
+            tab_rows[0:32, :].bitcast(I32),
+            tab_scales.rearrange("a b c -> b a c").bitcast(I32),
+        )
+        nc.gpsimd.memset(tab_rows[32:64, :].bitcast(I32), 0)
+        nc.gpsimd.memset(tab_rows[64:P, :].bitcast(I32), 0)
         tab_w = [load_words(tab_words[0], "tab_w0")]
-        wp_raw.append(load_wp(1))
         wq_raw = keep.tile([P, PASSES, 2 * H], U8, name="wq_raw", align_bytes=64)
         nc.sync.dma_start(wq_raw[:].bitcast(I32), wq_words.rearrange("a p c -> p a c").bitcast(I32))
         for quad in range(QUADS):
@@ -97,211 +110,206 @@ def tile_list_mancala_kick_drift_kernel(
                 wq_plane_raw[32 * quad : 32 * quad + 4, :, :].bitcast(I32),
                 wq_scales[:, 4 * quad : 4 * quad + 4, :].rearrange("a r c -> r a c").bitcast(I32),
             )
+        kap_sb = load_column(kap, "kap_sb")
         tab_w.append(load_words(tab_words[1], "tab_w1"))
-        v_plane = keep.tile([P, S], U8, name="v_plane", align_bytes=64)
-        gather(v_plane[:], tab_plane[:], idx[:], U8)
-        nc.sync.dma_start(v_plane1[0:MOVED, :].bitcast(I32), v_plane[16 : 16 + MOVED, :].bitcast(I32))
-        kap_sb = keep.tile([P, PACK], F32, name="kap_sb")
-        nc.sync.dma_start(kap_sb[:], kap.rearrange("(p t) -> p t", t=PACK))
-        gq_sb = keep.tile([P, PACK], F32, name="gq_sb")
-        nc.sync.dma_start(gq_sb[:], gq.rearrange("(p t) -> p t", t=PACK))
-        wg = [load_wg(0)]
-        idx3 = load_list(offs3, "idx3")
-        page = [load_page(0)]
-        wg.append(load_wg(1))
-        page.append(load_page(1))
+        v_rows = keep.tile([P, S], U8, name="v_rows", align_bytes=64)
+        gather(v_rows[:], tab_rows[:], idx[:], U8)
+        for quad in range(QUADS):
+            nc.sync.dma_start(
+                v_planes[32 * quad : 32 * quad + 4, :, :].bitcast(I32),
+                v_rows[8 * quad : 8 * quad + 8, :].bitcast(I32),
+            )
+        wp_raw = [load_wp(0)]
+        gq_sb = load_column(gq, "gq_sb")
         idx2 = load_list(offs2, "idx2")
         for quad in range(QUADS):
             nc.sync.dma_start(
                 tab2_plane[32 * quad : 32 * quad + 4, :].bitcast(I32),
                 tab2_scales[0, 4 * quad : 4 * quad + 4, :].bitcast(I32),
             )
-        tab2_w = load_words(tab2_words[0], "tab2_w")
+        wp_raw.append(load_wp(1))
+        wg = [load_wg(0)]
+        idx3 = load_list(offs3, "idx3")
+        page = [load_page(0)]
+        wg.append(load_wg(1))
+        page.append(load_page(1))
         late_wg = keep.tile([P, 2, S], F32, name="late_wg")
         for quad in (0, 2, 1, 3):
             nc.sync.dma_start(
                 late_wg[32 * quad : 32 * quad + 32, :, :],
                 wgs.rearrange("(p t) j -> p t j", t=PACK)[:, 2:PACK, :],
             )
-        for t in range(2, PACK):
-            page.append(load_page(t))
+        page.append(load_page(2))
+        tab2_w = load_words(tab2_words[0], "tab2_w")
+        page.append(load_page(3))
         idx4 = load_list(offs4, "idx4")
 
-        v_w0a = keep.tile([P, BANK], U32, name="v_w0a", align_bytes=64)
-        gather(v_w0a[:], tab_w[0][:], idx[:, 0:32], U32)
-        v_w0b = keep.tile([P, BANK], U32, name="v_w0b", align_bytes=64)
-        gather(v_w0b[:], tab_w[0][:], idx[:, 32:64], U32)
-
-        def quantise_wp(a, codes_tag):
-            grouped = keep.tile([P, H * PACK], BF16, name="wp_grouped%d" % a, align_bytes=64)
-            nc.scalar.copy(
-                grouped[:].rearrange("p (t m j) -> p m t j", t=PACK, j=PACK),
-                wp_raw[a][:].rearrange("p j (m t) -> p m t j", t=PACK),
-            )
-            codes = keep.tile([P, H], U32, name="wp_codes", tag=codes_tag, align_bytes=64)
-            plane = keep.tile([P, H], U8, name="wp_plane%d" % a, align_bytes=64)
-            nc.vector.quantize_mx(out=codes[:].bitcast(FP8X4), scales=plane[:], in_=grouped[:])
-            return codes, plane
-
-        wp_mx = [quantise_wp(0, "tab_w0")]
-        wq_perm = keep.tile([P, PASSES, 2 * H], U8, name="wq_perm", tag="wp_grouped0", align_bytes=64)
-        nc.vector.tensor_copy(
-            wq_perm[:].bitcast(U16).rearrange("p a (t m) -> p a t m", t=PACK),
-            wq_raw[:].bitcast(U16).rearrange("p a (m t) -> p a t m", t=PACK),
+        v_w = []
+        for a in range(PASSES):
+            pair = []
+            for u in range(2):
+                tile = keep.tile([P, BANK], U32, name="v_w%d%d" % (a, u), align_bytes=64)
+                gather(tile[:], tab_w[a][:], idx[:, 32 * u : 32 * (u + 1)], U32)
+                pair.append(tile)
+            v_w.append(pair)
+        wq_perm = keep.tile([P, PASSES, 2 * H], U8, name="wq_perm", align_bytes=64)
+        nc.scalar.copy(
+            wq_perm[:].bitcast(U16).rearrange("p a (t m) -> p a m t", t=PACK),
+            wq_raw[:].bitcast(U16).rearrange("p a (m t) -> p a m t", t=PACK),
         )
         wq_plane = keep.tile([P, PASSES, H], U8, name="wq_plane", align_bytes=64)
-        nc.vector.tensor_copy(
+        nc.gpsimd.tensor_copy(
             wq_plane[:].rearrange("p a (t m) -> p a t m", t=PACK),
             wq_plane_raw[:].rearrange("p a (m t) -> p a t m", t=PACK),
         )
-        wp_mx.append(quantise_wp(1, "wq_plane_raw"))
-        v_w1a = keep.tile([P, BANK], U32, name="v_w1a", align_bytes=64)
-        gather(v_w1a[:], tab_w[1][:], idx[:, 0:32], U32)
-        v_w1b = keep.tile([P, BANK], U32, name="v_w1b", tag="wp_grouped1", align_bytes=64)
-        gather(v_w1b[:], tab_w[1][:], idx[:, 32:64], U32)
-        v_w = [[v_w0a[:], v_w0b[:]], [v_w1a[:], v_w1b[:]]]
+        v2_plane = [in_turn(BANK, U8)]
+        gather(v2_plane[0][:], tab2_plane[:], idx2[:, 0:32], U8)
 
         last = PACK - 1
-        halves = range(S // BANK)
-        early = [(t, u) for u in halves for t in range(2)]
-        new, sine, state, neg_kicked = {}, {}, {}, {}
-        late_new = {2: keep.tile([P, S], F32, name="late_new2", align_bytes=64)}
-        late_new[last] = shared.tile([P, S], F32, name="late_new3", offset=17408, align_bytes=64)
-        late_sine = {
-            t: shared.tile([P, S], F32, name="late_sine%d" % t, offset=21504 + 4096 * (t - 2), align_bytes=64)
-            for t in (2, last)
-        }
-        late_state = {
-            t: shared.tile([P, S], F32, name="late_state%d" % t, offset=29696 + 4096 * (t - 2), align_bytes=64)
-            for t in (2, last)
-        }
-        for t in (2, last):
-            for u in halves:
-                new[t, u] = late_new[t][:, u * BANK : (u + 1) * BANK]
-                sine[t, u] = late_sine[t][:, u * BANK : (u + 1) * BANK]
-                state[t, u] = late_state[t][:, u * BANK : (u + 1) * BANK]
 
-        def q_pass(q, t, u, a):
-            nc.tensor.matmul_mx(
-                out=q[:],
-                lhsT=wq_perm[:, a, 2 * P * t : 2 * P * (t + 1)].bitcast(FP4X4),
-                lhsT_scale=wq_plane[:, a, P * t : P * (t + 1)],
-                rhs=v_w[a][u].bitcast(FP8X4),
-                rhs_scale=(v_plane, v_plane1)[a][:, u * BANK : (u + 1) * BANK],
-                start=(a == 0),
-                stop=(a == PASSES - 1),
-            )
-
-        def mom_pass(mom, t, u, a):
-            nc.tensor.matmul_mx(
-                out=mom[:],
-                lhsT=wp_mx[a][0][:, P * t : P * (t + 1)].bitcast(FP8X4),
-                lhsT_scale=wp_mx[a][1][:, P * t : P * (t + 1)],
-                rhs=v_w[a][u].bitcast(FP8X4),
-                rhs_scale=(v_plane, v_plane1)[a][:, u * BANK : (u + 1) * BANK],
-                start=(a == 0),
-                stop=(a == PASSES - 1),
-            )
-
-        def open_group(name, one_pass, t, u):
-            bank = psum.tile([P, BANK], F32, name=name, tag="bank")
-            one_pass(bank, t, u, 0)
-            return bank
-
-        def products(t, u, q=None, mom=None):
-            if q is None:
-                q = open_group("q", q_pass, t, u)
-            q_pass(q, t, u, 1)
-            if mom is None:
-                mom = open_group("mom", mom_pass, t, u)
-            mom_pass(mom, t, u, 1)
-            if t < 2:
-                sine[t, u] = ring.tile([P, BANK], F32, name="emptied", bufs=7, align_bytes=64)[:]
-                nc.scalar.activation(sine[t, u], q[:], SIN)
-                return q, mom
-            if t == 2:
-                nc.scalar.activation(sine[t, u], q[:], SIN)
-                nc.scalar.activation(state[t, u], q[:], COPY, scale=gq_sb[:, t : t + 1])
-                return q, mom
-            if (t, u) == (last, 1):
-                raw = shared.tile([P, BANK], F32, name="last_raw_sine", offset=0, align_bytes=64)
+        def q_product(t, u):
+            if t == 1:
+                q = psum.tile([P, BANK], F32, name="q", tag="bank")
             else:
+                q = psum.tile([P, BANK], F32, name="q", tag="q_pair", bufs=2)
+            order = (0, 1) if t == 0 else (1, 0)
+            for a in order:
+                nc.tensor.matmul_mx(
+                    out=q[:],
+                    lhsT=wq_perm[:, a, 2 * P * t : 2 * P * (t + 1)].bitcast(FP4X4),
+                    lhsT_scale=wq_plane[:, a, P * t : P * (t + 1)],
+                    rhs=v_w[a][u][:].bitcast(FP8X4),
+                    rhs_scale=v_planes[:, a, half(u)],
+                    start=(a == order[0]),
+                    stop=(a == order[1]),
+                )
+            return q
+
+        wp_mx = {}
+
+        def mom_product(t, u):
+            mom = psum.tile([P, BANK], F32, name="mom", tag="bank")
+            for a in range(PASSES):
+                codes, plane = wp_mx[a, t]
+                nc.tensor.matmul_mx(
+                    out=mom[:],
+                    lhsT=codes.bitcast(FP8X4),
+                    lhsT_scale=plane,
+                    rhs=v_w[a][u][:].bitcast(FP8X4),
+                    rhs_scale=v_planes[:, a, half(u)],
+                    start=(a == 0),
+                    stop=(a == PASSES - 1),
+                )
+            return mom
+
+        def scaled_sine(t, q, dst, raw=None):
+            if raw is None:
                 raw = ring.tile([P, BANK], F32, name="raw_sine", align_bytes=64)
             nc.scalar.activation(raw[:], q[:], SIN)
-            nc.scalar.activation(state[t, u], q[:], COPY, scale=gq_sb[:, t : t + 1])
-            nc.scalar.copy(new[t, u], mom[:])
-            nc.scalar.activation(sine[t, u], raw[:], COPY, scale=kap_sb[:, t : t + 1])
-            return q, mom
+            nc.scalar.activation(dst, raw[:], COPY, scale=kap_sb[:, t : t + 1])
 
-        def in_turn(width):
-            return ring.tile([P, width], F32, name="in_turn", bufs=9, align_bytes=64)
+        def emptied():
+            return ring.tile([P, BANK], F32, name="emptied", bufs=6, align_bytes=64)
 
-        def kick(t, u, mom, dst):
-            neg_kicked[t, u] = dst
-            nc.vector.scalar_tensor_tensor(dst, sine[t, u], kap_sb[:, t : t + 1], mom[:], MULT, SUB)
+        def drift_less_sine(t, q, ksin):
+            dst = in_turn(BANK, F32)
+            nc.vector.scalar_tensor_tensor(dst[:], q[:], gq_sb[:, t : t + 1], ksin[:], MULT, SUB)
+            return dst
 
-        def advance(t, u, dst):
-            new[t, u] = dst
+        grouped = shared.tile([P, PACK, PASSES, BANK], BF16, name="grouped", offset=21 * KB, align_bytes=64)
+
+        def grouped_view(a, first, slices):
+            return grouped[:, first : first + slices, a, :].rearrange("p t (m j) -> p m t j", j=PACK)
+
+        def raw_view(a, first, slices):
+            return wp_raw[a][:].rearrange("p j (m t) -> p m t j", t=PACK)[:, :, first : first + slices, :]
+
+        def quantise_wp(first, slices):
+            width = P * PASSES * slices
+            codes = in_turn(width, U32)
+            plane = keep.tile([P, width], U8, name="wp_plane%d" % first, align_bytes=64)
+            values = grouped[:, first : first + slices, :, :].rearrange("p t a c -> p (t a c)")
+            nc.vector.quantize_mx(out=codes[:].bitcast(FP8X4), scales=plane[:], in_=values)
+            for i in range(slices):
+                for a in range(PASSES):
+                    cols = slice(P * (PASSES * i + a), P * (PASSES * i + a + 1))
+                    wp_mx[a, first + i] = (codes[:, cols], plane[:, cols])
+
+        def round_on_gpsimd(dst, src, factor):
+            nc.gpsimd.tensor_scalar(dst, src, factor, 0.0, MULT, ADD)
+
+        q = {(t, u): q_product(t, u) for t in range(2) for u in range(2)}
+        ksin, part = {}, {}
+        for u in range(2):
+            ksin[0, u] = emptied()
+            scaled_sine(0, q[0, u], ksin[0, u][:])
+            part[0, u] = drift_less_sine(0, q[0, u], ksin[0, u])
+            q[2, u] = q_product(2, u)
+
+        round_on_gpsimd(grouped_view(0, 0, PACK), raw_view(0, 0, PACK), 1.0)
+        nc.scalar.copy(grouped_view(1, 0, 1), raw_view(1, 0, 1))
+        nc.vector.tensor_copy(grouped_view(1, 1, last), raw_view(1, 1, last))
+        quantise_wp(0, 1)
+        for u in range(2):
+            ksin[1, u] = emptied()
+            scaled_sine(1, q[1, u], ksin[1, u][:], in_turn(BANK, F32))
+        quantise_wp(1, 1)
+        quantise_wp(2, 2)
+        mom = {(t, u): mom_product(t, u) for t in range(2) for u in range(2)}
+
+        def scatter(t, cols, values):
+            nc.vector.tensor_copy(page[t][:].indirect(idx3[:, cols.start // 16 : cols.stop // 16]), values)
+
+        h0 = []
+        for u in range(2):
+            h0.append(in_turn(BANK, F32))
+            nc.vector.tensor_tensor(h0[u][:], mom[0, u][:], part[0, u][:], ADD)
+        for u in range(2):
+            part[1, u] = drift_less_sine(1, q[1, u], ksin[1, u])
+        for u in range(2):
+            new0 = in_turn(BANK, F32)
+            nc.gpsimd.tensor_tensor(new0[:], h0[u][:], wg[0][:, half(u)], MULT)
+            scatter(0, half(u), new0[:])
+
+        mom1 = keep.tile([P, S], F32, name="mom1", align_bytes=64)
+        new1 = keep.tile([P, S], F32, name="new1", align_bytes=64)
+        for u in range(2):
+            nc.scalar.copy(mom1[:, half(u)], mom[1, u][:])
+        for u in range(2):
             h = keep.tile([P, BANK], F32, name="h", align_bytes=64)
-            if (t, u) == (0, 0):
-                nc.vector.scalar_tensor_tensor(
-                    h[:], made[t, u][0][:], gq_sb[:, t : t + 1], neg_kicked[t, u], MULT, SUB
-                )
+            nc.gpsimd.tensor_tensor(h[:], mom1[:, half(u)], part[1, u][:], ADD)
+            nc.gpsimd.tensor_tensor(new1[:, half(u)], h[:], wg[1][:, half(u)], MULT)
+        scatter(1, slice(0, S), new1[:])
+
+        for t in (2, last):
+            base = 21 * KB + 12 * KB * (t - 2)
+            late_sine = shared.tile([P, S], F32, name="late_sine%d" % t, offset=base, align_bytes=64)
+            late_state = shared.tile([P, S], F32, name="late_state%d" % t, offset=base + 4 * KB, align_bytes=64)
+            late_mom = shared.tile([P, S], F32, name="late_mom%d" % t, offset=base + 8 * KB, align_bytes=64)
+            for u in range(2):
+                q_late = q[t, u] if t == 2 else q_product(t, u)
+                mom_late = mom_product(t, u)
+                if (t, u) == (last, 1):
+                    raw = shared.tile([P, BANK], F32, name="last_raw_sine", offset=0, align_bytes=64)
+                else:
+                    raw = in_turn(BANK, F32)
+                nc.scalar.activation(late_state[:, half(u)], q_late[:], COPY, scale=gq_sb[:, t : t + 1])
+                nc.scalar.copy(late_mom[:, half(u)], mom_late[:])
+                scaled_sine(t, q_late, late_sine[:, half(u)], raw)
+            h = keep.tile([P, S], F32, name="h", align_bytes=64)
+            nc.gpsimd.tensor_tensor(h[:], late_state[:], late_mom[:], ADD)
+            nc.gpsimd.tensor_tensor(h[:], h[:], late_sine[:], SUB)
+            if t == 2:
+                new2 = keep.tile([P, S], F32, name="new2", align_bytes=64)
+                nc.gpsimd.tensor_tensor(new2[:], h[:], late_wg[:, 0, :], MULT)
+                scatter(2, slice(0, S), new2[:])
             else:
-                nc.gpsimd.tensor_tensor(h[:], state[t, u], neg_kicked[t, u], SUB)
-            nc.gpsimd.tensor_tensor(dst, h[:], wg[t][:, u * BANK : (u + 1) * BANK], MULT)
+                new3 = shared.tile([P, S], F32, name="new3", offset=17 * KB, align_bytes=64)
+                for u in range(2):
+                    nc.gpsimd.tensor_tensor(new3[:, half(u)], h[:, half(u)], late_wg[:, 1, half(u)], MULT)
+                    scatter(last, half(u), new3[:, half(u)])
 
-        def scatter(t, u):
-            nc.vector.tensor_copy(page[t][:].indirect(idx3[:, 32 * u : 32 * (u + 1)]), new[t, u])
-
-        def interleave(t, c, copy, both):
-            cols = slice(c * BANK, (c + 1) * BANK)
-            src = page[t][:, cols]
-            if both:
-                copy(grouped_page[:, cols, t:], src.unsqueeze(2).broadcast_to([P, BANK, 2]))
-            else:
-                copy(grouped_page[:, cols, t], src)
-
-        def round_on_gpsimd(dst, src):
-            nc.gpsimd.tensor_scalar(dst, src, one[:], 0.0, MULT, ADD)
-
-        made = {}
-        moms = [open_group("mom", mom_pass, t, u) for t, u in early]
-        qs = [open_group("q", q_pass, t, u) for t, u in early]
-        for (t, u), q, mom in zip(early, qs, moms):
-            made[t, u] = products(t, u, q, mom)
-        for t, u in ((0, 1), (1, 0), (1, 1)):
-            state[t, u] = ring.tile([P, BANK], F32, name="emptied", bufs=7, align_bytes=64)[:]
-            nc.scalar.activation(state[t, u], made[t, u][0][:], COPY, scale=gq_sb[:, t : t + 1])
-        kick(0, 0, made[0, 0][1], in_turn(BANK)[:])
-        advance(0, 0, in_turn(BANK)[:])
-        for t, u in ((0, 1), (1, 0), (1, 1)):
-            kick(t, u, made[t, u][1], in_turn(BANK)[:])
-        scatter(0, 0)
-        advance(0, 1, in_turn(BANK)[:])
-        scatter(0, 1)
-        advance(1, 0, in_turn(BANK)[:])
-        late_kick = in_turn(S)
-        for u in halves:
-            kick(2, u, products(2, u)[1], late_kick[:, u * BANK : (u + 1) * BANK])
-        for u in halves:
-            products(last, u)
-        scatter(1, 0)
-        advance(1, 1, in_turn(BANK)[:])
-        scatter(1, 1)
-        h = keep.tile([P, S], F32, name="h", align_bytes=64)
-        nc.gpsimd.tensor_tensor(h[:], late_state[2][:], late_kick[:], SUB)
-        nc.gpsimd.tensor_tensor(late_new[2][:], h[:], late_wg[:, 0, :], MULT)
-        nc.vector.tensor_copy(page[2][:].indirect(idx3[:]), late_new[2][:])
-        h = keep.tile([P, S], F32, name="h", align_bytes=64)
-        nc.gpsimd.tensor_tensor(h[:], late_state[last][:], late_new[last][:], ADD)
-        nc.gpsimd.tensor_tensor(h[:], h[:], late_sine[last][:], SUB)
-        for u in halves:
-            cols = slice(u * BANK, (u + 1) * BANK)
-            nc.gpsimd.tensor_tensor(new[last, u], h[:, cols], late_wg[:, 1, cols], MULT)
-            scatter(last, u)
-
-        prior_sb = shared.tile([P, S // P, S], F32, name="prior_sb", offset=20992, align_bytes=64)
+        prior_sb = shared.tile([P, S // P, S], F32, name="prior_sb", offset=20 * KB + 512, align_bytes=64)
         for n in range(0, S // P, 2):
             nc.sync.dma_start(
                 prior_sb[:, n : n + 2, :],
@@ -310,30 +318,27 @@ def tile_list_mancala_kick_drift_kernel(
 
         grouped_page = shared.tile([P, T, PACK], BF16, name="grouped_page", offset=0, align_bytes=64)
         for t in range(2):
-            for c in range(T // BANK):
-                interleave(t, c, nc.scalar.copy, False)
+            nc.scalar.copy(grouped_page[:, :, t], page[t][:])
         one = keep.tile([P, 1], F32, name="one", tag="h", align_bytes=64)
         nc.gpsimd.memset(one[:], 1.0)
         for t in (2, last):
-            for c in (2, 3):
-                interleave(t, c, nc.scalar.copy, False)
-            for c in (0, 1):
-                interleave(t, c, round_on_gpsimd, False)
+            for cols in (slice(2 * BANK, 3 * BANK), slice(SPLIT, 2 * BANK), slice(3 * BANK, T)):
+                nc.scalar.copy(grouped_page[:, cols, t], page[t][:, cols])
+            for cols in (slice(0, BANK), slice(BANK, SPLIT)):
+                round_on_gpsimd(grouped_page[:, cols, t], page[t][:, cols], one[:])
 
-        v2_words = shared.tile([P, S], U32, name="v2_words", offset=16384, align_bytes=64)
-        v2_plane = [shared.tile([P, BANK], U8, name="v2_plane_a", offset=20480, align_bytes=64)]
-        gather(v2_words[:, 0:BANK], tab2_w[:], idx2[:, 0:32], U32)
-        gather(v2_plane[0][:], tab2_plane[:], idx2[:, 0:32], U8)
-        gather(v2_words[:, BANK:S], tab2_w[:], idx2[:, 32:64], U32)
-        chunk_order = [2, 0, 3, 1]
+        v2_words = shared.tile([P, S], U32, name="v2_words", offset=16 * KB, align_bytes=64)
+        for u in range(2):
+            gather(v2_words[:, half(u)], tab2_w[:], idx2[:, 32 * u : 32 * (u + 1)], U32)
+        chunk_order = [2, 0, 1, 3]
         page_codes, page_planes = {}, {}
         for c in chunk_order:
-            codes = keep.tile([P, BANK], U32, name="page_codes", tag=("v_w0a", "v_w0b", "v_w1a", "wp_grouped1")[c], align_bytes=64)
+            codes = keep.tile([P, BANK], U32, name="page_codes", tag="v_w%d%d" % (c // 2, c % 2), align_bytes=64)
             plane = keep.tile([P, BANK], U8, name="page_plane%d" % c, align_bytes=64)
             nc.vector.quantize_mx(
                 out=codes[:].bitcast(FP8X4),
                 scales=plane[:],
-                in_=grouped_page[:, c * BANK : (c + 1) * BANK, :].rearrange("p n t -> p (n t)"),
+                in_=grouped_page[:, half(c), :].rearrange("p n t -> p (n t)"),
             )
             page_codes[c] = codes
             page_planes[c] = plane
@@ -354,7 +359,7 @@ def tile_list_mancala_kick_drift_kernel(
                     start=True,
                     stop=True,
                 )
-                nc.scalar.copy(scores[:, c * BANK : (c + 1) * BANK], e[:])
+                nc.scalar.copy(scores[:, half(c)], e[:])
             picked = keep.tile([P, S], F32, name="picked", tag=("wg0", "wg1", "late_wg")[n % 3])
             widths = LAST_WIDTHS if n == tiles - 1 else (S,)
             first = 0

@@ -85,7 +85,7 @@ def tile_list_mancala_kick_drift_kernel(
             return tile
 
         def in_turn(width, dtype):
-            return ring.tile([P, width], dtype, name="in_turn", bufs=17, align_bytes=64)
+            return ring.tile([P, width], dtype, name="in_turn", bufs=13, align_bytes=64)
 
         def half(u):
             return slice(u * BANK, (u + 1) * BANK)
@@ -168,7 +168,7 @@ def tile_list_mancala_kick_drift_kernel(
         last = PACK - 1
 
         def q_product(t, u):
-            if t == 1:
+            if t % 2 == 1:
                 q = psum.tile([P, BANK], F32, name="q", tag="bank")
             else:
                 q = psum.tile([P, BANK], F32, name="q", tag="q_pair", bufs=2)
@@ -211,9 +211,8 @@ def tile_list_mancala_kick_drift_kernel(
         def emptied():
             return ring.tile([P, BANK], F32, name="emptied", bufs=6, align_bytes=64)
 
-        def drift_less_sine(t, q, ksin):
-            dst = in_turn(BANK, F32)
-            nc.vector.scalar_tensor_tensor(dst[:], q[:], gq_sb[:, t : t + 1], ksin[:], MULT, SUB)
+        def drift_less_sine(t, q, ksin, dst):
+            nc.vector.scalar_tensor_tensor(dst[:], q[:], gq_sb[:, t : t + 1], ksin, MULT, SUB)
             return dst
 
         grouped = shared.tile([P, PACK, PASSES, BANK], BF16, name="grouped", offset=21 * KB, align_bytes=64)
@@ -243,7 +242,7 @@ def tile_list_mancala_kick_drift_kernel(
         for u in range(2):
             ksin[0, u] = emptied()
             scaled_sine(0, q[0, u], ksin[0, u][:])
-            part[0, u] = drift_less_sine(0, q[0, u], ksin[0, u])
+            part[0, u] = drift_less_sine(0, q[0, u], ksin[0, u][:], in_turn(BANK, F32))
             q[2, u] = q_product(2, u)
 
         round_on_gpsimd(grouped_view(0, 0, PACK), raw_view(0, 0, PACK), 1.0)
@@ -260,54 +259,69 @@ def tile_list_mancala_kick_drift_kernel(
         def scatter(t, cols, values):
             nc.vector.tensor_copy(page[t][:].indirect(idx3[:, cols.start // 16 : cols.stop // 16]), values)
 
+        def reused(name, u):
+            return keep.tile([P, BANK], F32, name="%s%d" % (name, u), align_bytes=64)
+
+        def sum_tile(width, place):
+            return shared.tile([P, width], F32, name="sum%d_%d" % (width, place), offset=(53 + 4 * place) * KB, align_bytes=64)
+
+        def late_tile(name, t, place):
+            return shared.tile([P, S], F32, name=name, offset=(21 + 12 * (t - 2) + 4 * place) * KB, align_bytes=64)
+
         h0 = []
         for u in range(2):
-            h0.append(in_turn(BANK, F32))
+            h0.append(sum_tile(BANK, u))
             nc.vector.tensor_tensor(h0[u][:], mom[0, u][:], part[0, u][:], ADD)
-        for u in range(2):
-            part[1, u] = drift_less_sine(1, q[1, u], ksin[1, u])
-        for u in range(2):
-            new0 = in_turn(BANK, F32)
-            nc.gpsimd.tensor_tensor(new0[:], h0[u][:], wg[0][:, half(u)], MULT)
-            scatter(0, half(u), new0[:])
-
+        sine2, mom2 = late_tile("sine2", 2, 0), late_tile("mom2", 2, 2)
         mom1 = keep.tile([P, S], F32, name="mom1", align_bytes=64)
-        new1 = keep.tile([P, S], F32, name="new1", align_bytes=64)
+        for u in range(2):
+            part[1, u] = drift_less_sine(1, q[1, u], ksin[1, u][:], in_turn(BANK, F32))
+            scaled_sine(2, q[2, u], sine2[:, half(u)], in_turn(BANK, F32))
         for u in range(2):
             nc.scalar.copy(mom1[:, half(u)], mom[1, u][:])
+
         for u in range(2):
-            h = keep.tile([P, BANK], F32, name="h", align_bytes=64)
-            nc.gpsimd.tensor_tensor(h[:], mom1[:, half(u)], part[1, u][:], ADD)
-            nc.gpsimd.tensor_tensor(new1[:, half(u)], h[:], wg[1][:, half(u)], MULT)
+            new0 = reused("first_new", u)
+            nc.gpsimd.tensor_tensor(new0[:], h0[u][:], wg[0][:, half(u)], MULT)
+            scatter(0, half(u), new0[:])
+        for u in range(2):
+            part[2, u] = drift_less_sine(2, q[2, u], sine2[:, half(u)], reused("first_new", u))
+
+        new1 = keep.tile([P, S], F32, name="new1", align_bytes=64)
+        h1 = []
+        for u in range(2):
+            h1.append(sum_tile(BANK, u))
+            nc.gpsimd.tensor_tensor(h1[u][:], mom1[:, half(u)], part[1, u][:], ADD)
+        for u in range(2):
+            nc.gpsimd.tensor_tensor(new1[:, half(u)], h1[u][:], wg[1][:, half(u)], MULT)
         scatter(1, slice(0, S), new1[:])
 
-        for t in (2, last):
-            base = 21 * KB + 12 * KB * (t - 2)
-            late_sine = shared.tile([P, S], F32, name="late_sine%d" % t, offset=base, align_bytes=64)
-            late_state = shared.tile([P, S], F32, name="late_state%d" % t, offset=base + 4 * KB, align_bytes=64)
-            late_mom = shared.tile([P, S], F32, name="late_mom%d" % t, offset=base + 8 * KB, align_bytes=64)
-            for u in range(2):
-                q_late = q[t, u] if t == 2 else q_product(t, u)
-                mom_late = mom_product(t, u)
-                if (t, u) == (last, 1):
-                    raw = shared.tile([P, BANK], F32, name="last_raw_sine", offset=0, align_bytes=64)
-                else:
-                    raw = in_turn(BANK, F32)
-                nc.scalar.activation(late_state[:, half(u)], q_late[:], COPY, scale=gq_sb[:, t : t + 1])
-                nc.scalar.copy(late_mom[:, half(u)], mom_late[:])
-                scaled_sine(t, q_late, late_sine[:, half(u)], raw)
-            h = keep.tile([P, S], F32, name="h", align_bytes=64)
-            nc.gpsimd.tensor_tensor(h[:], late_state[:], late_mom[:], ADD)
-            nc.gpsimd.tensor_tensor(h[:], h[:], late_sine[:], SUB)
-            if t == 2:
-                new2 = keep.tile([P, S], F32, name="new2", align_bytes=64)
-                nc.gpsimd.tensor_tensor(new2[:], h[:], late_wg[:, 0, :], MULT)
-                scatter(2, slice(0, S), new2[:])
+        for u in range(2):
+            nc.scalar.copy(mom2[:, half(u)], mom_product(2, u)[:])
+        h = sum_tile(S, 0)
+        for u in range(2):
+            nc.gpsimd.tensor_tensor(h[:, half(u)], part[2, u][:], mom2[:, half(u)], ADD)
+        new2 = keep.tile([P, S], F32, name="new2", align_bytes=64)
+        nc.gpsimd.tensor_tensor(new2[:], h[:], late_wg[:, 0, :], MULT)
+        scatter(2, slice(0, S), new2[:])
+
+        sine3, state3, mom3 = (late_tile(name, last, i) for i, name in enumerate(("sine3", "state3", "mom3")))
+        for u in range(2):
+            q3 = q_product(last, u)
+            nc.scalar.activation(state3[:, half(u)], q3[:], COPY, scale=gq_sb[:, last:PACK])
+            nc.scalar.copy(mom3[:, half(u)], mom_product(last, u)[:])
+            if u == 0:
+                raw = in_turn(BANK, F32)
             else:
-                new3 = shared.tile([P, S], F32, name="new3", offset=17 * KB, align_bytes=64)
-                for u in range(2):
-                    nc.gpsimd.tensor_tensor(new3[:, half(u)], h[:, half(u)], late_wg[:, 1, half(u)], MULT)
-                    scatter(last, half(u), new3[:, half(u)])
+                raw = shared.tile([P, BANK], F32, name="last_raw_sine", offset=0, align_bytes=64)
+            scaled_sine(last, q3, sine3[:, half(u)], raw)
+        h = sum_tile(S, 0)
+        nc.gpsimd.tensor_tensor(h[:], state3[:], mom3[:], ADD)
+        nc.gpsimd.tensor_tensor(h[:], h[:], sine3[:], SUB)
+        new3 = shared.tile([P, S], F32, name="new3", offset=17 * KB, align_bytes=64)
+        for u in range(2):
+            nc.gpsimd.tensor_tensor(new3[:, half(u)], h[:, half(u)], late_wg[:, 1, half(u)], MULT)
+            scatter(last, half(u), new3[:, half(u)])
 
         prior_sb = shared.tile([P, S // P, S], F32, name="prior_sb", offset=20 * KB + 512, align_bytes=64)
         for n in range(0, S // P, 2):
@@ -319,7 +333,7 @@ def tile_list_mancala_kick_drift_kernel(
         grouped_page = shared.tile([P, T, PACK], BF16, name="grouped_page", offset=0, align_bytes=64)
         for t in range(2):
             nc.scalar.copy(grouped_page[:, :, t], page[t][:])
-        one = keep.tile([P, 1], F32, name="one", tag="h", align_bytes=64)
+        one = sum_tile(1, 0)
         nc.gpsimd.memset(one[:], 1.0)
         for t in (2, last):
             for cols in (slice(2 * BANK, 3 * BANK), slice(SPLIT, 2 * BANK), slice(3 * BANK, T)):

@@ -158,7 +158,7 @@ def tile_list_mancala_kick_drift_kernel(
             wq_raw[:].bitcast(U16).rearrange("p a (m t) -> p a m t", t=PACK),
         )
         wq_plane = keep.tile([P, PASSES, H], U8, name="wq_plane", align_bytes=64)
-        nc.gpsimd.tensor_copy(
+        nc.vector.tensor_copy(
             wq_plane[:].rearrange("p a (t m) -> p a t m", t=PACK),
             wq_plane_raw[:].rearrange("p a (m t) -> p a t m", t=PACK),
         )
@@ -172,7 +172,7 @@ def tile_list_mancala_kick_drift_kernel(
                 q = psum.tile([P, BANK], F32, name="q", tag="bank")
             else:
                 q = psum.tile([P, BANK], F32, name="q", tag="q_pair", bufs=2)
-            order = (0, 1) if t == 0 else (1, 0)
+            order = (0, 1) if (t, u) == (0, 0) else (1, 0)
             for a in order:
                 nc.tensor.matmul_mx(
                     out=q[:],
@@ -237,23 +237,25 @@ def tile_list_mancala_kick_drift_kernel(
         def round_on_gpsimd(dst, src, factor):
             nc.gpsimd.tensor_scalar(dst, src, factor, 0.0, MULT, ADD)
 
-        q = {(t, u): q_product(t, u) for t in range(2) for u in range(2)}
+        q = {(t, u): q_product(t, u) for u in range(2) for t in range(2)}
         ksin, part = {}, {}
-        for u in range(2):
-            ksin[0, u] = emptied()
-            scaled_sine(0, q[0, u], ksin[0, u][:])
-            part[0, u] = drift_less_sine(0, q[0, u], ksin[0, u][:], in_turn(BANK, F32))
-            q[2, u] = q_product(2, u)
+        for t in range(2):
+            ksin[t, 0] = emptied()
+            scaled_sine(t, q[t, 0], ksin[t, 0][:])
+        part[0, 0] = drift_less_sine(0, q[0, 0], ksin[0, 0][:], in_turn(BANK, F32))
+        q[2, 0] = q_product(2, 0)
 
         round_on_gpsimd(grouped_view(0, 0, PACK), raw_view(0, 0, PACK), 1.0)
         nc.scalar.copy(grouped_view(1, 0, 1), raw_view(1, 0, 1))
         nc.vector.tensor_copy(grouped_view(1, 1, last), raw_view(1, 1, last))
         quantise_wp(0, 1)
-        for u in range(2):
-            ksin[1, u] = emptied()
-            scaled_sine(1, q[1, u], ksin[1, u][:], in_turn(BANK, F32))
-        quantise_wp(1, 1)
-        quantise_wp(2, 2)
+        for t in range(2):
+            ksin[t, 1] = emptied()
+            scaled_sine(t, q[t, 1], ksin[t, 1][:], in_turn(BANK, F32))
+            if t == 0:
+                part[1, 0] = drift_less_sine(1, q[1, 0], ksin[1, 0][:], in_turn(BANK, F32))
+                quantise_wp(1, 1)
+                quantise_wp(2, 2)
         mom = {(t, u): mom_product(t, u) for t in range(2) for u in range(2)}
 
         def scatter(t, cols, values):
@@ -268,15 +270,16 @@ def tile_list_mancala_kick_drift_kernel(
         def late_tile(name, t, place):
             return shared.tile([P, S], F32, name=name, offset=(21 + 12 * (t - 2) + 4 * place) * KB, align_bytes=64)
 
-        h0 = []
-        for u in range(2):
-            h0.append(sum_tile(BANK, u))
-            nc.vector.tensor_tensor(h0[u][:], mom[0, u][:], part[0, u][:], ADD)
+        h0 = [sum_tile(BANK, 0), sum_tile(BANK, 1)]
+        nc.vector.tensor_tensor(h0[0][:], mom[0, 0][:], part[0, 0][:], ADD)
+        part[0, 1] = drift_less_sine(0, q[0, 1], ksin[0, 1][:], in_turn(BANK, F32))
+        q[2, 1] = q_product(2, 1)
         sine2, mom2 = late_tile("sine2", 2, 0), late_tile("mom2", 2, 2)
         mom1 = keep.tile([P, S], F32, name="mom1", align_bytes=64)
-        for u in range(2):
-            part[1, u] = drift_less_sine(1, q[1, u], ksin[1, u][:], in_turn(BANK, F32))
-            scaled_sine(2, q[2, u], sine2[:, half(u)], in_turn(BANK, F32))
+        scaled_sine(2, q[2, 0], sine2[:, half(0)], in_turn(BANK, F32))
+        part[1, 1] = drift_less_sine(1, q[1, 1], ksin[1, 1][:], in_turn(BANK, F32))
+        nc.vector.tensor_tensor(h0[1][:], mom[0, 1][:], part[0, 1][:], ADD)
+        scaled_sine(2, q[2, 1], sine2[:, half(1)], in_turn(BANK, F32))
         for u in range(2):
             nc.scalar.copy(mom1[:, half(u)], mom[1, u][:])
 

@@ -91,9 +91,10 @@ def tile_list_mancala_kick_drift_kernel(
             return slice(u * BANK, (u + 1) * BANK)
 
         tab_rows = keep.tile([P, T], U8, name="tab_rows", align_bytes=64)
+        tab2_rows = keep.tile([P, T], U8, name="tab2_rows", align_bytes=64)
         wq_plane_raw = zeroed([P, PASSES, H], "wq_plane_raw")
         v_planes = zeroed([P, PASSES, S], "v_planes")
-        tab2_plane = zeroed([P, T], "tab2_plane")
+        v2_plane = zeroed([P, S], "v2_plane")
 
         idx = load_list(offs, "idx")
         nc.sync.dma_start(
@@ -102,19 +103,18 @@ def tile_list_mancala_kick_drift_kernel(
         )
         nc.gpsimd.memset(tab_rows[32:64, :].bitcast(I32), 0)
         nc.gpsimd.memset(tab_rows[64:P, :].bitcast(I32), 0)
+        nc.gpsimd.memset(tab2_rows[:].bitcast(I32), 0)
         tab_w = [load_words(tab_words[0], "tab_w0")]
         wq_raw = keep.tile([P, PASSES, 2 * H], U8, name="wq_raw", align_bytes=64)
         nc.sync.dma_start(wq_raw[:].bitcast(I32), wq_words.rearrange("a p c -> p a c").bitcast(I32))
-        for quad in range(QUADS):
-            nc.sync.dma_start(
-                wq_plane_raw[32 * quad : 32 * quad + 4, :, :].bitcast(I32),
-                wq_scales[:, 4 * quad : 4 * quad + 4, :].rearrange("a r c -> r a c").bitcast(I32),
-            )
+        wq_rows = wq_scales.rearrange("a (q r) c -> r q a c", r=4).bitcast(I32)
+        for r in range(4):
+            nc.sync.dma_start(wq_plane_raw[r:P:32, :, :].bitcast(I32), wq_rows[r])
         kap_sb = load_column(kap, "kap_sb")
         tab_w.append(load_words(tab_words[1], "tab_w1"))
         v_rows = keep.tile([P, S], U8, name="v_rows", align_bytes=64)
         gather(v_rows[:], tab_rows[:], idx[:], U8)
-        for quad in range(QUADS):
+        for quad in (0, 2, 1, 3):
             nc.sync.dma_start(
                 v_planes[32 * quad : 32 * quad + 4, :, :].bitcast(I32),
                 v_rows[8 * quad : 8 * quad + 8, :].bitcast(I32),
@@ -122,11 +122,7 @@ def tile_list_mancala_kick_drift_kernel(
         wp_raw = [load_wp(0)]
         gq_sb = load_column(gq, "gq_sb")
         idx2 = load_list(offs2, "idx2")
-        for quad in range(QUADS):
-            nc.sync.dma_start(
-                tab2_plane[32 * quad : 32 * quad + 4, :].bitcast(I32),
-                tab2_scales[0, 4 * quad : 4 * quad + 4, :].bitcast(I32),
-            )
+        nc.sync.dma_start(tab2_rows[0:16, :].bitcast(I32), tab2_scales[0].bitcast(I32))
         wp_raw.append(load_wp(1))
         wg = [load_wg(0)]
         idx3 = load_list(offs3, "idx3")
@@ -144,14 +140,15 @@ def tile_list_mancala_kick_drift_kernel(
         page.append(load_page(3))
         idx4 = load_list(offs4, "idx4")
 
-        v_w = []
-        for a in range(PASSES):
+        def gather_words(a):
             pair = []
             for u in range(2):
                 tile = keep.tile([P, BANK], U32, name="v_w%d%d" % (a, u), align_bytes=64)
                 gather(tile[:], tab_w[a][:], idx[:, 32 * u : 32 * (u + 1)], U32)
                 pair.append(tile)
-            v_w.append(pair)
+            return pair
+
+        v_w = [gather_words(0)]
         wq_perm = keep.tile([P, PASSES, 2 * H], U8, name="wq_perm", align_bytes=64)
         nc.scalar.copy(
             wq_perm[:].bitcast(U16).rearrange("p a (t m) -> p a m t", t=PACK),
@@ -162,8 +159,14 @@ def tile_list_mancala_kick_drift_kernel(
             wq_plane[:].rearrange("p a (t m) -> p a t m", t=PACK),
             wq_plane_raw[:].rearrange("p a (m t) -> p a t m", t=PACK),
         )
-        v2_plane = [in_turn(BANK, U8)]
-        gather(v2_plane[0][:], tab2_plane[:], idx2[:, 0:32], U8)
+
+        def gather_v2_scales(u, rows):
+            gather(rows[:], tab2_rows[:], idx2[:, 32 * u : 32 * (u + 1)], U8)
+            for r in range(4):
+                nc.sync.dma_start(v2_plane[r:P:32, half(u)].bitcast(I32), rows[r:16:4, :].bitcast(I32))
+
+        v_w.append(gather_words(1))
+        gather_v2_scales(0, in_turn(BANK, U8))
 
         last = PACK - 1
 
@@ -261,9 +264,6 @@ def tile_list_mancala_kick_drift_kernel(
         def scatter(t, cols, values):
             nc.vector.tensor_copy(page[t][:].indirect(idx3[:, cols.start // 16 : cols.stop // 16]), values)
 
-        def reused(name, u):
-            return keep.tile([P, BANK], F32, name="%s%d" % (name, u), align_bytes=64)
-
         def sum_tile(width, place):
             return shared.tile([P, width], F32, name="sum%d_%d" % (width, place), offset=(53 + 4 * place) * KB, align_bytes=64)
 
@@ -279,31 +279,33 @@ def tile_list_mancala_kick_drift_kernel(
         scaled_sine(2, q[2, 0], sine2[:, half(0)], in_turn(BANK, F32))
         part[1, 1] = drift_less_sine(1, q[1, 1], ksin[1, 1][:], in_turn(BANK, F32))
         nc.vector.tensor_tensor(h0[1][:], mom[0, 1][:], part[0, 1][:], ADD)
+        nc.scalar.copy(mom1[:, half(0)], mom[1, 0][:])
         scaled_sine(2, q[2, 1], sine2[:, half(1)], in_turn(BANK, F32))
-        for u in range(2):
-            nc.scalar.copy(mom1[:, half(u)], mom[1, u][:])
+        nc.scalar.copy(mom1[:, half(1)], mom[1, 1][:])
 
+        def chained(name, offset):
+            return shared.tile([P, BANK], F32, name=name, offset=59 * KB + offset, align_bytes=64)
+
+        new0 = [chained("new00", KB), chained("new01", 6 * KB)]
+        nc.gpsimd.tensor_tensor(new0[0][:], h0[0][:], wg[0][:, half(0)], MULT)
+        scatter(0, half(0), new0[0][:])
+        nc.gpsimd.tensor_tensor(new0[1][:], h0[1][:], wg[0][:, half(1)], MULT)
+        part2 = shared.tile([P, S], F32, name="part2", offset=61 * KB, align_bytes=64)
         for u in range(2):
-            new0 = reused("first_new", u)
-            nc.gpsimd.tensor_tensor(new0[:], h0[u][:], wg[0][:, half(u)], MULT)
-            scatter(0, half(u), new0[:])
-        for u in range(2):
-            part[2, u] = drift_less_sine(2, q[2, u], sine2[:, half(u)], reused("first_new", u))
+            drift_less_sine(2, q[2, u], sine2[:, half(u)], part2[:, half(u)])
+        scatter(0, half(1), new0[1][:])
 
         new1 = keep.tile([P, S], F32, name="new1", align_bytes=64)
-        h1 = []
         for u in range(2):
-            h1.append(sum_tile(BANK, u))
-            nc.gpsimd.tensor_tensor(h1[u][:], mom1[:, half(u)], part[1, u][:], ADD)
-        for u in range(2):
-            nc.gpsimd.tensor_tensor(new1[:, half(u)], h1[u][:], wg[1][:, half(u)], MULT)
+            h = sum_tile(BANK, u)
+            nc.gpsimd.tensor_tensor(h[:], mom1[:, half(u)], part[1, u][:], ADD)
+            nc.gpsimd.tensor_tensor(new1[:, half(u)], h[:], wg[1][:, half(u)], MULT)
         scatter(1, slice(0, S), new1[:])
 
         for u in range(2):
             nc.scalar.copy(mom2[:, half(u)], mom_product(2, u)[:])
         h = sum_tile(S, 0)
-        for u in range(2):
-            nc.gpsimd.tensor_tensor(h[:, half(u)], part[2, u][:], mom2[:, half(u)], ADD)
+        nc.gpsimd.tensor_tensor(h[:], part2[:], mom2[:], ADD)
         new2 = keep.tile([P, S], F32, name="new2", align_bytes=64)
         nc.gpsimd.tensor_tensor(new2[:], h[:], late_wg[:, 0, :], MULT)
         scatter(2, slice(0, S), new2[:])
@@ -359,8 +361,7 @@ def tile_list_mancala_kick_drift_kernel(
             )
             page_codes[c] = codes
             page_planes[c] = plane
-        v2_plane.append(shared.tile([P, BANK], U8, name="v2_plane_b", offset=0, align_bytes=64))
-        gather(v2_plane[1][:], tab2_plane[:], idx2[:, 32:64], U8)
+        gather_v2_scales(1, shared.tile([P, BANK], U8, name="v2_rows_b", offset=0, align_bytes=64))
 
         tiles = S // P
         for n in range(tiles):
@@ -370,7 +371,7 @@ def tile_list_mancala_kick_drift_kernel(
                 nc.tensor.matmul_mx(
                     out=e[:],
                     lhsT=v2_words[:, n * P : (n + 1) * P].bitcast(FP8X4),
-                    lhsT_scale=v2_plane[n // 4][:, (n % 4) * P : (n % 4 + 1) * P],
+                    lhsT_scale=v2_plane[:, n * P : (n + 1) * P],
                     rhs=page_codes[c][:].bitcast(FP8X4),
                     rhs_scale=page_planes[c][:],
                     start=True,

@@ -39,7 +39,7 @@ def tile_list_mancala_kick_drift_kernel(
         keep = ctx.enter_context(tc.tile_pool(name="keep", bufs=1))
         ring = ctx.enter_context(tc.tile_pool(name="ring", bufs=2))
         shared = ctx.enter_context(tc.tile_pool(name="shared", bufs=1))
-        psum = ctx.enter_context(tc.psum_pool(name="psum", bufs=6))
+        psum = ctx.enter_context(tc.psum_pool(name="psum", bufs=8))
 
         def load_list(src, name):
             tile = lists.tile([P, S // 16], U16, name=name)
@@ -84,14 +84,12 @@ def tile_list_mancala_kick_drift_kernel(
             nc.sync.dma_start(tile[:], src.rearrange("(p t) -> p t", t=PACK))
             return tile
 
-        def in_turn(width, dtype):
-            return ring.tile([P, width], dtype, name="in_turn", bufs=13, align_bytes=64)
-
         def half(u):
             return slice(u * BANK, (u + 1) * BANK)
 
         tab_rows = keep.tile([P, T], U8, name="tab_rows", align_bytes=64)
         tab2_rows = keep.tile([P, T], U8, name="tab2_rows", align_bytes=64)
+        nc.gpsimd.memset(tab2_rows[0:32, :].bitcast(I32), 0)
         wq_plane_raw = zeroed([P, PASSES, H], "wq_plane_raw")
         v_planes = zeroed([P, PASSES, S], "v_planes")
         v2_plane = zeroed([P, S], "v2_plane")
@@ -103,15 +101,17 @@ def tile_list_mancala_kick_drift_kernel(
         )
         nc.gpsimd.memset(tab_rows[32:64, :].bitcast(I32), 0)
         nc.gpsimd.memset(tab_rows[64:P, :].bitcast(I32), 0)
-        nc.gpsimd.memset(tab2_rows[:].bitcast(I32), 0)
-        tab_w = [load_words(tab_words[0], "tab_w0")]
+        idx2 = load_list(offs2, "idx2")
+        nc.sync.dma_start(tab2_rows[0:16, :].bitcast(I32), tab2_scales[0].bitcast(I32))
+        nc.gpsimd.memset(tab2_rows[32:64, :].bitcast(I32), 0)
+        nc.gpsimd.memset(tab2_rows[64:P, :].bitcast(I32), 0)
+        wp_raw = [load_wp(0)]
         wq_raw = keep.tile([P, PASSES, 2 * H], U8, name="wq_raw", align_bytes=64)
         nc.sync.dma_start(wq_raw[:].bitcast(I32), wq_words.rearrange("a p c -> p a c").bitcast(I32))
         wq_rows = wq_scales.rearrange("a (q r) c -> r q a c", r=4).bitcast(I32)
         for r in range(4):
             nc.sync.dma_start(wq_plane_raw[r:P:32, :, :].bitcast(I32), wq_rows[r])
-        kap_sb = load_column(kap, "kap_sb")
-        tab_w.append(load_words(tab_words[1], "tab_w1"))
+        tab_w = [load_words(tab_words[0], "tab_w0")]
         v_rows = keep.tile([P, S], U8, name="v_rows", align_bytes=64)
         gather(v_rows[:], tab_rows[:], idx[:], U8)
         for quad in (0, 2, 1, 3):
@@ -119,11 +119,10 @@ def tile_list_mancala_kick_drift_kernel(
                 v_planes[32 * quad : 32 * quad + 4, :, :].bitcast(I32),
                 v_rows[8 * quad : 8 * quad + 8, :].bitcast(I32),
             )
-        wp_raw = [load_wp(0)]
-        gq_sb = load_column(gq, "gq_sb")
-        idx2 = load_list(offs2, "idx2")
-        nc.sync.dma_start(tab2_rows[0:16, :].bitcast(I32), tab2_scales[0].bitcast(I32))
         wp_raw.append(load_wp(1))
+        tab_w.append(load_words(tab_words[1], "tab_w1"))
+        kap_sb = load_column(kap, "kap_sb")
+        gq_sb = load_column(gq, "gq_sb")
         wg = [load_wg(0)]
         idx3 = load_list(offs3, "idx3")
         page = [load_page(0)]
@@ -140,6 +139,11 @@ def tile_list_mancala_kick_drift_kernel(
         page.append(load_page(3))
         idx4 = load_list(offs4, "idx4")
 
+        v2_rows = keep.tile([P, S], U8, name="v2_rows", align_bytes=64)
+        gather(v2_rows[:], tab2_rows[:], idx2[:], U8)
+        for r in range(4):
+            nc.sync.dma_start(v2_plane[r:P:32, :].bitcast(I32), v2_rows[r:16:4, :].bitcast(I32))
+
         def gather_words(a):
             pair = []
             for u in range(2):
@@ -148,7 +152,20 @@ def tile_list_mancala_kick_drift_kernel(
                 pair.append(tile)
             return pair
 
-        v_w = [gather_words(0)]
+        def round_wp(copy, grouped, a, first, slices):
+            copy(
+                grouped[:].rearrange("p (t m j) -> p m t j", t=PACK, j=PACK)[:, :, first : first + slices, :],
+                wp_raw[a][:].rearrange("p j (m t) -> p m t j", t=PACK)[:, :, first : first + slices, :],
+            )
+
+        def quantise_wp(a, grouped):
+            codes = keep.tile([P, H], U32, name="wp_codes%d" % a, align_bytes=64)
+            plane = keep.tile([P, H], U8, name="wp_plane%d" % a, align_bytes=64)
+            nc.vector.quantize_mx(out=codes[:].bitcast(FP8X4), scales=plane[:], in_=grouped[:])
+            return codes, plane
+
+        grouped = [keep.tile([P, H * PACK], BF16, name="grouped%d" % a, align_bytes=64) for a in range(PASSES)]
+        round_wp(nc.scalar.copy, grouped[0], 0, 0, PACK)
         wq_perm = keep.tile([P, PASSES, 2 * H], U8, name="wq_perm", align_bytes=64)
         nc.scalar.copy(
             wq_perm[:].bitcast(U16).rearrange("p a (t m) -> p a m t", t=PACK),
@@ -159,174 +176,138 @@ def tile_list_mancala_kick_drift_kernel(
             wq_plane[:].rearrange("p a (t m) -> p a t m", t=PACK),
             wq_plane_raw[:].rearrange("p a (m t) -> p a t m", t=PACK),
         )
-
-        def gather_v2_scales(u, rows):
-            gather(rows[:], tab2_rows[:], idx2[:, 32 * u : 32 * (u + 1)], U8)
-            for r in range(4):
-                nc.sync.dma_start(v2_plane[r:P:32, half(u)].bitcast(I32), rows[r:16:4, :].bitcast(I32))
-
+        v_w = [gather_words(0)]
+        wp_mx = [quantise_wp(0, grouped[0])]
+        round_wp(nc.scalar.copy, grouped[1], 1, 0, 2)
+        round_wp(nc.vector.tensor_copy, grouped[1], 1, 2, 2)
+        wp_mx.append(quantise_wp(1, grouped[1]))
         v_w.append(gather_words(1))
-        gather_v2_scales(0, in_turn(BANK, U8))
 
         last = PACK - 1
 
-        def q_product(t, u):
-            if t % 2 == 1:
-                q = psum.tile([P, BANK], F32, name="q", tag="bank")
-            else:
-                q = psum.tile([P, BANK], F32, name="q", tag="q_pair", bufs=2)
-            order = (0, 1) if (t, u) == (0, 0) else (1, 0)
-            for a in order:
-                nc.tensor.matmul_mx(
-                    out=q[:],
-                    lhsT=wq_perm[:, a, 2 * P * t : 2 * P * (t + 1)].bitcast(FP4X4),
-                    lhsT_scale=wq_plane[:, a, P * t : P * (t + 1)],
-                    rhs=v_w[a][u][:].bitcast(FP8X4),
-                    rhs_scale=v_planes[:, a, half(u)],
-                    start=(a == order[0]),
-                    stop=(a == order[1]),
-                )
-            return q
+        def q_pass(q, t, u, a):
+            nc.tensor.matmul_mx(
+                out=q[:],
+                lhsT=wq_perm[:, a, 2 * P * t : 2 * P * (t + 1)].bitcast(FP4X4),
+                lhsT_scale=wq_plane[:, a, P * t : P * (t + 1)],
+                rhs=v_w[a][u][:].bitcast(FP8X4),
+                rhs_scale=v_planes[:, a, half(u)],
+                start=(a == 0),
+                stop=(a == PASSES - 1),
+            )
 
-        wp_mx = {}
+        def mom_pass(mom, t, u, a):
+            nc.tensor.matmul_mx(
+                out=mom[:],
+                lhsT=wp_mx[a][0][:, P * t : P * (t + 1)].bitcast(FP8X4),
+                lhsT_scale=wp_mx[a][1][:, P * t : P * (t + 1)],
+                rhs=v_w[a][u][:].bitcast(FP8X4),
+                rhs_scale=v_planes[:, a, half(u)],
+                start=(a == 0),
+                stop=(a == PASSES - 1),
+            )
 
-        def mom_product(t, u):
-            mom = psum.tile([P, BANK], F32, name="mom", tag="bank")
-            for a in range(PASSES):
-                codes, plane = wp_mx[a, t]
-                nc.tensor.matmul_mx(
-                    out=mom[:],
-                    lhsT=codes.bitcast(FP8X4),
-                    lhsT_scale=plane,
-                    rhs=v_w[a][u][:].bitcast(FP8X4),
-                    rhs_scale=v_planes[:, a, half(u)],
-                    start=(a == 0),
-                    stop=(a == PASSES - 1),
-                )
-            return mom
+        def opened(one_pass, t, u):
+            bank = psum.tile([P, BANK], F32, name="bank")
+            one_pass(bank, t, u, 0)
+            return bank
 
-        def scaled_sine(t, q, dst, raw=None):
-            if raw is None:
-                raw = ring.tile([P, BANK], F32, name="raw_sine", align_bytes=64)
-            nc.scalar.activation(raw[:], q[:], SIN)
-            nc.scalar.activation(dst, raw[:], COPY, scale=kap_sb[:, t : t + 1])
+        def whole(one_pass, t, u):
+            bank = opened(one_pass, t, u)
+            one_pass(bank, t, u, 1)
+            return bank
 
         def emptied():
-            return ring.tile([P, BANK], F32, name="emptied", bufs=6, align_bytes=64)
+            return ring.tile([P, BANK], F32, name="emptied", bufs=9, align_bytes=64)
 
-        def drift_less_sine(t, q, ksin, dst):
-            nc.vector.scalar_tensor_tensor(dst[:], q[:], gq_sb[:, t : t + 1], ksin, MULT, SUB)
+        def sine_of(q):
+            dst = emptied()
+            nc.scalar.activation(dst[:], q[:], SIN)
             return dst
 
-        grouped = shared.tile([P, PACK, PASSES, BANK], BF16, name="grouped", offset=21 * KB, align_bytes=64)
+        def drift_term(dst, t, q):
+            nc.scalar.activation(dst, q[:], COPY, scale=gq_sb[:, t : t + 1])
 
-        def grouped_view(a, first, slices):
-            return grouped[:, first : first + slices, a, :].rearrange("p t (m j) -> p m t j", j=PACK)
-
-        def raw_view(a, first, slices):
-            return wp_raw[a][:].rearrange("p j (m t) -> p m t j", t=PACK)[:, :, first : first + slices, :]
-
-        def quantise_wp(first, slices):
-            width = P * PASSES * slices
-            codes = in_turn(width, U32)
-            plane = keep.tile([P, width], U8, name="wp_plane%d" % first, align_bytes=64)
-            values = grouped[:, first : first + slices, :, :].rearrange("p t a c -> p (t a c)")
-            nc.vector.quantize_mx(out=codes[:].bitcast(FP8X4), scales=plane[:], in_=values)
-            for i in range(slices):
-                for a in range(PASSES):
-                    cols = slice(P * (PASSES * i + a), P * (PASSES * i + a + 1))
-                    wp_mx[a, first + i] = (codes[:, cols], plane[:, cols])
-
-        def round_on_gpsimd(dst, src, factor):
-            nc.gpsimd.tensor_scalar(dst, src, factor, 0.0, MULT, ADD)
-
-        q = {(t, u): q_product(t, u) for u in range(2) for t in range(2)}
-        ksin, part = {}, {}
-        for t in range(2):
-            ksin[t, 0] = emptied()
-            scaled_sine(t, q[t, 0], ksin[t, 0][:])
-        part[0, 0] = drift_less_sine(0, q[0, 0], ksin[0, 0][:], in_turn(BANK, F32))
-        q[2, 0] = q_product(2, 0)
-
-        round_on_gpsimd(grouped_view(0, 0, PACK), raw_view(0, 0, PACK), 1.0)
-        nc.scalar.copy(grouped_view(1, 0, 1), raw_view(1, 0, 1))
-        nc.vector.tensor_copy(grouped_view(1, 1, last), raw_view(1, 1, last))
-        quantise_wp(0, 1)
-        for t in range(2):
-            ksin[t, 1] = emptied()
-            scaled_sine(t, q[t, 1], ksin[t, 1][:], in_turn(BANK, F32))
-            if t == 0:
-                part[1, 0] = drift_less_sine(1, q[1, 0], ksin[1, 0][:], in_turn(BANK, F32))
-                quantise_wp(1, 1)
-                quantise_wp(2, 2)
-        mom = {(t, u): mom_product(t, u) for t in range(2) for u in range(2)}
+        def kick(dst, t, sine, mom):
+            nc.vector.scalar_tensor_tensor(dst, sine[:], kap_sb[:, t : t + 1], mom[:], MULT, SUB)
 
         def scatter(t, cols, values):
             nc.vector.tensor_copy(page[t][:].indirect(idx3[:, cols.start // 16 : cols.stop // 16]), values)
 
-        def sum_tile(width, place):
-            return shared.tile([P, width], F32, name="sum%d_%d" % (width, place), offset=(53 + 4 * place) * KB, align_bytes=64)
+        def round_on_gpsimd(dst, src, factor):
+            nc.gpsimd.tensor_scalar(dst, src, factor, 0.0, MULT, ADD)
 
-        def late_tile(name, t, place):
-            return shared.tile([P, S], F32, name=name, offset=(21 + 12 * (t - 2) + 4 * place) * KB, align_bytes=64)
+        def placed(name, width, offset):
+            return shared.tile([P, width], F32, name=name, offset=offset * KB, align_bytes=64)
 
-        h0 = [sum_tile(BANK, 0), sum_tile(BANK, 1)]
-        nc.vector.tensor_tensor(h0[0][:], mom[0, 0][:], part[0, 0][:], ADD)
-        part[0, 1] = drift_less_sine(0, q[0, 1], ksin[0, 1][:], in_turn(BANK, F32))
-        q[2, 1] = q_product(2, 1)
-        sine2, mom2 = late_tile("sine2", 2, 0), late_tile("mom2", 2, 2)
-        mom1 = keep.tile([P, S], F32, name="mom1", align_bytes=64)
-        scaled_sine(2, q[2, 0], sine2[:, half(0)], in_turn(BANK, F32))
-        part[1, 1] = drift_less_sine(1, q[1, 1], ksin[1, 1][:], in_turn(BANK, F32))
-        nc.vector.tensor_tensor(h0[1][:], mom[0, 1][:], part[0, 1][:], ADD)
-        nc.scalar.copy(mom1[:, half(0)], mom[1, 0][:])
-        scaled_sine(2, q[2, 1], sine2[:, half(1)], in_turn(BANK, F32))
-        nc.scalar.copy(mom1[:, half(1)], mom[1, 1][:])
-
-        def chained(name, offset):
-            return shared.tile([P, BANK], F32, name=name, offset=59 * KB + offset, align_bytes=64)
-
-        new0 = [chained("new00", KB), chained("new01", 6 * KB)]
-        nc.gpsimd.tensor_tensor(new0[0][:], h0[0][:], wg[0][:, half(0)], MULT)
-        scatter(0, half(0), new0[0][:])
-        nc.gpsimd.tensor_tensor(new0[1][:], h0[1][:], wg[0][:, half(1)], MULT)
-        part2 = shared.tile([P, S], F32, name="part2", offset=61 * KB, align_bytes=64)
+        early = [(t, u) for u in range(2) for t in range(2)]
+        q = {key: opened(q_pass, *key) for key in early}
+        mom = {key: opened(mom_pass, *key) for key in early}
+        sine, state, kicked = {}, {}, {}
+        for t, u in early:
+            q_pass(q[t, u], t, u, 1)
+            mom_pass(mom[t, u], t, u, 1)
+            sine[t, u] = sine_of(q[t, u])
+            if (t, u) == (0, 1):
+                state[t, u] = emptied()
+                drift_term(state[t, u][:], t, q[t, u])
         for u in range(2):
-            drift_less_sine(2, q[2, u], sine2[:, half(u)], part2[:, half(u)])
+            state[1, u] = emptied()
+            drift_term(state[1, u][:], 1, q[1, u])
+
+        kicked[0, 0] = placed("kicked00", BANK, 21)
+        kick(kicked[0, 0][:], 0, sine[0, 0], mom[0, 0])
+        h = placed("h00", BANK, 54)
+        nc.vector.scalar_tensor_tensor(h[:], q[0, 0][:], gq_sb[:, 0:1], kicked[0, 0][:], MULT, SUB)
+        new0 = [placed("new00", BANK, 60), placed("new01", BANK, 62)]
+        nc.gpsimd.tensor_tensor(new0[0][:], h[:], wg[0][:, half(0)], MULT)
+        for t, u in ((0, 1), (1, 0), (1, 1)):
+            kicked[t, u] = placed("kicked%d%d" % (t, u), BANK, 21 + 2 * (2 * t + u))
+            kick(kicked[t, u][:], t, sine[t, u], mom[t, u])
+        scatter(0, half(0), new0[0][:])
+
+        h = placed("h01", BANK, 53)
+        nc.gpsimd.tensor_tensor(h[:], state[0, 1][:], kicked[0, 1][:], SUB)
+        nc.gpsimd.tensor_tensor(new0[1][:], h[:], wg[0][:, half(1)], MULT)
+        kicked2 = placed("kicked2", S, 57)
+        state2 = placed("state2", S, 29)
+        q2 = []
+        for u in range(2):
+            q2.append(whole(q_pass, 2, u))
+            kick(kicked2[:, half(u)], 2, sine_of(q2[u]), whole(mom_pass, 2, u))
+        for u in range(2):
+            drift_term(state2[:, half(u)], 2, q2[u])
         scatter(0, half(1), new0[1][:])
 
         new1 = keep.tile([P, S], F32, name="new1", align_bytes=64)
         for u in range(2):
-            h = sum_tile(BANK, u)
-            nc.gpsimd.tensor_tensor(h[:], mom1[:, half(u)], part[1, u][:], ADD)
+            h = placed("h1%d" % u, BANK, 55 - 2 * u)
+            nc.gpsimd.tensor_tensor(h[:], state[1, u][:], kicked[1, u][:], SUB)
             nc.gpsimd.tensor_tensor(new1[:, half(u)], h[:], wg[1][:, half(u)], MULT)
         scatter(1, slice(0, S), new1[:])
 
-        for u in range(2):
-            nc.scalar.copy(mom2[:, half(u)], mom_product(2, u)[:])
-        h = sum_tile(S, 0)
-        nc.gpsimd.tensor_tensor(h[:], part2[:], mom2[:], ADD)
+        h = placed("h2", S, 53)
+        nc.gpsimd.tensor_tensor(h[:], state2[:], kicked2[:], SUB)
         new2 = keep.tile([P, S], F32, name="new2", align_bytes=64)
         nc.gpsimd.tensor_tensor(new2[:], h[:], late_wg[:, 0, :], MULT)
         scatter(2, slice(0, S), new2[:])
 
-        sine3, state3, mom3 = (late_tile(name, last, i) for i, name in enumerate(("sine3", "state3", "mom3")))
+        sine3, state3, mom3 = placed("sine3", S, 33), placed("state3", S, 37), placed("mom3", S, 41)
         for u in range(2):
-            q3 = q_product(last, u)
-            nc.scalar.activation(state3[:, half(u)], q3[:], COPY, scale=gq_sb[:, last:PACK])
-            nc.scalar.copy(mom3[:, half(u)], mom_product(last, u)[:])
-            if u == 0:
-                raw = in_turn(BANK, F32)
-            else:
-                raw = shared.tile([P, BANK], F32, name="last_raw_sine", offset=0, align_bytes=64)
-            scaled_sine(last, q3, sine3[:, half(u)], raw)
-        h = sum_tile(S, 0)
-        nc.gpsimd.tensor_tensor(h[:], state3[:], mom3[:], ADD)
-        nc.gpsimd.tensor_tensor(h[:], h[:], sine3[:], SUB)
-        new3 = shared.tile([P, S], F32, name="new3", offset=17 * KB, align_bytes=64)
-        for u in range(2):
-            nc.gpsimd.tensor_tensor(new3[:, half(u)], h[:, half(u)], late_wg[:, 1, half(u)], MULT)
-            scatter(last, half(u), new3[:, half(u)])
+            q3 = whole(q_pass, last, u)
+            drift_term(state3[:, half(u)], last, q3)
+            nc.scalar.copy(mom3[:, half(u)], whole(mom_pass, last, u)[:])
+            raw = placed("raw_sine%d" % u, BANK, 45 if u == 0 else 0)
+            nc.scalar.activation(raw[:], q3[:], SIN)
+            nc.scalar.activation(sine3[:, half(u)], raw[:], COPY, scale=kap_sb[:, last:PACK])
+        drifted = placed("drifted3", S, 53)
+        nc.gpsimd.tensor_tensor(drifted[:], state3[:], mom3[:], ADD)
+        h = placed("h3", S, 17)
+        nc.gpsimd.tensor_tensor(h[:], drifted[:], sine3[:], SUB)
+        new3 = keep.tile([P, BANK], F32, name="new3", align_bytes=64)
+        nc.gpsimd.tensor_tensor(new3[:], h[:, half(0)], late_wg[:, 1, half(0)], MULT)
+        scatter(last, half(0), new3[:])
+        nc.vector.tensor_tensor(page[last][:].indirect(idx3[:, 32:64]), h[:, half(1)], late_wg[:, 1, half(1)], MULT)
 
         prior_sb = shared.tile([P, S // P, S], F32, name="prior_sb", offset=20 * KB + 512, align_bytes=64)
         for n in range(0, S // P, 2):
@@ -338,7 +319,7 @@ def tile_list_mancala_kick_drift_kernel(
         grouped_page = shared.tile([P, T, PACK], BF16, name="grouped_page", offset=0, align_bytes=64)
         for t in range(2):
             nc.scalar.copy(grouped_page[:, :, t], page[t][:])
-        one = sum_tile(1, 0)
+        one = placed("one", 1, 53)
         nc.gpsimd.memset(one[:], 1.0)
         for t in (2, last):
             for cols in (slice(2 * BANK, 3 * BANK), slice(SPLIT, 2 * BANK), slice(3 * BANK, T)):
@@ -361,7 +342,6 @@ def tile_list_mancala_kick_drift_kernel(
             )
             page_codes[c] = codes
             page_planes[c] = plane
-        gather_v2_scales(1, shared.tile([P, BANK], U8, name="v2_rows_b", offset=0, align_bytes=64))
 
         tiles = S // P
         for n in range(tiles):
@@ -377,7 +357,10 @@ def tile_list_mancala_kick_drift_kernel(
                     start=True,
                     stop=True,
                 )
-                nc.scalar.copy(scores[:, half(c)], e[:])
+                if n == 0 and c == chunk_order[-1]:
+                    nc.vector.tensor_copy(scores[:, half(c)], e[:])
+                else:
+                    nc.scalar.copy(scores[:, half(c)], e[:])
             picked = keep.tile([P, S], F32, name="picked", tag=("wg0", "wg1", "late_wg")[n % 3])
             widths = LAST_WIDTHS if n == tiles - 1 else (S,)
             first = 0

@@ -70,12 +70,12 @@ def tile_list_mancala_kick_drift_kernel(
             nc.sync.dma_start(tile[:], page0.rearrange("(p t) c -> t p c", t=PACK)[t])
             return tile
 
-        def load_wg(t):
-            tile = keep.tile([P, S], F32, name="wg%d" % t)
+        def load_wg(first, width, name):
+            tile = keep.tile([P, width], F32, name=name, align_bytes=64)
             for quad in (0, 2, 1, 3):
                 nc.sync.dma_start(
                     tile[32 * quad : 32 * quad + 32, :],
-                    wgs.rearrange("(p t) j -> t p j", t=PACK)[t],
+                    wgs.rearrange("(p t) j -> p (t j)", t=PACK)[:, first : first + width],
                 )
             return tile
 
@@ -123,12 +123,12 @@ def tile_list_mancala_kick_drift_kernel(
         tab_w.append(load_words(tab_words[1], "tab_w1"))
         kap_sb = load_column(kap, "kap_sb")
         gq_sb = load_column(gq, "gq_sb")
-        wg = [load_wg(0)]
+        first_wg = load_wg(0, BANK, "first_wg")
         idx3 = load_list(offs3, "idx3")
         page = [load_page(0)]
-        wg.append(load_wg(1))
+        next_wg = load_wg(BANK, 3 * BANK, "next_wg")
         page.append(load_page(1))
-        late_wg = keep.tile([P, 2, S], F32, name="late_wg")
+        late_wg = keep.tile([P, 2, S], F32, name="late_wg", align_bytes=64)
         for quad in (0, 2, 1, 3):
             nc.sync.dma_start(
                 late_wg[32 * quad : 32 * quad + 32, :, :],
@@ -260,7 +260,7 @@ def tile_list_mancala_kick_drift_kernel(
         h = placed("h00", BANK, 54)
         nc.vector.scalar_tensor_tensor(h[:], q[0, 0][:], gq_sb[:, 0:1], kicked[0, 0][:], MULT, SUB)
         new0 = [placed("new00", BANK, 60), placed("new01", BANK, 62)]
-        nc.gpsimd.tensor_tensor(new0[0][:], h[:], wg[0][:, half(0)], MULT)
+        nc.gpsimd.tensor_tensor(new0[0][:], h[:], first_wg[:], MULT)
         for t, u in ((0, 1), (1, 0), (1, 1)):
             kicked[t, u] = placed("kicked%d%d" % (t, u), BANK, 21 + 2 * (2 * t + u))
             kick(kicked[t, u][:], t, sine[t, u], mom[t, u])
@@ -268,7 +268,7 @@ def tile_list_mancala_kick_drift_kernel(
 
         h = placed("h01", BANK, 53)
         nc.gpsimd.tensor_tensor(h[:], state[0, 1][:], kicked[0, 1][:], SUB)
-        nc.gpsimd.tensor_tensor(new0[1][:], h[:], wg[0][:, half(1)], MULT)
+        nc.gpsimd.tensor_tensor(new0[1][:], h[:], next_wg[:, half(0)], MULT)
         kicked2 = placed("kicked2", S, 57)
         state2 = placed("state2", S, 29)
         q2 = []
@@ -283,7 +283,7 @@ def tile_list_mancala_kick_drift_kernel(
         for u in range(2):
             h = placed("h1%d" % u, BANK, 55 - 2 * u)
             nc.gpsimd.tensor_tensor(h[:], state[1, u][:], kicked[1, u][:], SUB)
-            nc.gpsimd.tensor_tensor(new1[:, half(u)], h[:], wg[1][:, half(u)], MULT)
+            nc.gpsimd.tensor_tensor(new1[:, half(u)], h[:], next_wg[:, half(u + 1)], MULT)
         scatter(1, slice(0, S), new1[:])
 
         h = placed("h2", S, 53)
@@ -361,7 +361,7 @@ def tile_list_mancala_kick_drift_kernel(
                     nc.vector.tensor_copy(scores[:, half(c)], e[:])
                 else:
                     nc.scalar.copy(scores[:, half(c)], e[:])
-            picked = keep.tile([P, S], F32, name="picked", tag=("wg0", "wg1", "late_wg")[n % 3])
+            picked = keep.tile([P, S], F32, name="picked", tag=("new1", "next_wg", "late_wg")[n % 3], align_bytes=64)
             widths = LAST_WIDTHS if n == tiles - 1 else (S,)
             first = 0
             for width in widths:

@@ -218,7 +218,7 @@ def tile_list_mancala_kick_drift_kernel(
             return bank
 
         def emptied():
-            return ring.tile([P, BANK], F32, name="emptied", bufs=9, align_bytes=64)
+            return ring.tile([P, BANK], F32, name="emptied", bufs=7, align_bytes=64)
 
         def sine_of(q):
             dst = emptied()
@@ -251,9 +251,9 @@ def tile_list_mancala_kick_drift_kernel(
             if (t, u) == (0, 1):
                 state[t, u] = emptied()
                 drift_term(state[t, u][:], t, q[t, u])
+        state1 = placed("state1", S, 47)
         for u in range(2):
-            state[1, u] = emptied()
-            drift_term(state[1, u][:], 1, q[1, u])
+            drift_term(state1[:, half(u)], 1, q[1, u])
 
         kicked[0, 0] = placed("kicked00", BANK, 21)
         kick(kicked[0, 0][:], 0, sine[0, 0], mom[0, 0])
@@ -261,9 +261,11 @@ def tile_list_mancala_kick_drift_kernel(
         nc.vector.scalar_tensor_tensor(h[:], q[0, 0][:], gq_sb[:, 0:1], kicked[0, 0][:], MULT, SUB)
         new0 = [placed("new00", BANK, 60), placed("new01", BANK, 62)]
         nc.gpsimd.tensor_tensor(new0[0][:], h[:], first_wg[:], MULT)
-        for t, u in ((0, 1), (1, 0), (1, 1)):
-            kicked[t, u] = placed("kicked%d%d" % (t, u), BANK, 21 + 2 * (2 * t + u))
-            kick(kicked[t, u][:], t, sine[t, u], mom[t, u])
+        kicked[0, 1] = placed("kicked01", BANK, 23)
+        kick(kicked[0, 1][:], 0, sine[0, 1], mom[0, 1])
+        kicked1 = placed("kicked1", S, 25)
+        for u in range(2):
+            kick(kicked1[:, half(u)], 1, sine[1, u], mom[1, u])
         scatter(0, half(0), new0[0][:])
 
         h = placed("h01", BANK, 53)
@@ -280,10 +282,9 @@ def tile_list_mancala_kick_drift_kernel(
         scatter(0, half(1), new0[1][:])
 
         new1 = keep.tile([P, S], F32, name="new1", align_bytes=64)
-        for u in range(2):
-            h = placed("h1%d" % u, BANK, 55 - 2 * u)
-            nc.gpsimd.tensor_tensor(h[:], state[1, u][:], kicked[1, u][:], SUB)
-            nc.gpsimd.tensor_tensor(new1[:, half(u)], h[:], next_wg[:, half(u + 1)], MULT)
+        h = placed("h1", S, 53)
+        nc.gpsimd.tensor_tensor(h[:], state1[:], kicked1[:], SUB)
+        nc.gpsimd.tensor_tensor(new1[:], h[:], next_wg[:, BANK:], MULT)
         scatter(1, slice(0, S), new1[:])
 
         h = placed("h2", S, 53)
@@ -300,14 +301,13 @@ def tile_list_mancala_kick_drift_kernel(
             raw = placed("raw_sine%d" % u, BANK, 45 if u == 0 else 0)
             nc.scalar.activation(raw[:], q3[:], SIN)
             nc.scalar.activation(sine3[:, half(u)], raw[:], COPY, scale=kap_sb[:, last:PACK])
-        drifted = placed("drifted3", S, 53)
-        nc.gpsimd.tensor_tensor(drifted[:], state3[:], mom3[:], ADD)
-        h = placed("h3", S, 17)
-        nc.gpsimd.tensor_tensor(h[:], drifted[:], sine3[:], SUB)
-        new3 = keep.tile([P, BANK], F32, name="new3", align_bytes=64)
-        nc.gpsimd.tensor_tensor(new3[:], h[:, half(0)], late_wg[:, 1, half(0)], MULT)
-        scatter(last, half(0), new3[:])
-        nc.vector.tensor_tensor(page[last][:].indirect(idx3[:, 32:64]), h[:, half(1)], late_wg[:, 1, half(1)], MULT)
+        h = placed("h3", S, 53)
+        nc.gpsimd.tensor_tensor(h[:], state3[:], mom3[:], ADD)
+        nc.gpsimd.tensor_tensor(h[:], h[:], sine3[:], SUB)
+        new3 = placed("new3", S, 17)
+        for u in range(2):
+            nc.gpsimd.tensor_tensor(new3[:, half(u)], h[:, half(u)], late_wg[:, 1, half(u)], MULT)
+            scatter(last, half(u), new3[:, half(u)])
 
         prior_sb = shared.tile([P, S // P, S], F32, name="prior_sb", offset=20 * KB + 512, align_bytes=64)
         for n in range(0, S // P, 2):
@@ -357,7 +357,7 @@ def tile_list_mancala_kick_drift_kernel(
                     start=True,
                     stop=True,
                 )
-                if n == 0 and c == chunk_order[-1]:
+                if n == 0 and c in chunk_order[2:]:
                     nc.vector.tensor_copy(scores[:, half(c)], e[:])
                 else:
                     nc.scalar.copy(scores[:, half(c)], e[:])

@@ -123,12 +123,20 @@ def tile_list_mancala_kick_drift_kernel(
         tab_w.append(load_words(tab_words[1], "tab_w1"))
         kap_sb = load_column(kap, "kap_sb")
         gq_sb = load_column(gq, "gq_sb")
+        v2_rows = keep.tile([P, S], U8, name="v2_rows", align_bytes=64)
+        gather(v2_rows[:], tab2_rows[:], idx2[:], U8)
+
+        def move_v2_rows(r):
+            nc.sync.dma_start(v2_plane[r:P:32, :].bitcast(I32), v2_rows[r:16:4, :].bitcast(I32))
+
         first_wg = load_wg(0, BANK, "first_wg")
         idx3 = load_list(offs3, "idx3")
         page = [load_page(0)]
         next_wg = load_wg(BANK, 3 * BANK, "next_wg")
         page.append(load_page(1))
-        late_wg = keep.tile([P, 2, S], F32, name="late_wg", align_bytes=64)
+        idx4 = load_list(offs4, "idx4")
+        move_v2_rows(0)
+        late_wg = ring.tile([P, 2, S], F32, name="late_pair", align_bytes=64)
         for quad in (0, 2, 1, 3):
             nc.sync.dma_start(
                 late_wg[32 * quad : 32 * quad + 32, :, :],
@@ -137,12 +145,8 @@ def tile_list_mancala_kick_drift_kernel(
         page.append(load_page(2))
         tab2_w = load_words(tab2_words[0], "tab2_w")
         page.append(load_page(3))
-        idx4 = load_list(offs4, "idx4")
-
-        v2_rows = keep.tile([P, S], U8, name="v2_rows", align_bytes=64)
-        gather(v2_rows[:], tab2_rows[:], idx2[:], U8)
-        for r in range(4):
-            nc.sync.dma_start(v2_plane[r:P:32, :].bitcast(I32), v2_rows[r:16:4, :].bitcast(I32))
+        for r in range(1, 4):
+            move_v2_rows(r)
 
         def gather_words(a):
             pair = []
@@ -259,7 +263,7 @@ def tile_list_mancala_kick_drift_kernel(
         kick(kicked[0, 0][:], 0, sine[0, 0], mom[0, 0])
         h = placed("h00", BANK, 54)
         nc.vector.scalar_tensor_tensor(h[:], q[0, 0][:], gq_sb[:, 0:1], kicked[0, 0][:], MULT, SUB)
-        new0 = [placed("new00", BANK, 60), placed("new01", BANK, 62)]
+        new0 = [placed("new00", BANK, 57), placed("new01", BANK, 59)]
         nc.gpsimd.tensor_tensor(new0[0][:], h[:], first_wg[:], MULT)
         kicked[0, 1] = placed("kicked01", BANK, 23)
         kick(kicked[0, 1][:], 0, sine[0, 1], mom[0, 1])
@@ -271,7 +275,7 @@ def tile_list_mancala_kick_drift_kernel(
         h = placed("h01", BANK, 53)
         nc.gpsimd.tensor_tensor(h[:], state[0, 1][:], kicked[0, 1][:], SUB)
         nc.gpsimd.tensor_tensor(new0[1][:], h[:], next_wg[:, half(0)], MULT)
-        kicked2 = placed("kicked2", S, 57)
+        kicked2 = ring.tile([P, S], F32, name="late_pair", align_bytes=64)
         state2 = placed("state2", S, 29)
         q2 = []
         for u in range(2):
@@ -305,9 +309,8 @@ def tile_list_mancala_kick_drift_kernel(
         nc.gpsimd.tensor_tensor(h[:], state3[:], mom3[:], ADD)
         nc.gpsimd.tensor_tensor(h[:], h[:], sine3[:], SUB)
         new3 = placed("new3", S, 17)
-        for u in range(2):
-            nc.gpsimd.tensor_tensor(new3[:, half(u)], h[:, half(u)], late_wg[:, 1, half(u)], MULT)
-            scatter(last, half(u), new3[:, half(u)])
+        nc.gpsimd.tensor_tensor(new3[:], h[:], late_wg[:, 1, :], MULT)
+        scatter(last, slice(0, S), new3[:])
 
         prior_sb = shared.tile([P, S // P, S], F32, name="prior_sb", offset=20 * KB + 512, align_bytes=64)
         for n in range(0, S // P, 2):
@@ -361,7 +364,7 @@ def tile_list_mancala_kick_drift_kernel(
                     nc.vector.tensor_copy(scores[:, half(c)], e[:])
                 else:
                     nc.scalar.copy(scores[:, half(c)], e[:])
-            picked = keep.tile([P, S], F32, name="picked", tag=("new1", "next_wg", "late_wg")[n % 3], align_bytes=64)
+            picked = keep.tile([P, S], F32, name="picked", tag=("new1", "next_wg", "new2")[n % 3], align_bytes=64)
             widths = LAST_WIDTHS if n == tiles - 1 else (S,)
             first = 0
             for width in widths:

@@ -70,8 +70,10 @@ def tile_list_mancala_kick_drift_kernel(
             nc.sync.dma_start(tile[:], page0.rearrange("(p t) c -> t p c", t=PACK)[t])
             return tile
 
-        def load_wg(first, width, name):
-            tile = keep.tile([P, width], F32, name=name, align_bytes=64)
+        def placed(name, width, offset):
+            return shared.tile([P, width], F32, name=name, offset=offset * KB, align_bytes=64)
+
+        def load_wg(tile, first, width):
             for quad in (0, 2, 1, 3):
                 nc.sync.dma_start(
                     tile[32 * quad : 32 * quad + 32, :],
@@ -129,14 +131,14 @@ def tile_list_mancala_kick_drift_kernel(
         def move_v2_rows(r):
             nc.sync.dma_start(v2_plane[r:P:32, :].bitcast(I32), v2_rows[r:16:4, :].bitcast(I32))
 
-        first_wg = load_wg(0, BANK, "first_wg")
+        first_wg = load_wg(placed("first_wg", BANK, 53), 0, BANK)
         idx3 = load_list(offs3, "idx3")
         page = [load_page(0)]
-        next_wg = load_wg(BANK, 3 * BANK, "next_wg")
+        next_wg = load_wg(keep.tile([P, 3 * BANK], F32, name="next_wg", align_bytes=64), BANK, 3 * BANK)
         page.append(load_page(1))
         idx4 = load_list(offs4, "idx4")
         move_v2_rows(0)
-        late_wg = ring.tile([P, 2, S], F32, name="late_pair", align_bytes=64)
+        late_wg = ring.tile([P, 2, S], F32, name="late_turn", bufs=4, align_bytes=64)
         for quad in (0, 2, 1, 3):
             nc.sync.dma_start(
                 late_wg[32 * quad : 32 * quad + 32, :, :],
@@ -168,7 +170,10 @@ def tile_list_mancala_kick_drift_kernel(
             nc.vector.quantize_mx(out=codes[:].bitcast(FP8X4), scales=plane[:], in_=grouped[:])
             return codes, plane
 
-        grouped = [keep.tile([P, H * PACK], BF16, name="grouped%d" % a, align_bytes=64) for a in range(PASSES)]
+        grouped = [
+            shared.tile([P, H * PACK], BF16, name="grouped%d" % a, offset=(8 + 4 * a) * KB, align_bytes=64)
+            for a in range(PASSES)
+        ]
         round_wp(nc.scalar.copy, grouped[0], 0, 0, PACK)
         wq_perm = keep.tile([P, PASSES, 2 * H], U8, name="wq_perm", align_bytes=64)
         nc.scalar.copy(
@@ -222,7 +227,7 @@ def tile_list_mancala_kick_drift_kernel(
             return bank
 
         def emptied():
-            return ring.tile([P, BANK], F32, name="emptied", bufs=7, align_bytes=64)
+            return ring.tile([P, BANK], F32, name="emptied", bufs=5, align_bytes=64)
 
         def sine_of(q):
             dst = emptied()
@@ -241,8 +246,8 @@ def tile_list_mancala_kick_drift_kernel(
         def round_on_gpsimd(dst, src, factor):
             nc.gpsimd.tensor_scalar(dst, src, factor, 0.0, MULT, ADD)
 
-        def placed(name, width, offset):
-            return shared.tile([P, width], F32, name=name, offset=offset * KB, align_bytes=64)
+        def in_turn(width):
+            return ring.tile([P, width], F32, name="in_turn", bufs=3, align_bytes=64)
 
         early = [(t, u) for u in range(2) for t in range(2)]
         q = {key: opened(q_pass, *key) for key in early}
@@ -261,21 +266,20 @@ def tile_list_mancala_kick_drift_kernel(
 
         kicked[0, 0] = placed("kicked00", BANK, 21)
         kick(kicked[0, 0][:], 0, sine[0, 0], mom[0, 0])
-        h = placed("h00", BANK, 54)
+        h = in_turn(BANK)
         nc.vector.scalar_tensor_tensor(h[:], q[0, 0][:], gq_sb[:, 0:1], kicked[0, 0][:], MULT, SUB)
-        new0 = [placed("new00", BANK, 57), placed("new01", BANK, 59)]
-        nc.gpsimd.tensor_tensor(new0[0][:], h[:], first_wg[:], MULT)
-        kicked[0, 1] = placed("kicked01", BANK, 23)
+        new0 = placed("new00", BANK, 55)
+        nc.gpsimd.tensor_tensor(new0[:], h[:], first_wg[:], MULT)
+        kicked1 = in_turn(S)
+        kick(kicked1[:, half(0)], 1, sine[1, 0], mom[1, 0])
+        kicked[0, 1] = in_turn(BANK)
         kick(kicked[0, 1][:], 0, sine[0, 1], mom[0, 1])
-        kicked1 = placed("kicked1", S, 25)
-        for u in range(2):
-            kick(kicked1[:, half(u)], 1, sine[1, u], mom[1, u])
-        scatter(0, half(0), new0[0][:])
+        kick(kicked1[:, half(1)], 1, sine[1, 1], mom[1, 1])
+        scatter(0, half(0), new0[:])
 
         h = placed("h01", BANK, 53)
         nc.gpsimd.tensor_tensor(h[:], state[0, 1][:], kicked[0, 1][:], SUB)
-        nc.gpsimd.tensor_tensor(new0[1][:], h[:], next_wg[:, half(0)], MULT)
-        kicked2 = ring.tile([P, S], F32, name="late_pair", align_bytes=64)
+        kicked2 = ring.tile([P, S], F32, name="late_turn", bufs=4, align_bytes=64)
         state2 = placed("state2", S, 29)
         q2 = []
         for u in range(2):
@@ -283,21 +287,26 @@ def tile_list_mancala_kick_drift_kernel(
             kick(kicked2[:, half(u)], 2, sine_of(q2[u]), whole(mom_pass, 2, u))
         for u in range(2):
             drift_term(state2[:, half(u)], 2, q2[u])
-        scatter(0, half(1), new0[1][:])
+        new0 = ring.tile([P, BANK], F32, name="late_turn", bufs=4, align_bytes=64)
+        nc.gpsimd.tensor_tensor(new0[:], h[:], next_wg[:, half(0)], MULT)
+        scatter(0, half(1), new0[:])
 
-        new1 = keep.tile([P, S], F32, name="new1", align_bytes=64)
-        h = placed("h1", S, 53)
+        def wide():
+            return ring.tile([P, S], F32, name="wide", bufs=4, align_bytes=64)
+
+        h = ring.tile([P, S], F32, name="late_turn", bufs=4, align_bytes=64)
         nc.gpsimd.tensor_tensor(h[:], state1[:], kicked1[:], SUB)
+        new1 = wide()
         nc.gpsimd.tensor_tensor(new1[:], h[:], next_wg[:, BANK:], MULT)
         scatter(1, slice(0, S), new1[:])
 
-        h = placed("h2", S, 53)
+        h = wide()
         nc.gpsimd.tensor_tensor(h[:], state2[:], kicked2[:], SUB)
-        new2 = keep.tile([P, S], F32, name="new2", align_bytes=64)
+        new2 = wide()
         nc.gpsimd.tensor_tensor(new2[:], h[:], late_wg[:, 0, :], MULT)
         scatter(2, slice(0, S), new2[:])
 
-        sine3, state3, mom3 = placed("sine3", S, 33), placed("state3", S, 37), placed("mom3", S, 41)
+        sine3, state3, mom3 = placed("sine3", S, 53), placed("state3", S, 37), placed("mom3", S, 41)
         for u in range(2):
             q3 = whole(q_pass, last, u)
             drift_term(state3[:, half(u)], last, q3)
@@ -305,7 +314,7 @@ def tile_list_mancala_kick_drift_kernel(
             raw = placed("raw_sine%d" % u, BANK, 45 if u == 0 else 0)
             nc.scalar.activation(raw[:], q3[:], SIN)
             nc.scalar.activation(sine3[:, half(u)], raw[:], COPY, scale=kap_sb[:, last:PACK])
-        h = placed("h3", S, 53)
+        h = wide()
         nc.gpsimd.tensor_tensor(h[:], state3[:], mom3[:], ADD)
         nc.gpsimd.tensor_tensor(h[:], h[:], sine3[:], SUB)
         new3 = placed("new3", S, 17)
@@ -364,7 +373,7 @@ def tile_list_mancala_kick_drift_kernel(
                     nc.vector.tensor_copy(scores[:, half(c)], e[:])
                 else:
                     nc.scalar.copy(scores[:, half(c)], e[:])
-            picked = keep.tile([P, S], F32, name="picked", tag=("new1", "next_wg", "new2")[n % 3], align_bytes=64)
+            picked = wide()
             widths = LAST_WIDTHS if n == tiles - 1 else (S,)
             first = 0
             for width in widths:

@@ -24,7 +24,7 @@ PACK = 4
 BANK = 512
 PASSES = K // (P * PACK)
 QUADS = 4
-SPLIT = 768
+SPLIT = 640
 LAST_WIDTHS = (512, 384, 128)
 KB = 1024
 
@@ -333,11 +333,14 @@ def tile_list_mancala_kick_drift_kernel(
             nc.scalar.copy(grouped_page[:, :, t], page[t][:])
         one = placed("one", 1, 53)
         nc.gpsimd.memset(one[:], 1.0)
-        for t in (2, last):
-            for cols in (slice(2 * BANK, 3 * BANK), slice(SPLIT, 2 * BANK), slice(3 * BANK, T)):
-                nc.scalar.copy(grouped_page[:, cols, t], page[t][:, cols])
-            for cols in (slice(0, BANK), slice(BANK, SPLIT)):
-                round_on_gpsimd(grouped_page[:, cols, t], page[t][:, cols], one[:])
+        for cols in (slice(2 * BANK, 3 * BANK), slice(SPLIT, 2 * BANK), slice(3 * BANK, T)):
+            nc.scalar.copy(grouped_page[:, cols, 2], page[2][:, cols])
+        round_on_gpsimd(grouped_page[:, 0:SPLIT, 2], page[2][:, 0:SPLIT], one[:])
+        after = placed("after", 1, 53)
+        nc.gpsimd.memset(after[:], 1.0)
+        for cols in (slice(2 * BANK, 3 * BANK), slice(SPLIT, 2 * BANK), slice(3 * BANK, T)):
+            nc.scalar.copy(grouped_page[:, cols, last], page[last][:, cols])
+        nc.vector.tensor_scalar(grouped_page[:, 0:SPLIT, last], page[last][:, 0:SPLIT], after[:], None, MULT)
 
         v2_words = shared.tile([P, S], U32, name="v2_words", offset=16 * KB, align_bytes=64)
         for u in range(2):

@@ -24,7 +24,7 @@ PACK = 4
 BANK = 512
 PASSES = K // (P * PACK)
 QUADS = 4
-SPLIT = 640
+SPLIT = 768
 LAST_WIDTHS = (512, 384, 128)
 KB = 1024
 
@@ -342,14 +342,13 @@ def tile_list_mancala_kick_drift_kernel(
             nc.scalar.copy(grouped_page[:, cols, last], page[last][:, cols])
         nc.vector.tensor_scalar(grouped_page[:, 0:SPLIT, last], page[last][:, 0:SPLIT], after[:], None, MULT)
 
-        v2_words = shared.tile([P, S], U32, name="v2_words", offset=16 * KB, align_bytes=64)
-        for u in range(2):
-            gather(v2_words[:, half(u)], tab2_w[:], idx2[:, 32 * u : 32 * (u + 1)], U32)
+        v2_words = [shared.tile([P, BANK], U32, name="v2_words", offset=17 * KB, align_bytes=64)]
+        gather(v2_words[0][:], tab2_w[:], idx2[:, 0:32], U32)
         chunk_order = [2, 0, 1, 3]
         page_codes, page_planes = {}, {}
         for c in chunk_order:
             codes = keep.tile([P, BANK], U32, name="page_codes", tag="v_w%d%d" % (c // 2, c % 2), align_bytes=64)
-            plane = keep.tile([P, BANK], U8, name="page_plane%d" % c, align_bytes=64)
+            plane = ring.tile([P, BANK], U8, name="page_plane", tag="emptied", bufs=5, align_bytes=64)
             nc.vector.quantize_mx(
                 out=codes[:].bitcast(FP8X4),
                 scales=plane[:],
@@ -357,6 +356,8 @@ def tile_list_mancala_kick_drift_kernel(
             )
             page_codes[c] = codes
             page_planes[c] = plane
+        v2_words.append(ring.tile([P, BANK], U32, name="v2_words_late", tag="emptied", bufs=5, align_bytes=64))
+        gather(v2_words[1][:], tab2_w[:], idx2[:, 32:64], U32)
 
         tiles = S // P
         for n in range(tiles):
@@ -365,17 +366,14 @@ def tile_list_mancala_kick_drift_kernel(
                 e = psum.tile([P, BANK], F32, name="e", tag="bank")
                 nc.tensor.matmul_mx(
                     out=e[:],
-                    lhsT=v2_words[:, n * P : (n + 1) * P].bitcast(FP8X4),
+                    lhsT=v2_words[n // 4][:, n % 4 * P : (n % 4 + 1) * P].bitcast(FP8X4),
                     lhsT_scale=v2_plane[:, n * P : (n + 1) * P],
                     rhs=page_codes[c][:].bitcast(FP8X4),
                     rhs_scale=page_planes[c][:],
                     start=True,
                     stop=True,
                 )
-                if n == 0 and c in chunk_order[2:]:
-                    nc.vector.tensor_copy(scores[:, half(c)], e[:])
-                else:
-                    nc.scalar.copy(scores[:, half(c)], e[:])
+                nc.scalar.copy(scores[:, half(c)], e[:])
             picked = wide()
             widths = LAST_WIDTHS if n == tiles - 1 else (S,)
             first = 0

@@ -105,8 +105,8 @@ def tile_list_mancala_kick_drift_kernel(
         nc.gpsimd.memset(tab_rows[64:P, :].bitcast(I32), 0)
         idx2 = load_list(offs2, "idx2")
         nc.sync.dma_start(tab2_rows[0:16, :].bitcast(I32), tab2_scales[0].bitcast(I32))
-        nc.gpsimd.memset(tab2_rows[32:64, :].bitcast(I32), 0)
-        nc.gpsimd.memset(tab2_rows[64:P, :].bitcast(I32), 0)
+        nc.vector.memset(tab2_rows[32:64, :].bitcast(I32), 0)
+        nc.vector.memset(tab2_rows[64:P, :].bitcast(I32), 0)
         wp_raw = [load_wp(0)]
         wq_raw = keep.tile([P, PASSES, 2 * H], U8, name="wq_raw", align_bytes=64)
         nc.sync.dma_start(wq_raw[:].bitcast(I32), wq_words.rearrange("a p c -> p a c").bitcast(I32))
@@ -153,7 +153,7 @@ def tile_list_mancala_kick_drift_kernel(
         def gather_words(a):
             pair = []
             for u in range(2):
-                tile = keep.tile([P, BANK], U32, name="v_w%d%d" % (a, u), align_bytes=64)
+                tile = keep.tile([P, BANK], U32, name="v_w%d%d" % (a, u), bufs=1 + a * u, align_bytes=64)
                 gather(tile[:], tab_w[a][:], idx[:, 32 * u : 32 * (u + 1)], U32)
                 pair.append(tile)
             return pair
@@ -164,11 +164,13 @@ def tile_list_mancala_kick_drift_kernel(
                 wp_raw[a][:].rearrange("p j (m t) -> p m t j", t=PACK)[:, :, first : first + slices, :],
             )
 
-        def quantise_wp(a, grouped):
-            codes = keep.tile([P, H], U32, name="wp_codes%d" % a, align_bytes=64)
-            plane = keep.tile([P, H], U8, name="wp_plane%d" % a, align_bytes=64)
-            nc.vector.quantize_mx(out=codes[:].bitcast(FP8X4), scales=plane[:], in_=grouped[:])
-            return codes, plane
+        def quantise_wp(a, first, slices, tag, bufs):
+            codes = keep.tile([P, P * slices], U32, name="wp_codes", tag=tag, bufs=bufs, align_bytes=64)
+            plane = keep.tile([P, P * slices], U8, name="wp_plane%d%d" % (a, first), align_bytes=64)
+            source = grouped[a][:, BANK * first : BANK * (first + slices)]
+            nc.vector.quantize_mx(out=codes[:].bitcast(FP8X4), scales=plane[:], in_=source)
+            for t in range(slices):
+                wp_mx[a, first + t] = codes[:, P * t : P * (t + 1)], plane[:, P * t : P * (t + 1)]
 
         grouped = [
             shared.tile([P, H * PACK], BF16, name="grouped%d" % a, offset=(8 + 4 * a) * KB, align_bytes=64)
@@ -186,11 +188,13 @@ def tile_list_mancala_kick_drift_kernel(
             wq_plane_raw[:].rearrange("p a (m t) -> p a t m", t=PACK),
         )
         v_w = [gather_words(0)]
-        wp_mx = [quantise_wp(0, grouped[0])]
+        wp_mx = {}
+        quantise_wp(0, 0, PACK, "wp_codes0", 1)
         round_wp(nc.scalar.copy, grouped[1], 1, 0, 2)
-        round_wp(nc.vector.tensor_copy, grouped[1], 1, 2, 2)
-        wp_mx.append(quantise_wp(1, grouped[1]))
+        round_wp(nc.scalar.copy, grouped[1], 1, 2, 2)
+        quantise_wp(1, 0, 2, "wp_codes1", 1)
         v_w.append(gather_words(1))
+        quantise_wp(1, 2, 2, "v_w11", 2)
 
         last = PACK - 1
 
@@ -208,8 +212,8 @@ def tile_list_mancala_kick_drift_kernel(
         def mom_pass(mom, t, u, a):
             nc.tensor.matmul_mx(
                 out=mom[:],
-                lhsT=wp_mx[a][0][:, P * t : P * (t + 1)].bitcast(FP8X4),
-                lhsT_scale=wp_mx[a][1][:, P * t : P * (t + 1)],
+                lhsT=wp_mx[a, t][0].bitcast(FP8X4),
+                lhsT_scale=wp_mx[a, t][1],
                 rhs=v_w[a][u][:].bitcast(FP8X4),
                 rhs_scale=v_planes[:, a, half(u)],
                 start=(a == 0),
@@ -347,7 +351,7 @@ def tile_list_mancala_kick_drift_kernel(
         chunk_order = [2, 0, 1, 3]
         page_codes, page_planes = {}, {}
         for c in chunk_order:
-            codes = keep.tile([P, BANK], U32, name="page_codes", tag="v_w%d%d" % (c // 2, c % 2), align_bytes=64)
+            codes = keep.tile([P, BANK], U32, name="page_codes", tag="v_w%d%d" % (c // 2, c % 2), bufs=1 + c // 3, align_bytes=64)
             plane = ring.tile([P, BANK], U8, name="page_plane", tag="emptied", bufs=5, align_bytes=64)
             nc.vector.quantize_mx(
                 out=codes[:].bitcast(FP8X4),

@@ -24,7 +24,8 @@ PACK = 4
 BANK = 512
 PASSES = K // (P * PACK)
 QUADS = 4
-SPLIT = 768
+SPLIT = 896
+FIRST_ROWS = 256
 LAST_WIDTHS = (512, 384, 128)
 KB = 1024
 
@@ -346,13 +347,16 @@ def tile_list_mancala_kick_drift_kernel(
             nc.scalar.copy(grouped_page[:, cols, last], page[last][:, cols])
         nc.vector.tensor_scalar(grouped_page[:, 0:SPLIT, last], page[last][:, 0:SPLIT], after[:], None, MULT)
 
-        v2_words = [shared.tile([P, BANK], U32, name="v2_words", offset=17 * KB, align_bytes=64)]
-        gather(v2_words[0][:], tab2_w[:], idx2[:, 0:32], U32)
+        v2_words = [shared.tile([P, FIRST_ROWS], U32, name="v2_words", offset=17 * KB, align_bytes=64)]
+        gather(v2_words[0][:], tab2_w[:], idx2[:, 0 : FIRST_ROWS // 16], U32)
         chunk_order = [2, 0, 1, 3]
         page_codes, page_planes = {}, {}
         for c in chunk_order:
             codes = keep.tile([P, BANK], U32, name="page_codes", tag="v_w%d%d" % (c // 2, c % 2), bufs=1 + c // 3, align_bytes=64)
-            plane = ring.tile([P, BANK], U8, name="page_plane", tag="emptied", bufs=5, align_bytes=64)
+            if c == chunk_order[-1]:
+                plane = ring.tile([P, BANK], U8, name="page_plane", tag="in_turn", bufs=3, align_bytes=64)
+            else:
+                plane = ring.tile([P, BANK], U8, name="page_plane", tag="emptied", bufs=5, align_bytes=64)
             nc.vector.quantize_mx(
                 out=codes[:].bitcast(FP8X4),
                 scales=plane[:],
@@ -360,17 +364,19 @@ def tile_list_mancala_kick_drift_kernel(
             )
             page_codes[c] = codes
             page_planes[c] = plane
-        v2_words.append(ring.tile([P, BANK], U32, name="v2_words_late", tag="emptied", bufs=5, align_bytes=64))
-        gather(v2_words[1][:], tab2_w[:], idx2[:, 32:64], U32)
+        v2_words.append(ring.tile([P, S - FIRST_ROWS], U32, name="v2_words_late", tag="in_turn", bufs=3, align_bytes=64))
+        gather(v2_words[1][:], tab2_w[:], idx2[:, FIRST_ROWS // 16 :], U32)
 
         tiles = S // P
         for n in range(tiles):
             scores = keep.tile([P, T], F32, name="scores", tag=("wp_raw0", "wp_raw1", "tab_w1")[n % 3], align_bytes=64)
+            start = n * P
+            rows = v2_words[0][:, start : start + P] if start < FIRST_ROWS else v2_words[1][:, start - FIRST_ROWS : start - FIRST_ROWS + P]
             for c in chunk_order:
                 e = psum.tile([P, BANK], F32, name="e", tag="bank")
                 nc.tensor.matmul_mx(
                     out=e[:],
-                    lhsT=v2_words[n // 4][:, n % 4 * P : (n % 4 + 1) * P].bitcast(FP8X4),
+                    lhsT=rows.bitcast(FP8X4),
                     lhsT_scale=v2_plane[:, n * P : (n + 1) * P],
                     rhs=page_codes[c][:].bitcast(FP8X4),
                     rhs_scale=page_planes[c][:],

@@ -115,6 +115,7 @@ def tile_list_mancala_kick_drift_kernel(
         for r in range(4):
             nc.sync.dma_start(wq_plane_raw[r:P:32, :, :].bitcast(I32), wq_rows[r])
         tab_w = [load_words(tab_words[0], "tab_w0")]
+        wp_raw.append(load_wp(1))
         v_rows = keep.tile([P, S], U8, name="v_rows", align_bytes=64)
         gather(v_rows[:], tab_rows[:], idx[:], U8)
         for quad in (0, 2, 1, 3):
@@ -122,7 +123,6 @@ def tile_list_mancala_kick_drift_kernel(
                 v_planes[32 * quad : 32 * quad + 4, :, :].bitcast(I32),
                 v_rows[8 * quad : 8 * quad + 8, :].bitcast(I32),
             )
-        wp_raw.append(load_wp(1))
         tab_w.append(load_words(tab_words[1], "tab_w1"))
         kap_sb = load_column(kap, "kap_sb")
         gq_sb = load_column(gq, "gq_sb")

from contextlib import ExitStack

import concourse.mybir as mybir

K, H, T, S = 1024, 512, 2048, 1024
FLOPS = 2 * 2 * K * H * S + 2 * H * S * T

F32 = mybir.dt.float32
BF16 = mybir.dt.bfloat16
I32 = mybir.dt.int32
U32 = mybir.dt.uint32
U16 = mybir.dt.uint16
U8 = mybir.dt.uint8
FP8X4 = mybir.dt.float8_e4m3fn_x4
FP4X4 = mybir.dt.float4_e2m1fn_x4
MULT = mybir.AluOpType.mult
ADD = mybir.AluOpType.add
SUB = mybir.AluOpType.subtract
SIN = mybir.ActivationFunctionType.Sin
COPY = mybir.ActivationFunctionType.Copy

P = 128
PACK = 4
BANK = 512
PASSES = K // (P * PACK)
QUADS = 4
SPLIT = 896
FIRST_ROWS = 256
LAST_WIDTHS = (512, 384, 128)
KB = 1024


def tile_list_mancala_kick_drift_kernel(
    tc, tab_words, tab_scales, tab2_words, tab2_scales, offs, offs2, offs3, offs4,
    wq_words, wq_scales, wp, kap, gq, page0, wgs, prior, out,
):
    nc = tc.nc
    with ExitStack() as ctx:
        lists = ctx.enter_context(tc.tile_pool(name="lists", bufs=1))
        keep = ctx.enter_context(tc.tile_pool(name="keep", bufs=1))
        ring = ctx.enter_context(tc.tile_pool(name="ring", bufs=2))
        shared = ctx.enter_context(tc.tile_pool(name="shared", bufs=1))
        psum = ctx.enter_context(tc.psum_pool(name="psum", bufs=8))

        def load_list(src, name):
            tile = lists.tile([P, S // 16], U16, name=name)
            nc.sync.dma_start(tile[:], src)
            return tile

        def zeroed(shape, name):
            tile = keep.tile(shape, U8, name=name, align_bytes=64)
            nc.vector.memset(tile[:].bitcast(I32), 0)
            return tile

        def load_words(src, name):
            tile = keep.tile([P, T], I32, name=name, align_bytes=64)
            nc.sync.dma_start(tile[:], src.rearrange("p n i -> p (n i)").bitcast(I32))
            return tile

        def gather(dst, window, offsets, dtype):
            nc.vector.tensor_copy(dst.bitcast(dtype), window.bitcast(dtype).indirect(offsets))

        def load_wp(a):
            tile = keep.tile([P, PACK, H], F32, name="wp_raw%d" % a, align_bytes=64)
            rows = wp[a * P * PACK : (a + 1) * P * PACK, :]
            nc.sync.dma_start(tile[:], rows.rearrange("(p j) c -> p j c", j=PACK))
            return tile

        def load_page(t):
            tile = keep.tile([P, T], F32, name="page%d" % t)
            nc.sync.dma_start(tile[:], page0.rearrange("(p t) c -> t p c", t=PACK)[t])
            return tile

        def placed(name, width, offset):
            return shared.tile([P, width], F32, name=name, offset=offset * KB, align_bytes=64)

        def load_wg(tile, first, width):
            for quad in (0, 2, 1, 3):
                nc.sync.dma_start(
                    tile[32 * quad : 32 * quad + 32, :],
                    wgs.rearrange("(p t) j -> p (t j)", t=PACK)[:, first : first + width],
                )
            return tile

        def load_column(src, name):
            tile = keep.tile([P, PACK], F32, name=name)
            nc.sync.dma_start(tile[:], src.rearrange("(p t) -> p t", t=PACK))
            return tile

        def half(u):
            return slice(u * BANK, (u + 1) * BANK)

        tab_rows = keep.tile([P, T], U8, name="tab_rows", align_bytes=64)
        tab2_rows = keep.tile([P, T], U8, name="tab2_rows", align_bytes=64)
        nc.gpsimd.memset(tab2_rows[0:32, :].bitcast(I32), 0)
        wq_plane_raw = zeroed([P, PASSES, H], "wq_plane_raw")
        v_planes = zeroed([P, PASSES, S], "v_planes")
        v2_plane = zeroed([P, S], "v2_plane")

        idx = load_list(offs, "idx")
        nc.sync.dma_start(
            tab_rows[0:32, :].bitcast(I32),
            tab_scales.rearrange("a b c -> b a c").bitcast(I32),
        )
        nc.gpsimd.memset(tab_rows[32:64, :].bitcast(I32), 0)
        nc.gpsimd.memset(tab_rows[64:P, :].bitcast(I32), 0)
        idx2 = load_list(offs2, "idx2")
        nc.sync.dma_start(tab2_rows[0:16, :].bitcast(I32), tab2_scales[0].bitcast(I32))
        nc.vector.memset(tab2_rows[32:64, :].bitcast(I32), 0)
        nc.vector.memset(tab2_rows[64:P, :].bitcast(I32), 0)
        wp_raw = [load_wp(0)]
        wq_raw = keep.tile([P, PASSES, 2 * H], U8, name="wq_raw", align_bytes=64)
        nc.sync.dma_start(wq_raw[:].bitcast(I32), wq_words.rearrange("a p c -> p a c").bitcast(I32))
        wq_rows = wq_scales.rearrange("a (q r) c -> r q a c", r=4).bitcast(I32)
        for r in range(4):
            nc.sync.dma_start(wq_plane_raw[r:P:32, :, :].bitcast(I32), wq_rows[r])
        tab_w = [load_words(tab_words[0], "tab_w0")]
        wp_raw.append(load_wp(1))
        v_rows = keep.tile([P, S], U8, name="v_rows", align_bytes=64)
        gather(v_rows[:], tab_rows[:], idx[:], U8)
        for quad in (0, 2, 1, 3):
            nc.sync.dma_start(
                v_planes[32 * quad : 32 * quad + 4, :, :].bitcast(I32),
                v_rows[8 * quad : 8 * quad + 8, :].bitcast(I32),
            )
        tab_w.append(load_words(tab_words[1], "tab_w1"))
        kap_sb = load_column(kap, "kap_sb")
        gq_sb = load_column(gq, "gq_sb")
        v2_rows = keep.tile([P, S], U8, name="v2_rows", align_bytes=64)
        gather(v2_rows[:], tab2_rows[:], idx2[:], U8)

        def move_v2_rows(r):
            nc.sync.dma_start(v2_plane[r:P:32, :].bitcast(I32), v2_rows[r:16:4, :].bitcast(I32))

        first_wg = load_wg(placed("first_wg", BANK, 53), 0, BANK)
        idx3 = load_list(offs3, "idx3")
        page = [load_page(0)]
        next_wg = load_wg(keep.tile([P, 3 * BANK], F32, name="next_wg", align_bytes=64), BANK, 3 * BANK)
        page.append(load_page(1))
        idx4 = load_list(offs4, "idx4")
        move_v2_rows(0)
        late_wg = ring.tile([P, 2, S], F32, name="late_turn", bufs=4, align_bytes=64)
        for quad in (0, 2, 1, 3):
            nc.sync.dma_start(
                late_wg[32 * quad : 32 * quad + 32, :, :],
                wgs.rearrange("(p t) j -> p t j", t=PACK)[:, 2:PACK, :],
            )
        page.append(load_page(2))
        tab2_w = load_words(tab2_words[0], "tab2_w")
        page.append(load_page(3))
        for r in range(1, 4):
            move_v2_rows(r)

        def gather_words(a):
            pair = []
            for u in range(2):
                tile = keep.tile([P, BANK], U32, name="v_w%d%d" % (a, u), bufs=1 + a * u, align_bytes=64)
                gather(tile[:], tab_w[a][:], idx[:, 32 * u : 32 * (u + 1)], U32)
                pair.append(tile)
            return pair

        def round_wp(copy, grouped, a, first, slices):
            copy(
                grouped[:].rearrange("p (t m j) -> p m t j", t=PACK, j=PACK)[:, :, first : first + slices, :],
                wp_raw[a][:].rearrange("p j (m t) -> p m t j", t=PACK)[:, :, first : first + slices, :],
            )

        def quantise_wp(a, first, slices, tag, bufs):
            codes = keep.tile([P, P * slices], U32, name="wp_codes", tag=tag, bufs=bufs, align_bytes=64)
            plane = keep.tile([P, P * slices], U8, name="wp_plane%d%d" % (a, first), align_bytes=64)
            source = grouped[a][:, BANK * first : BANK * (first + slices)]
            nc.vector.quantize_mx(out=codes[:].bitcast(FP8X4), scales=plane[:], in_=source)
            for t in range(slices):
                wp_mx[a, first + t] = codes[:, P * t : P * (t + 1)], plane[:, P * t : P * (t + 1)]

        grouped = [
            shared.tile([P, H * PACK], BF16, name="grouped%d" % a, offset=(8 + 4 * a) * KB, align_bytes=64)
            for a in range(PASSES)
        ]
        round_wp(nc.scalar.copy, grouped[0], 0, 0, PACK)
        wq_perm = keep.tile([P, PASSES, 2 * H], U8, name="wq_perm", align_bytes=64)
        nc.scalar.copy(
            wq_perm[:].bitcast(U16).rearrange("p a (t m) -> p a m t", t=PACK),
            wq_raw[:].bitcast(U16).rearrange("p a (m t) -> p a m t", t=PACK),
        )
        wq_plane = keep.tile([P, PASSES, H], U8, name="wq_plane", align_bytes=64)
        nc.vector.tensor_copy(
            wq_plane[:].rearrange("p a (t m) -> p a t m", t=PACK),
            wq_plane_raw[:].rearrange("p a (m t) -> p a t m", t=PACK),
        )
        v_w = [gather_words(0)]
        wp_mx = {}
        quantise_wp(0, 0, PACK, "wp_codes0", 1)
        round_wp(nc.scalar.copy, grouped[1], 1, 0, 2)
        round_wp(nc.scalar.copy, grouped[1], 1, 2, 2)
        quantise_wp(1, 0, 2, "wp_codes1", 1)
        v_w.append(gather_words(1))
        quantise_wp(1, 2, 2, "v_w11", 2)

        last = PACK - 1

        def q_pass(q, t, u, a):
            nc.tensor.matmul_mx(
                out=q[:],
                lhsT=wq_perm[:, a, 2 * P * t : 2 * P * (t + 1)].bitcast(FP4X4),
                lhsT_scale=wq_plane[:, a, P * t : P * (t + 1)],
                rhs=v_w[a][u][:].bitcast(FP8X4),
                rhs_scale=v_planes[:, a, half(u)],
                start=(a == 0),
                stop=(a == PASSES - 1),
            )

        def mom_pass(mom, t, u, a):
            nc.tensor.matmul_mx(
                out=mom[:],
                lhsT=wp_mx[a, t][0].bitcast(FP8X4),
                lhsT_scale=wp_mx[a, t][1],
                rhs=v_w[a][u][:].bitcast(FP8X4),
                rhs_scale=v_planes[:, a, half(u)],
                start=(a == 0),
                stop=(a == PASSES - 1),
            )

        def opened(one_pass, t, u):
            bank = psum.tile([P, BANK], F32, name="bank")
            one_pass(bank, t, u, 0)
            return bank

        def whole(one_pass, t, u):
            bank = opened(one_pass, t, u)
            one_pass(bank, t, u, 1)
            return bank

        def emptied():
            return ring.tile([P, BANK], F32, name="emptied", bufs=5, align_bytes=64)

        def sine_of(q):
            dst = emptied()
            nc.scalar.activation(dst[:], q[:], SIN)
            return dst

        def drift_term(dst, t, q):
            nc.scalar.activation(dst, q[:], COPY, scale=gq_sb[:, t : t + 1])

        def kick(dst, t, sine, mom):
            nc.vector.scalar_tensor_tensor(dst, sine[:], kap_sb[:, t : t + 1], mom[:], MULT, SUB)

        def scatter(t, cols, values):
            nc.vector.tensor_copy(page[t][:].indirect(idx3[:, cols.start // 16 : cols.stop // 16]), values)

        def round_on_gpsimd(dst, src, factor):
            nc.gpsimd.tensor_scalar(dst, src, factor, 0.0, MULT, ADD)

        def in_turn(width):
            return ring.tile([P, width], F32, name="in_turn", bufs=3, align_bytes=64)

        early = [(t, u) for u in range(2) for t in range(2)]
        q = {key: opened(q_pass, *key) for key in early}
        mom = {key: opened(mom_pass, *key) for key in early}
        sine, state, kicked = {}, {}, {}
        for t, u in early:
            q_pass(q[t, u], t, u, 1)
            mom_pass(mom[t, u], t, u, 1)
            sine[t, u] = sine_of(q[t, u])
            if (t, u) == (0, 1):
                state[t, u] = emptied()
                drift_term(state[t, u][:], t, q[t, u])
        state1 = placed("state1", S, 47)
        for u in range(2):
            drift_term(state1[:, half(u)], 1, q[1, u])

        kicked[0, 0] = placed("kicked00", BANK, 21)
        kick(kicked[0, 0][:], 0, sine[0, 0], mom[0, 0])
        h = in_turn(BANK)
        nc.vector.scalar_tensor_tensor(h[:], q[0, 0][:], gq_sb[:, 0:1], kicked[0, 0][:], MULT, SUB)
        new0 = placed("new00", BANK, 55)
        nc.gpsimd.tensor_tensor(new0[:], h[:], first_wg[:], MULT)
        kicked1 = in_turn(S)
        kick(kicked1[:, half(0)], 1, sine[1, 0], mom[1, 0])
        kicked[0, 1] = in_turn(BANK)
        kick(kicked[0, 1][:], 0, sine[0, 1], mom[0, 1])
        kick(kicked1[:, half(1)], 1, sine[1, 1], mom[1, 1])
        scatter(0, half(0), new0[:])

        h = placed("h01", BANK, 53)
        nc.gpsimd.tensor_tensor(h[:], state[0, 1][:], kicked[0, 1][:], SUB)
        kicked2 = ring.tile([P, S], F32, name="late_turn", bufs=4, align_bytes=64)
        state2 = placed("state2", S, 29)
        q2 = []
        for u in range(2):
            q2.append(whole(q_pass, 2, u))
            kick(kicked2[:, half(u)], 2, sine_of(q2[u]), whole(mom_pass, 2, u))
        for u in range(2):
            drift_term(state2[:, half(u)], 2, q2[u])
        new0 = ring.tile([P, BANK], F32, name="late_turn", bufs=4, align_bytes=64)
        nc.gpsimd.tensor_tensor(new0[:], h[:], next_wg[:, half(0)], MULT)
        scatter(0, half(1), new0[:])

        def wide():
            return ring.tile([P, S], F32, name="wide", bufs=4, align_bytes=64)

        h = ring.tile([P, S], F32, name="late_turn", bufs=4, align_bytes=64)
        nc.gpsimd.tensor_tensor(h[:], state1[:], kicked1[:], SUB)
        new1 = wide()
        nc.gpsimd.tensor_tensor(new1[:], h[:], next_wg[:, BANK:], MULT)
        scatter(1, slice(0, S), new1[:])

        h = wide()
        nc.gpsimd.tensor_tensor(h[:], state2[:], kicked2[:], SUB)
        new2 = wide()
        nc.gpsimd.tensor_tensor(new2[:], h[:], late_wg[:, 0, :], MULT)
        scatter(2, slice(0, S), new2[:])

        sine3, state3, mom3 = placed("sine3", S, 53), placed("state3", S, 37), placed("mom3", S, 41)
        for u in range(2):
            q3 = whole(q_pass, last, u)
            drift_term(state3[:, half(u)], last, q3)
            nc.scalar.copy(mom3[:, half(u)], whole(mom_pass, last, u)[:])
            raw = placed("raw_sine%d" % u, BANK, 45 if u == 0 else 0)
            nc.scalar.activation(raw[:], q3[:], SIN)
            nc.scalar.activation(sine3[:, half(u)], raw[:], COPY, scale=kap_sb[:, last:PACK])
        h = wide()
        nc.gpsimd.tensor_tensor(h[:], state3[:], mom3[:], ADD)
        nc.gpsimd.tensor_tensor(h[:], h[:], sine3[:], SUB)
        new3 = placed("new3", S, 17)
        nc.gpsimd.tensor_tensor(new3[:], h[:], late_wg[:, 1, :], MULT)
        scatter(last, slice(0, S), new3[:])

        prior_sb = shared.tile([P, S // P, S], F32, name="prior_sb", offset=20 * KB + 512, align_bytes=64)
        for n in range(0, S // P, 2):
            nc.sync.dma_start(
                prior_sb[:, n : n + 2, :],
                prior[P * n : P * (n + 2), :].rearrange("(g p) m -> p g m", p=P),
            )

        grouped_page = shared.tile([P, T, PACK], BF16, name="grouped_page", offset=0, align_bytes=64)
        for t in range(2):
            nc.scalar.copy(grouped_page[:, :, t], page[t][:])
        one = placed("one", 1, 53)
        nc.gpsimd.memset(one[:], 1.0)
        for cols in (slice(2 * BANK, 3 * BANK), slice(SPLIT, 2 * BANK), slice(3 * BANK, T)):
            nc.scalar.copy(grouped_page[:, cols, 2], page[2][:, cols])
        round_on_gpsimd(grouped_page[:, 0:SPLIT, 2], page[2][:, 0:SPLIT], one[:])
        after = placed("after", 1, 53)
        nc.gpsimd.memset(after[:], 1.0)
        for cols in (slice(2 * BANK, 3 * BANK), slice(SPLIT, 2 * BANK), slice(3 * BANK, T)):
            nc.scalar.copy(grouped_page[:, cols, last], page[last][:, cols])
        nc.vector.tensor_scalar(grouped_page[:, 0:SPLIT, last], page[last][:, 0:SPLIT], after[:], None, MULT)

        v2_words = [shared.tile([P, FIRST_ROWS], U32, name="v2_words", offset=17 * KB, align_bytes=64)]
        gather(v2_words[0][:], tab2_w[:], idx2[:, 0 : FIRST_ROWS // 16], U32)
        chunk_order = [2, 0, 1, 3]
        page_codes, page_planes = {}, {}
        for c in chunk_order:
            codes = keep.tile([P, BANK], U32, name="page_codes", tag="v_w%d%d" % (c // 2, c % 2), bufs=1 + c // 3, align_bytes=64)
            if c == chunk_order[-1]:
                plane = ring.tile([P, BANK], U8, name="page_plane", tag="in_turn", bufs=3, align_bytes=64)
            else:
                plane = ring.tile([P, BANK], U8, name="page_plane", tag="emptied", bufs=5, align_bytes=64)
            nc.vector.quantize_mx(
                out=codes[:].bitcast(FP8X4),
                scales=plane[:],
                in_=grouped_page[:, half(c), :].rearrange("p n t -> p (n t)"),
            )
            page_codes[c] = codes
            page_planes[c] = plane
        v2_words.append(ring.tile([P, S - FIRST_ROWS], U32, name="v2_words_late", tag="in_turn", bufs=3, align_bytes=64))
        gather(v2_words[1][:], tab2_w[:], idx2[:, FIRST_ROWS // 16 :], U32)

        tiles = S // P
        for n in range(tiles):
            scores = keep.tile([P, T], F32, name="scores", tag=("wp_raw0", "wp_raw1", "tab_w1")[n % 3], align_bytes=64)
            start = n * P
            rows = v2_words[0][:, start : start + P] if start < FIRST_ROWS else v2_words[1][:, start - FIRST_ROWS : start - FIRST_ROWS + P]
            for c in chunk_order:
                e = psum.tile([P, BANK], F32, name="e", tag="bank")
                nc.tensor.matmul_mx(
                    out=e[:],
                    lhsT=rows.bitcast(FP8X4),
                    lhsT_scale=v2_plane[:, n * P : (n + 1) * P],
                    rhs=page_codes[c][:].bitcast(FP8X4),
                    rhs_scale=page_planes[c][:],
                    start=True,
                    stop=True,
                )
                nc.scalar.copy(scores[:, half(c)], e[:])
            picked = wide()
            widths = LAST_WIDTHS if n == tiles - 1 else (S,)
            first = 0
            for width in widths:
                cols = slice(first, first + width)
                nc.vector.tensor_tensor(
                    picked[:, cols],
                    scores[:].indirect(idx4[:, first // 16 : (first + width) // 16]),
                    prior_sb[:, n, cols],
                    ADD,
                )
                nc.sync.dma_start(out[n * P : (n + 1) * P, cols], picked[:, cols])
                first = first + width
